import numpy as np
import ml_dtypes


def mxq(x, axis, fmt="e4m3"):
    dtype, down = {"e4m3": (ml_dtypes.float8_e4m3fn, 7), "e5m2": (ml_dtypes.float8_e5m2, 14)}[fmt]
    v = np.moveaxis(np.asarray(x, np.float32).astype(ml_dtypes.bfloat16).astype(np.float64), axis, -1)
    blocks = v.reshape(v.shape[:-1] + (-1, 32))
    amax = np.abs(blocks).max(-1, keepdims=True)
    byte = np.maximum(np.where(amax > 0, np.frexp(amax)[1] - 1 + 127, 0) - down, 1)
    scale = np.exp2(byte - 127.0)
    codes = (blocks / scale).astype(np.float32).astype(dtype).astype(np.float64)
    return np.moveaxis((codes * scale).reshape(v.shape), -1, axis)


WIDE = False


def mx_kscale(k):
    if not WIDE:
        return np.ones(k)
    levels = np.array([10, -10, 5, -5, 0])
    if k % 512:
        return np.exp2(np.random.permutation(np.resize(levels, k // 32))).repeat(32)
    a = np.empty((k // 512, 16))
    for p in range(k // 512):
        a[p, :8] = np.random.permutation(np.resize(levels, 8))
        for g in range(8):
            far = levels[np.abs(levels - a[p, g]) >= 10]
            a[p, g + 8] = far[np.random.randint(len(far))]
    return np.exp2(a.ravel()).repeat(32)


def f64(x):
    return np.asarray(x).astype(np.float64)


def striped(idx):
    return np.tile(idx.reshape(-1, 16).T, (8, 1)).astype(np.uint16)


def unstriped(offs):
    return offs[:16].T.reshape(-1).astype(np.int64)


E2M1 = np.array([0.0, 0.5, 1.0, 1.5, 2.0, 3.0, 4.0, 6.0, -0.0, -0.5, -1.0, -1.5, -2.0, -3.0, -4.0, -6.0])


def pack_weight(w, fmt):
    k, n = w.shape
    w = f64(np.asarray(w, np.float32).astype(ml_dtypes.bfloat16)).reshape(k // 32, 32, n)
    amax = np.abs(w).max(1)
    if fmt == "e4m3":
        byte = np.frexp(amax)[1] - 1 + 127 - 7
    else:
        mant, ex = np.frexp(amax / 6.0)
        byte = np.where(mant > 0.5, ex, ex - 1) + 127
    byte = np.clip(np.where(amax > 0, byte, 1), 1, 254)
    scaled = (w * np.exp2(127.0 - byte)[:, None, :]).reshape(k, n).astype(np.float32)
    by_word = np.ascontiguousarray(scaled.reshape(k // 512, 128, 4, n).transpose(0, 1, 3, 2))
    if fmt == "e4m3":
        words = by_word.astype(ml_dtypes.float8_e4m3fn).view(np.uint8)
    else:
        c = by_word.astype(ml_dtypes.float4_e2m1fn).view(np.uint8) & 0xF
        words = (c[..., 0::2] | (c[..., 1::2] << 4)).reshape(k // 512, 128, 2 * n)
    return np.ascontiguousarray(words), np.ascontiguousarray(byte.astype(np.uint8).reshape(k // 512, 16, n))


def unpack_weight(words, scales, fmt):
    g, _, n = scales.shape
    words = np.ascontiguousarray(words).reshape(g, 128, n, -1)
    if fmt == "e4m3":
        vals = words.view(ml_dtypes.float8_e4m3fn).astype(np.float64)
    else:
        nib = np.empty((g, 128, n, 4), np.uint8)
        nib[..., 0::2] = words & 0xF
        nib[..., 1::2] = words >> 4
        vals = E2M1[nib]
    vals = vals * np.repeat(np.exp2(scales.astype(np.float64) - 127.0), 8, axis=1)[..., None]
    return vals.transpose(0, 1, 3, 2).reshape(g * 512, n)


def gelu(v):
    return 0.5 * v * (1.0 + np.tanh(np.sqrt(2.0 / np.pi) * (v + 0.044715 * v**3)))


K, T, E, C, H, HS, N = 512, 512, 8, 256, 512, 512, 128
TOP = 4


def by_expert(wq, xq):
    return np.concatenate([wq[e].T @ xq[:, e * C:(e + 1) * C] for e in range(E)], axis=1)


def setup_inputs():
    n = np.random.standard_normal
    s = mx_kscale(K)
    u = mx_kscale(H)
    v = mx_kscale(HS)
    deal = np.repeat(np.arange(E), C).reshape(TOP, T)[:, np.random.permutation(T)]
    deal = np.take_along_axis(deal, np.argsort(np.random.rand(TOP, T), axis=0), axis=0)
    for _ in range(8):
        s_, t_ = np.random.permutation(T).reshape(2, -1); r = np.random.randint(TOP, size=T // 2); x, y = deal[r, s_].copy(), deal[r, t_].copy()
        ok = ~((deal[:, s_] == y).any(0) | (deal[:, t_] == x).any(0)); deal[r[ok], s_[ok]] = y[ok]; deal[r[ok], t_[ok]] = x[ok]
    order = np.argsort(deal.reshape(-1) + 0.5 * np.random.rand(TOP * T))
    slot_token = order % T; pos = np.empty(TOP * T, np.int64); pos[order] = np.arange(TOP * T); pos = pos.reshape(TOP, T)
    g = np.random.uniform(0.5, 1.5, (TOP, T)); g = g / g.sum(0)
    x = pack_weight(n((K, T)) * s[:, None], "e4m3")
    w1 = [pack_weight(m, "e2m1") for m in n((E, K, H)) / np.sqrt(K) / s[None, :, None]]
    w3 = [pack_weight(m, "e2m1") for m in n((E, K, H)) / np.sqrt(K) / s[None, :, None] * u]
    w2 = [pack_weight(m, "e2m1") for m in n((E, H, N)) / np.sqrt(H) / u[None, :, None]]
    w1s = pack_weight(n((K, HS)) / np.sqrt(K) / s[:, None], "e4m3")
    w3s = pack_weight(n((K, HS)) / np.sqrt(K) / s[:, None] * v, "e4m3")
    w2s = pack_weight(n((HS, N)) / np.sqrt(HS) / v[:, None], "e4m3")
    return {
        "x_words": x[0],
        "x_scales": x[1],
        "w1_words": np.stack([m[0] for m in w1]),
        "w1_scales": np.stack([m[1] for m in w1]),
        "w3_words": np.stack([m[0] for m in w3]),
        "w3_scales": np.stack([m[1] for m in w3]),
        "w2_words": np.stack([m[0] for m in w2]),
        "w2_scales": np.stack([m[1] for m in w2]),
        "w1s_words": w1s[0],
        "w1s_scales": w1s[1],
        "w3s_words": w3s[0],
        "w3s_scales": w3s[1],
        "w2s_words": w2s[0],
        "w2s_scales": w2s[1],
        "gate": np.stack([np.tile(r, (128, 1)) for r in g]).astype(np.float32),
        "offs": striped(slot_token),
        "pos1": striped(pos[0]),
        "pos2": striped(pos[1]),
        "pos3": striped(pos[2]),
        "pos4": striped(pos[3]),
    }


def reference(x_words, x_scales, w1_words, w1_scales, w3_words, w3_scales, w2_words, w2_scales, w1s_words, w1s_scales, w3s_words, w3s_scales, w2s_words, w2s_scales, gate, offs, pos1, pos2, pos3, pos4):
    w1 = np.stack([unpack_weight(w1_words[e], w1_scales[e], "e2m1") for e in range(E)])
    w3 = np.stack([unpack_weight(w3_words[e], w3_scales[e], "e2m1") for e in range(E)])
    w2 = np.stack([unpack_weight(w2_words[e], w2_scales[e], "e2m1") for e in range(E)])
    w1s = unpack_weight(w1s_words, w1s_scales, "e4m3")
    w3s = unpack_weight(w3s_words, w3s_scales, "e4m3")
    w2s = unpack_weight(w2s_words, w2s_scales, "e4m3")
    idx = unstriped(offs)
    x = unpack_weight(x_words, x_scales, "e4m3")
    hs = gelu(w1s.T @ x) * (w3s.T @ x)
    ys = w2s.T @ mxq(hs, 0, "e4m3")
    h = gelu(by_expert(w1, x[:, idx])) * by_expert(w3, x[:, idx])
    y = by_expert(w2, mxq(h, 0, "e4m3"))
    c = sum(f64(gate[r, :1]) * y[:, unstriped(p)] for r, p in enumerate((pos1, pos2, pos3, pos4)))
    return ys + c

@@ -1,0 +1,203 @@
+from contextlib import ExitStack
+
+import concourse.mybir as mybir
+from concourse.masks import make_identity
+
+K, T, E, C, H, N, TOP = 512, 512, 8, 256, 512, 128, 4
+FLOPS = 3019898880
+
+F32 = mybir.dt.float32
+BF16 = mybir.dt.bfloat16
+I32 = mybir.dt.int32
+U32 = mybir.dt.uint32
+U16 = mybir.dt.uint16
+U8 = mybir.dt.uint8
+FP8X4 = mybir.dt.float8_e4m3fn_x4
+FP4X4 = mybir.dt.float4_e2m1fn_x4
+GELU = mybir.ActivationFunctionType.Gelu_apprx_tanh
+MULT = mybir.AluOpType.mult
+ADD = mybir.AluOpType.add
+
+P = 128
+GROUPS = E + T // C
+CHUNKS = ((0, 1), (1, 3), (3, 8))
+
+
+def tile_moe_shf_glu_gelu_kernel(
+    tc, x_words, x_scales, w1_words, w1_scales, w3_words, w3_scales, w2_words, w2_scales,
+    w1s_words, w1s_scales, w3s_words, w3s_scales, w2s_words, w2s_scales,
+    gate, offs, pos1, pos2, pos3, pos4, out,
+):
+    nc = tc.nc
+    with ExitStack() as ctx:
+        keep = ctx.enter_context(tc.tile_pool(name="keep", bufs=1))
+        ring = ctx.enter_context(tc.tile_pool(name="ring", bufs=3))
+        psum = ctx.enter_context(tc.psum_pool(name="psum", bufs=1))
+
+        def held(shape, dtype, name):
+            return keep.tile(shape, dtype, name=name, align_bytes=64)
+
+        def load_list(src, name):
+            t = keep.tile(list(src.shape), U16, name=name)
+            nc.sync.dma_start(t[:], src)
+            return t
+
+        def load_fp8_words(src, name):
+            t = held([P, src.shape[2]], I32, name)
+            nc.sync.dma_start(t[:], src[0].rearrange("p n d -> p (n d)").bitcast(I32))
+            return t
+
+        def load_fp4_words(src, lo, hi, name):
+            t = held([P, hi - lo, src.shape[3]], U8, name)
+            nc.sync.dma_start(t[:].bitcast(I32), src[lo:hi, 0].rearrange("e p n -> p e n").bitcast(I32))
+            return t
+
+        def zeroed_planes(src, name):
+            t = held([P, src.shape[0], src.shape[-1]], U8, name)
+            nc.vector.memset(t[:].rearrange("p e n -> p (e n)").bitcast(I32), 0)
+            return t
+
+        def load_planes(t, src):
+            for r in range(4):
+                nc.sync.dma_start(t[r:P:32].bitcast(I32), src[:, r:16:4, :].rearrange("e q n -> q e n").bitcast(I32))
+
+        xs3 = zeroed_planes(x_scales, "xs3")
+        s1 = zeroed_planes(w1_scales, "s1")
+        s3 = zeroed_planes(w3_scales, "s3")
+        warm = held([P, 1], F32, "warm")
+        nc.vector.memset(warm[:], 0.0)
+        warm_out = held([P, 1], F32, "warm_out")
+        nc.scalar.activation(warm_out[:], warm[:], GELU)
+        s2 = zeroed_planes(w2_scales, "s2")
+        s1s = zeroed_planes(w1s_scales, "s1s")
+        s3s = zeroed_planes(w3s_scales, "s3s")
+        s2s = zeroed_planes(w2s_scales, "s2s")
+        ident = held([P, P], F32, "ident")
+        make_identity(nc, ident[:])
+
+        offs_t = load_list(offs, "offs_t")
+        xw = load_fp8_words(x_words, "xw")
+        load_planes(xs3, x_scales)
+        xs = xs3[:, 0, :]
+        w1_t = [load_fp4_words(w1_words, 0, 1, "w1_0")]
+        w3_t = [load_fp4_words(w3_words, 0, 1, "w3_0")]
+        load_planes(s1, w1_scales[:, 0])
+        load_planes(s3, w3_scales[:, 0])
+        w1_t.append(load_fp4_words(w1_words, 1, 3, "w1_1"))
+        w3_t.append(load_fp4_words(w3_words, 1, 3, "w3_1"))
+        load_planes(s2, w2_scales[:, 0])
+        w2_t = load_fp4_words(w2_words, 0, E, "w2_t")
+        w1_t.append(load_fp4_words(w1_words, 3, 8, "w1_2"))
+        w3_t.append(load_fp4_words(w3_words, 3, 8, "w3_2"))
+        w1s_t = load_fp8_words(w1s_words, "w1s_t")
+        w3s_t = load_fp8_words(w3s_words, "w3s_t")
+        w2s_t = load_fp8_words(w2s_words, "w2s_t")
+        load_planes(s1s, w1s_scales)
+        load_planes(s3s, w3s_scales)
+        load_planes(s2s, w2s_scales)
+        pos_t = [load_list(src, "pos_t%d" % r) for r, src in enumerate((pos1, pos2, pos3, pos4))]
+        gate_t = held([P, TOP, T], F32, "gate_t")
+        nc.sync.dma_start(gate_t[:], gate.rearrange("r p t -> p r t"))
+
+        def first_layer(g):
+            if g >= E:
+                return ((w1s_t[:].bitcast(FP8X4), s1s[:, 0, :]), (w3s_t[:].bitcast(FP8X4), s3s[:, 0, :]))
+            c = [i for i, (lo, hi) in enumerate(CHUNKS) if lo <= g < hi][0]
+            j = g - CHUNKS[c][0]
+            return ((w1_t[c][:, j, :].bitcast(FP4X4), s1[:, g, :]), (w3_t[c][:, j, :].bitcast(FP4X4), s3[:, g, :]))
+
+        def second_layer(g):
+            if g >= E:
+                return w2s_t[:].bitcast(FP8X4), s2s[:, 0, :]
+            return w2_t[:, g, :].bitcast(FP4X4), s2[:, g, :]
+
+        tokens = {}
+        h = {}
+        h_t = {}
+        y_all = held([P, E * C], F32, "y_all")
+        shared = {}
+
+        def gather(g):
+            if g >= E:
+                cols = slice((g - E) * C, (g - E + 1) * C)
+                tokens[g] = (xw[:, cols], xs[:, cols])
+                return
+            idx = offs_t[:, g * C // 16:(g + 1) * C // 16]
+            words = ring.tile([P, C], U32, name="words", align_bytes=64)
+            scales = ring.tile([P, C], U8, name="scales", align_bytes=64)
+            nc.vector.tensor_copy(words[:], xw[:].bitcast(U32).indirect(idx))
+            nc.vector.tensor_copy(scales[:], xs.indirect(idx))
+            tokens[g] = (words[:], scales[:])
+
+        def front(g, j):
+            words, scales = tokens[g]
+            cols = slice(j * P, (j + 1) * P)
+            a = psum.tile([P, H], F32, name="a", bufs=2)
+            b = psum.tile([P, H], F32, name="b", bufs=3)
+            for acc, (w, s) in zip((a, b), first_layer(g)):
+                nc.tensor.matmul_mx(out=acc[:], lhsT=words[:, cols].bitcast(FP8X4), lhsT_scale=scales[:, cols],
+                                    rhs=w, rhs_scale=s, start=True, stop=True)
+            act = ring.tile([P, 2, P, 2], F32, name="act")
+            nc.scalar.activation(act[:], a[:].rearrange("s (p u e) -> s u p e", u=2, e=2), GELU)
+            h[g, j] = ring.tile([P, 2, P, 2], BF16, name="h", bufs=4)
+            nc.vector.tensor_tensor(h[g, j][:], b[:].rearrange("s (p u e) -> s u p e", u=2, e=2), act[:], MULT)
+
+        def turn(g):
+            turned = psum.tile([P, 2, 2, P], F32, name="turned", bufs=2)
+            for j in range(2):
+                pairs = h[g, j][:].rearrange("s u p e -> s (u p e)").bitcast(F32)
+                for u in range(2):
+                    nc.tensor.transpose(turned[:, j, u, :], pairs[:, u * P:(u + 1) * P], ident[:])
+            h_t[g] = ring.tile([P, C * 4], BF16, name="h_t", align_bytes=64)
+            nc.scalar.copy(h_t[g][:].bitcast(F32).rearrange("p (j s u) -> p j s u", j=2, u=2),
+                           turned[:].rearrange("p j u s -> p j s u"))
+
+        def back(g):
+            codes = ring.tile([P, C], U32, name="codes", align_bytes=64)
+            planes = ring.tile([P, C], U8, name="planes", align_bytes=64)
+            nc.vector.quantize_mx(out=codes[:].bitcast(FP8X4), scales=planes[:], in_=h_t[g][:])
+            w, s = second_layer(g)
+            if g <= E:
+                shared["y"] = psum.tile([P, T], F32, name="y")
+            cols = slice(0, C) if g <= E else slice(C, 2 * C)
+            y = shared["y"][:, cols]
+            nc.tensor.matmul_mx(out=y, lhsT=w, lhsT_scale=s, rhs=codes[:].bitcast(FP8X4), rhs_scale=planes[:],
+                                start=True, stop=True)
+            if g < E:
+                nc.scalar.copy(y_all[:, g * C:(g + 1) * C], y)
+
+        prod = {}
+
+        def combine(r):
+            prod[r] = held([P, T], F32, "prod%d" % r)
+            nc.vector.tensor_tensor(prod[r][:], y_all[:].indirect(pos_t[r][:]), gate_t[:, r, :], MULT)
+
+        gather(0)
+        gather(1)
+        for g in range(GROUPS):
+            front(g, 0)
+            if g >= 1:
+                turn(g - 1)
+            front(g, 1)
+            if g >= 1:
+                back(g - 1)
+            if g + 2 < GROUPS:
+                gather(g + 2)
+        turn(GROUPS - 1)
+        combine(0)
+        back(GROUPS - 1)
+        combine(1)
+        sum01 = held([P, T], F32, "sum01")
+        combine(2)
+        nc.vector.tensor_tensor(sum01[:], prod[0][:], prod[1][:], ADD)
+        combine(3)
+        sum2s = held([P, T], F32, "sum2s")
+        nc.vector.tensor_tensor(sum2s[:], shared["y"][:], prod[2][:], ADD)
+        halves = (slice(0, C), slice(C, T))
+        part = [held([P, C], F32, "part%d" % i) for i in range(2)]
+        res = [held([P, C], F32, "res%d" % i) for i in range(2)]
+        for i in range(2):
+            nc.vector.tensor_tensor(part[i][:], sum01[:, halves[i]], prod[3][:, halves[i]], ADD)
+        for i in range(2):
+            nc.vector.tensor_tensor(res[i][:], part[i][:], sum2s[:, halves[i]], ADD)
+            nc.sync.dma_start(out[:, halves[i]], res[i][:])

@@ -20,7 +20,10 @@ ADD = mybir.AluOpType.add
 
 P = 128
 GROUPS = E + T // C
-CHUNKS = ((0, 1), (1, 3), (3, 8))
+CHUNKS = ((0, 1), (1, 4), (4, 8))
+VECTOR_COPIES = (4, 5, 6)
+EARLY = 3
+HALF = H // 2
 
 
 def tile_moe_shf_glu_gelu_kernel(
@@ -52,22 +55,30 @@ def tile_moe_shf_glu_gelu_kernel(
             nc.sync.dma_start(t[:].bitcast(I32), src[lo:hi, 0].rearrange("e p n -> p e n").bitcast(I32))
             return t
 
+        def spread_plane(src, name):
+            t = held([P, src.shape[1]], U8, name)
+            for q in range(4):
+                rows = src[4 * q:4 * q + 4, :].bitcast(I32)
+                nc.sync.dma_start(t[32 * q:32 * q + 32, :].bitcast(I32), rows.unsqueeze(0).to_broadcast([8, 4, rows.shape[1]]))
+            return t
+
         def zeroed_planes(src, name):
             t = held([P, src.shape[0], src.shape[-1]], U8, name)
             nc.vector.memset(t[:].rearrange("p e n -> p (e n)").bitcast(I32), 0)
             return t
 
-        def load_planes(t, src):
+        def load_planes(t, src, queue=nc.sync):
             for r in range(4):
-                nc.sync.dma_start(t[r:P:32].bitcast(I32), src[:, r:16:4, :].rearrange("e q n -> q e n").bitcast(I32))
+                queue.dma_start(t[r:P:32].bitcast(I32), src[:, r:16:4, :].rearrange("e q n -> q e n").bitcast(I32))
 
-        xs3 = zeroed_planes(x_scales, "xs3")
-        s1 = zeroed_planes(w1_scales, "s1")
-        s3 = zeroed_planes(w3_scales, "s3")
+        s1 = [zeroed_planes(w1_scales[0:EARLY, 0], "s1a")]
+        s3 = [zeroed_planes(w3_scales[0:EARLY, 0], "s3a")]
         warm = held([P, 1], F32, "warm")
         nc.vector.memset(warm[:], 0.0)
         warm_out = held([P, 1], F32, "warm_out")
         nc.scalar.activation(warm_out[:], warm[:], GELU)
+        s1.append(zeroed_planes(w1_scales[EARLY:E, 0], "s1b"))
+        s3.append(zeroed_planes(w3_scales[EARLY:E, 0], "s3b"))
         s2 = zeroed_planes(w2_scales, "s2")
         s1s = zeroed_planes(w1s_scales, "s1s")
         s3s = zeroed_planes(w3s_scales, "s3s")
@@ -75,36 +86,41 @@ def tile_moe_shf_glu_gelu_kernel(
         ident = held([P, P], F32, "ident")
         make_identity(nc, ident[:])
 
-        offs_t = load_list(offs, "offs_t")
         xw = load_fp8_words(x_words, "xw")
-        load_planes(xs3, x_scales)
-        xs = xs3[:, 0, :]
-        w1_t = [load_fp4_words(w1_words, 0, 1, "w1_0")]
-        w3_t = [load_fp4_words(w3_words, 0, 1, "w3_0")]
-        load_planes(s1, w1_scales[:, 0])
-        load_planes(s3, w3_scales[:, 0])
-        w1_t.append(load_fp4_words(w1_words, 1, 3, "w1_1"))
-        w3_t.append(load_fp4_words(w3_words, 1, 3, "w3_1"))
+        xs = spread_plane(x_scales[0], "xs")
+        offs_t = load_list(offs, "offs_t")
+        w1_t = [load_fp4_words(w1_words, *CHUNKS[0], "w1_0")]
+        load_planes(s1[0], w1_scales[0:EARLY, 0])
+        w3_t = [load_fp4_words(w3_words, *CHUNKS[0], "w3_0")]
+        load_planes(s3[0], w3_scales[0:EARLY, 0])
+        load_planes(s1[1], w1_scales[EARLY:E, 0], nc.gpsimd)
+        load_planes(s3[1], w3_scales[EARLY:E, 0], nc.gpsimd)
+        w1_t.append(load_fp4_words(w1_words, *CHUNKS[1], "w1_1"))
+        w3_t.append(load_fp4_words(w3_words, *CHUNKS[1], "w3_1"))
         load_planes(s2, w2_scales[:, 0])
         w2_t = load_fp4_words(w2_words, 0, E, "w2_t")
-        w1_t.append(load_fp4_words(w1_words, 3, 8, "w1_2"))
-        w3_t.append(load_fp4_words(w3_words, 3, 8, "w3_2"))
+        w1_t.append(load_fp4_words(w1_words, *CHUNKS[2], "w1_2"))
+        w3_t.append(load_fp4_words(w3_words, *CHUNKS[2], "w3_2"))
         w1s_t = load_fp8_words(w1s_words, "w1s_t")
         w3s_t = load_fp8_words(w3s_words, "w3s_t")
         w2s_t = load_fp8_words(w2s_words, "w2s_t")
-        load_planes(s1s, w1s_scales)
-        load_planes(s3s, w3s_scales)
-        load_planes(s2s, w2s_scales)
+        load_planes(s1s, w1s_scales, nc.gpsimd)
+        load_planes(s3s, w3s_scales, nc.gpsimd)
+        load_planes(s2s, w2s_scales, nc.gpsimd)
         pos_t = [load_list(src, "pos_t%d" % r) for r, src in enumerate((pos1, pos2, pos3, pos4))]
         gate_t = held([P, TOP, T], F32, "gate_t")
         nc.sync.dma_start(gate_t[:], gate.rearrange("r p t -> p r t"))
 
-        def first_layer(g):
+        def first_layer(g, k):
+            cols = slice(k * HALF, (k + 1) * HALF)
             if g >= E:
-                return ((w1s_t[:].bitcast(FP8X4), s1s[:, 0, :]), (w3s_t[:].bitcast(FP8X4), s3s[:, 0, :]))
+                return ((w1s_t[:, cols].bitcast(FP8X4), s1s[:, 0, cols]), (w3s_t[:, cols].bitcast(FP8X4), s3s[:, 0, cols]))
             c = [i for i, (lo, hi) in enumerate(CHUNKS) if lo <= g < hi][0]
             j = g - CHUNKS[c][0]
-            return ((w1_t[c][:, j, :].bitcast(FP4X4), s1[:, g, :]), (w3_t[c][:, j, :].bitcast(FP4X4), s3[:, g, :]))
+            d, m = (0, g) if g < EARLY else (1, g - EARLY)
+            pairs = slice(2 * k * HALF, 2 * (k + 1) * HALF)
+            return ((w1_t[c][:, j, pairs].bitcast(FP4X4), s1[d][:, m, cols]),
+                    (w3_t[c][:, j, pairs].bitcast(FP4X4), s3[d][:, m, cols]))
 
         def second_layer(g):
             if g >= E:
@@ -123,31 +139,34 @@ def tile_moe_shf_glu_gelu_kernel(
                 tokens[g] = (xw[:, cols], xs[:, cols])
                 return
             idx = offs_t[:, g * C // 16:(g + 1) * C // 16]
-            words = ring.tile([P, C], U32, name="words", align_bytes=64)
-            scales = ring.tile([P, C], U8, name="scales", align_bytes=64)
+            words = ring.tile([P, C], U32, name="words", align_bytes=64, bufs=4)
+            scales = ring.tile([P, C], U8, name="scales", align_bytes=64, bufs=4)
             nc.vector.tensor_copy(words[:], xw[:].bitcast(U32).indirect(idx))
-            nc.vector.tensor_copy(scales[:], xs.indirect(idx))
+            nc.vector.tensor_copy(scales[:], xs[:].indirect(idx))
             tokens[g] = (words[:], scales[:])
 
-        def front(g, j):
+        def front(g, k):
             words, scales = tokens[g]
-            cols = slice(j * P, (j + 1) * P)
-            a = psum.tile([P, H], F32, name="a", bufs=2)
-            b = psum.tile([P, H], F32, name="b", bufs=3)
-            for acc, (w, s) in zip((a, b), first_layer(g)):
-                nc.tensor.matmul_mx(out=acc[:], lhsT=words[:, cols].bitcast(FP8X4), lhsT_scale=scales[:, cols],
-                                    rhs=w, rhs_scale=s, start=True, stop=True)
+            a = psum.tile([P, 2, HALF], F32, name="a", bufs=3)
+            b = psum.tile([P, 2, HALF], F32, name="b", bufs=3)
+            for acc, (w, s) in zip((a, b), first_layer(g, k)):
+                for j in range(2):
+                    cols = slice(j * P, (j + 1) * P)
+                    nc.tensor.matmul_mx(out=acc[:, j, :], lhsT=words[:, cols].bitcast(FP8X4), lhsT_scale=scales[:, cols],
+                                        rhs=w, rhs_scale=s, start=True, stop=True)
+            order = "s j (p u e) -> s u (j p) e"
             act = ring.tile([P, 2, P, 2], F32, name="act")
-            nc.scalar.activation(act[:], a[:].rearrange("s (p u e) -> s u p e", u=2, e=2), GELU)
-            h[g, j] = ring.tile([P, 2, P, 2], BF16, name="h", bufs=4)
-            nc.vector.tensor_tensor(h[g, j][:], b[:].rearrange("s (p u e) -> s u p e", u=2, e=2), act[:], MULT)
+            nc.scalar.activation(act[:], a[:].rearrange(order, u=2, e=2), GELU)
+            if k == 0:
+                h[g] = ring.tile([P, 2, 2, 2, P], BF16, name="h")
+            nc.vector.tensor_tensor(h[g][:, :, :, k, :], b[:].rearrange(order, u=2, e=2), act[:], MULT)
 
         def turn(g):
-            turned = psum.tile([P, 2, 2, P], F32, name="turned", bufs=2)
+            turned = psum.tile([P, 2, 2, P], F32, name="turned")
             for j in range(2):
-                pairs = h[g, j][:].rearrange("s u p e -> s (u p e)").bitcast(F32)
                 for u in range(2):
-                    nc.tensor.transpose(turned[:, j, u, :], pairs[:, u * P:(u + 1) * P], ident[:])
+                    pairs = h[g][:, u, j, :, :].rearrange("s k c -> s (k c)").bitcast(F32)
+                    nc.tensor.transpose(turned[:, j, u, :], pairs, ident[:])
             h_t[g] = ring.tile([P, C * 4], BF16, name="h_t", align_bytes=64)
             nc.scalar.copy(h_t[g][:].bitcast(F32).rearrange("p (j s u) -> p j s u", j=2, u=2),
                            turned[:].rearrange("p j u s -> p j s u"))
@@ -163,7 +182,9 @@ def tile_moe_shf_glu_gelu_kernel(
             y = shared["y"][:, cols]
             nc.tensor.matmul_mx(out=y, lhsT=w, lhsT_scale=s, rhs=codes[:].bitcast(FP8X4), rhs_scale=planes[:],
                                 start=True, stop=True)
-            if g < E:
+            if g in VECTOR_COPIES:
+                nc.vector.tensor_copy(y_all[:, g * C:(g + 1) * C], y)
+            elif g < E:
                 nc.scalar.copy(y_all[:, g * C:(g + 1) * C], y)
 
         prod = {}
@@ -173,16 +194,16 @@ def tile_moe_shf_glu_gelu_kernel(
             nc.vector.tensor_tensor(prod[r][:], y_all[:].indirect(pos_t[r][:]), gate_t[:, r, :], MULT)
 
         gather(0)
-        gather(1)
         for g in range(GROUPS):
             front(g, 0)
+            if g + 1 < GROUPS:
+                gather(g + 1)
             if g >= 1:
                 turn(g - 1)
             front(g, 1)
-            if g >= 1:
-                back(g - 1)
-            if g + 2 < GROUPS:
-                gather(g + 2)
+            if g >= 2:
+                back(g - 2)
+        back(GROUPS - 2)
         turn(GROUPS - 1)
         combine(0)
         back(GROUPS - 1)

@@ -21,8 +21,10 @@ ADD = mybir.AluOpType.add
 P = 128
 GROUPS = E + T // C
 CHUNKS = ((0, 1), (1, 4), (4, 8))
-VECTOR_COPIES = (4, 5, 6)
-EARLY = 3
+VECTOR_COPIES = (5, 6)
+EARLY = 4
+WORD_SLOTS = (0, 1, 2, 3, 0, 1, 2, 0)
+SCALE_SLOTS = (0, 1, 2, 3, 0, 1, 3, 3)
 HALF = H // 2
 
 
@@ -55,39 +57,38 @@ def tile_moe_shf_glu_gelu_kernel(
             nc.sync.dma_start(t[:].bitcast(I32), src[lo:hi, 0].rearrange("e p n -> p e n").bitcast(I32))
             return t
 
-        def spread_plane(src, name):
-            t = held([P, src.shape[1]], U8, name)
+        def spread_plane(t, src, queue=nc.sync):
             for q in range(4):
                 rows = src[4 * q:4 * q + 4, :].bitcast(I32)
-                nc.sync.dma_start(t[32 * q:32 * q + 32, :].bitcast(I32), rows.unsqueeze(0).to_broadcast([8, 4, rows.shape[1]]))
-            return t
+                queue.dma_start(t[32 * q:32 * q + 32, :].bitcast(I32),
+                                rows.unsqueeze(0).to_broadcast([8, 4, rows.shape[1]]))
 
-        def zeroed_planes(src, name):
+        def zeroed_planes(src, name, engine):
             t = held([P, src.shape[0], src.shape[-1]], U8, name)
-            nc.vector.memset(t[:].rearrange("p e n -> p (e n)").bitcast(I32), 0)
+            engine.memset(t[:].rearrange("p e n -> p (e n)").bitcast(I32), 0)
             return t
 
         def load_planes(t, src, queue=nc.sync):
             for r in range(4):
                 queue.dma_start(t[r:P:32].bitcast(I32), src[:, r:16:4, :].rearrange("e q n -> q e n").bitcast(I32))
 
-        s1 = [zeroed_planes(w1_scales[0:EARLY, 0], "s1a")]
-        s3 = [zeroed_planes(w3_scales[0:EARLY, 0], "s3a")]
-        warm = held([P, 1], F32, "warm")
-        nc.vector.memset(warm[:], 0.0)
-        warm_out = held([P, 1], F32, "warm_out")
-        nc.scalar.activation(warm_out[:], warm[:], GELU)
-        s1.append(zeroed_planes(w1_scales[EARLY:E, 0], "s1b"))
-        s3.append(zeroed_planes(w3_scales[EARLY:E, 0], "s3b"))
-        s2 = zeroed_planes(w2_scales, "s2")
-        s1s = zeroed_planes(w1s_scales, "s1s")
-        s3s = zeroed_planes(w3s_scales, "s3s")
-        s2s = zeroed_planes(w2s_scales, "s2s")
+        xw = held([P, T], I32, "xw")
+        xs = held([P, T], U8, "xs")
+        s1 = [zeroed_planes(w1_scales[0:EARLY, 0], "s1a", nc.vector)]
+        s3 = [zeroed_planes(w3_scales[0:EARLY, 0], "s3a", nc.vector)]
         ident = held([P, P], F32, "ident")
         make_identity(nc, ident[:])
+        warm = held([P, 1], F32, "warm")
+        nc.scalar.activation(warm[:], ident[:, 0:1], GELU)
+        s1.append(zeroed_planes(w1_scales[EARLY:E, 0], "s1b", nc.gpsimd))
+        s3.append(zeroed_planes(w3_scales[EARLY:E, 0], "s3b", nc.gpsimd))
+        s2 = zeroed_planes(w2_scales, "s2", nc.gpsimd)
+        s1s = held([P, H], U8, "s1s")
+        s3s = held([P, H], U8, "s3s")
+        s2s = held([P, N], U8, "s2s")
 
-        xw = load_fp8_words(x_words, "xw")
-        xs = spread_plane(x_scales[0], "xs")
+        nc.sync.dma_start(xw[:], x_words[0].rearrange("p n d -> p (n d)").bitcast(I32))
+        spread_plane(xs, x_scales[0])
         offs_t = load_list(offs, "offs_t")
         w1_t = [load_fp4_words(w1_words, *CHUNKS[0], "w1_0")]
         load_planes(s1[0], w1_scales[0:EARLY, 0])
@@ -104,9 +105,9 @@ def tile_moe_shf_glu_gelu_kernel(
         w1s_t = load_fp8_words(w1s_words, "w1s_t")
         w3s_t = load_fp8_words(w3s_words, "w3s_t")
         w2s_t = load_fp8_words(w2s_words, "w2s_t")
-        load_planes(s1s, w1s_scales, nc.gpsimd)
-        load_planes(s3s, w3s_scales, nc.gpsimd)
-        load_planes(s2s, w2s_scales, nc.gpsimd)
+        spread_plane(s1s, w1s_scales[0], nc.gpsimd)
+        spread_plane(s3s, w3s_scales[0])
+        spread_plane(s2s, w2s_scales[0])
         pos_t = [load_list(src, "pos_t%d" % r) for r, src in enumerate((pos1, pos2, pos3, pos4))]
         gate_t = held([P, TOP, T], F32, "gate_t")
         nc.sync.dma_start(gate_t[:], gate.rearrange("r p t -> p r t"))
@@ -114,7 +115,7 @@ def tile_moe_shf_glu_gelu_kernel(
         def first_layer(g, k):
             cols = slice(k * HALF, (k + 1) * HALF)
             if g >= E:
-                return ((w1s_t[:, cols].bitcast(FP8X4), s1s[:, 0, cols]), (w3s_t[:, cols].bitcast(FP8X4), s3s[:, 0, cols]))
+                return ((w1s_t[:, cols].bitcast(FP8X4), s1s[:, cols]), (w3s_t[:, cols].bitcast(FP8X4), s3s[:, cols]))
             c = [i for i, (lo, hi) in enumerate(CHUNKS) if lo <= g < hi][0]
             j = g - CHUNKS[c][0]
             d, m = (0, g) if g < EARLY else (1, g - EARLY)
@@ -124,7 +125,7 @@ def tile_moe_shf_glu_gelu_kernel(
 
         def second_layer(g):
             if g >= E:
-                return w2s_t[:].bitcast(FP8X4), s2s[:, 0, :]
+                return w2s_t[:].bitcast(FP8X4), s2s[:]
             return w2_t[:, g, :].bitcast(FP4X4), s2[:, g, :]
 
         tokens = {}
@@ -134,16 +135,16 @@ def tile_moe_shf_glu_gelu_kernel(
         shared = {}
 
         def gather(g):
-            if g >= E:
-                cols = slice((g - E) * C, (g - E + 1) * C)
-                tokens[g] = (xw[:, cols], xs[:, cols])
-                return
             idx = offs_t[:, g * C // 16:(g + 1) * C // 16]
-            words = ring.tile([P, C], U32, name="words", align_bytes=64, bufs=4)
-            scales = ring.tile([P, C], U8, name="scales", align_bytes=64, bufs=4)
+            words = held([P, C], U32, "words%d" % WORD_SLOTS[g])
+            scales = held([P, C], U8, "scales%d" % SCALE_SLOTS[g])
             nc.vector.tensor_copy(words[:], xw[:].bitcast(U32).indirect(idx))
             nc.vector.tensor_copy(scales[:], xs[:].indirect(idx))
             tokens[g] = (words[:], scales[:])
+
+        for g in range(E, GROUPS):
+            cols = slice((g - E) * C, (g - E + 1) * C)
+            tokens[g] = (xw[:, cols], xs[:, cols])
 
         def front(g, k):
             words, scales = tokens[g]
@@ -167,7 +168,10 @@ def tile_moe_shf_glu_gelu_kernel(
                 for u in range(2):
                     pairs = h[g][:, u, j, :, :].rearrange("s k c -> s (k c)").bitcast(F32)
                     nc.tensor.transpose(turned[:, j, u, :], pairs, ident[:])
-            h_t[g] = ring.tile([P, C * 4], BF16, name="h_t", align_bytes=64)
+            if g == GROUPS - 1:
+                h_t[g] = held([P, C * 4], BF16, "last")
+            else:
+                h_t[g] = ring.tile([P, C * 4], BF16, name="h_t", align_bytes=64)
             nc.scalar.copy(h_t[g][:].bitcast(F32).rearrange("p (j s u) -> p j s u", j=2, u=2),
                            turned[:].rearrange("p j u s -> p j s u"))
 
@@ -190,13 +194,13 @@ def tile_moe_shf_glu_gelu_kernel(
         prod = {}
 
         def combine(r):
-            prod[r] = held([P, T], F32, "prod%d" % r)
+            prod[r] = held([P, T], F32, "last" if r == TOP - 1 else "prod%d" % r)
             nc.vector.tensor_tensor(prod[r][:], y_all[:].indirect(pos_t[r][:]), gate_t[:, r, :], MULT)
 
         gather(0)
         for g in range(GROUPS):
             front(g, 0)
-            if g + 1 < GROUPS:
+            if g + 1 < E:
                 gather(g + 1)
             if g >= 1:
                 turn(g - 1)
@@ -207,18 +211,25 @@ def tile_moe_shf_glu_gelu_kernel(
         turn(GROUPS - 1)
         combine(0)
         back(GROUPS - 1)
-        combine(1)
-        sum01 = held([P, T], F32, "sum01")
-        combine(2)
-        nc.vector.tensor_tensor(sum01[:], prod[0][:], prod[1][:], ADD)
-        combine(3)
-        sum2s = held([P, T], F32, "sum2s")
-        nc.vector.tensor_tensor(sum2s[:], shared["y"][:], prod[2][:], ADD)
+        for r in range(1, TOP):
+            combine(r)
+
+        sums = [psum.tile([P, P], F32, name="a", bufs=3) for j in range(3)]
+        sums.append(psum.tile([P, P], F32, name="b", bufs=3))
+        for r in range(TOP - 1):
+            for j in range(4):
+                nc.tensor.matmul(sums[j][:], prod[r][:, j * P:(j + 1) * P], ident[:], is_transpose=True,
+                                 start=(r == 0), stop=(r == TOP - 2))
+        three = [psum.tile([P, 2, P], F32, name="b", bufs=3) for i in range(2)]
+        for j in range(4):
+            flipped = held([P, P], F32, "flipped%d" % j)
+            nc.scalar.copy(flipped[:], sums[j][:])
+            nc.tensor.transpose(three[j // 2][:, j % 2, :], flipped[:], ident[:])
         halves = (slice(0, C), slice(C, T))
         part = [held([P, C], F32, "part%d" % i) for i in range(2)]
-        res = [held([P, C], F32, "res%d" % i) for i in range(2)]
         for i in range(2):
-            nc.vector.tensor_tensor(part[i][:], sum01[:, halves[i]], prod[3][:, halves[i]], ADD)
+            nc.vector.tensor_tensor(part[i][:], shared["y"][:, halves[i]], prod[TOP - 1][:, halves[i]], ADD)
         for i in range(2):
-            nc.vector.tensor_tensor(res[i][:], part[i][:], sum2s[:, halves[i]], ADD)
-            nc.sync.dma_start(out[:, halves[i]], res[i][:])
+            res = held([P, C], F32, "res%d" % i)
+            nc.vector.tensor_tensor(res[:], three[i][:].rearrange("p j t -> p (j t)"), part[i][:], ADD)
+            nc.sync.dma_start(out[:, halves[i]], res[:])

@@ -21,10 +21,11 @@ ADD = mybir.AluOpType.add
 P = 128
 GROUPS = E + T // C
 CHUNKS = ((0, 1), (1, 4), (4, 8))
-VECTOR_COPIES = (5, 6)
-EARLY = 4
-WORD_SLOTS = (0, 1, 2, 3, 0, 1, 2, 0)
-SCALE_SLOTS = (0, 1, 2, 3, 0, 1, 3, 3)
+VECTOR_COPIES = (1, 6,)
+EARLY = 5
+WARM_PASSES = 3
+WORD_SLOTS = (0, 1, 2, 0, 1, 2, 6, 1)
+SCALE_SLOTS = (0, 1, 2, 3, 0, 1, 3, 1)
 HALF = H // 2
 
 
@@ -57,8 +58,8 @@ def tile_moe_shf_glu_gelu_kernel(
             nc.sync.dma_start(t[:].bitcast(I32), src[lo:hi, 0].rearrange("e p n -> p e n").bitcast(I32))
             return t
 
-        def spread_plane(t, src, queue=nc.sync):
-            for q in range(4):
+        def spread_plane(t, src, queue=nc.sync, quadrants=range(4)):
+            for q in quadrants:
                 rows = src[4 * q:4 * q + 4, :].bitcast(I32)
                 queue.dma_start(t[32 * q:32 * q + 32, :].bitcast(I32),
                                 rows.unsqueeze(0).to_broadcast([8, 4, rows.shape[1]]))
@@ -88,8 +89,9 @@ def tile_moe_shf_glu_gelu_kernel(
         s2s = held([P, N], U8, "s2s")
 
         nc.sync.dma_start(xw[:], x_words[0].rearrange("p n d -> p (n d)").bitcast(I32))
-        spread_plane(xs, x_scales[0])
+        spread_plane(xs, x_scales[0], quadrants=(0, 1))
         offs_t = load_list(offs, "offs_t")
+        spread_plane(xs, x_scales[0], quadrants=(2, 3))
         w1_t = [load_fp4_words(w1_words, *CHUNKS[0], "w1_0")]
         load_planes(s1[0], w1_scales[0:EARLY, 0])
         w3_t = [load_fp4_words(w3_words, *CHUNKS[0], "w3_0")]
@@ -156,18 +158,23 @@ def tile_moe_shf_glu_gelu_kernel(
                     nc.tensor.matmul_mx(out=acc[:, j, :], lhsT=words[:, cols].bitcast(FP8X4), lhsT_scale=scales[:, cols],
                                         rhs=w, rhs_scale=s, start=True, stop=True)
             order = "s j (p u e) -> s u (j p) e"
-            act = ring.tile([P, 2, P, 2], F32, name="act")
+            act = ring.tile([P, 2, P, 2], F32, name="act", bufs=3)
             nc.scalar.activation(act[:], a[:].rearrange(order, u=2, e=2), GELU)
             if k == 0:
                 h[g] = ring.tile([P, 2, 2, 2, P], BF16, name="h")
             nc.vector.tensor_tensor(h[g][:, :, :, k, :], b[:].rearrange(order, u=2, e=2), act[:], MULT)
 
+        turned_of = {}
+
         def turn(g):
-            turned = psum.tile([P, 2, 2, P], F32, name="turned")
+            turned = turned_of[g] = psum.tile([P, 2, 2, P], F32, name="turned")
             for j in range(2):
                 for u in range(2):
                     pairs = h[g][:, u, j, :, :].rearrange("s k c -> s (k c)").bitcast(F32)
                     nc.tensor.transpose(turned[:, j, u, :], pairs, ident[:])
+
+        def interleave(g):
+            turned = turned_of[g]
             if g == GROUPS - 1:
                 h_t[g] = held([P, C * 4], BF16, "last")
             else:
@@ -197,18 +204,26 @@ def tile_moe_shf_glu_gelu_kernel(
             prod[r] = held([P, T], F32, "last" if r == TOP - 1 else "prod%d" % r)
             nc.vector.tensor_tensor(prod[r][:], y_all[:].indirect(pos_t[r][:]), gate_t[:, r, :], MULT)
 
+        idle = psum.tile([P, T], F32, name="turned")
+        for i in range(WARM_PASSES):
+            nc.tensor.matmul_mx(out=idle[:], lhsT=xw[:, 0:P].bitcast(FP8X4), lhsT_scale=xs[:, 0:P],
+                                rhs=xw[:].bitcast(FP8X4), rhs_scale=xs[:], start=True, stop=True)
+
         gather(0)
         for g in range(GROUPS):
-            front(g, 0)
-            if g + 1 < E:
-                gather(g + 1)
             if g >= 1:
                 turn(g - 1)
+            front(g, 0)
+            if g >= 1:
+                interleave(g - 1)
             front(g, 1)
+            if g + 1 < E:
+                gather(g + 1)
             if g >= 2:
                 back(g - 2)
         back(GROUPS - 2)
         turn(GROUPS - 1)
+        interleave(GROUPS - 1)
         combine(0)
         back(GROUPS - 1)
         for r in range(1, TOP):

@@ -21,11 +21,10 @@ ADD = mybir.AluOpType.add
 P = 128
 GROUPS = E + T // C
 CHUNKS = ((0, 1), (1, 4), (4, 8))
-VECTOR_COPIES = (1, 6,)
 EARLY = 5
 WARM_PASSES = 3
-WORD_SLOTS = (0, 1, 2, 0, 1, 2, 6, 1)
-SCALE_SLOTS = (0, 1, 2, 3, 0, 1, 3, 1)
+WORD_TILES = 3
+SCALE_TILES = 4
 HALF = H // 2
 
 
@@ -138,8 +137,8 @@ def tile_moe_shf_glu_gelu_kernel(
 
         def gather(g):
             idx = offs_t[:, g * C // 16:(g + 1) * C // 16]
-            words = held([P, C], U32, "words%d" % WORD_SLOTS[g])
-            scales = held([P, C], U8, "scales%d" % SCALE_SLOTS[g])
+            words = held([P, C], U32, "words%d" % (g % WORD_TILES))
+            scales = held([P, C], U8, "scales%d" % (g % SCALE_TILES))
             nc.vector.tensor_copy(words[:], xw[:].bitcast(U32).indirect(idx))
             nc.vector.tensor_copy(scales[:], xs[:].indirect(idx))
             tokens[g] = (words[:], scales[:])
@@ -189,20 +188,22 @@ def tile_moe_shf_glu_gelu_kernel(
             w, s = second_layer(g)
             if g <= E:
                 shared["y"] = psum.tile([P, T], F32, name="y")
-            cols = slice(0, C) if g <= E else slice(C, 2 * C)
-            y = shared["y"][:, cols]
+            if g >= E:
+                for j in range(2):
+                    cols = slice(j * P, (j + 1) * P)
+                    block = 2 * (g - E) + j
+                    nc.tensor.matmul_mx(out=shared["y"][:, block * N:(block + 1) * N],
+                                        lhsT=codes[:, cols].bitcast(FP8X4), lhsT_scale=planes[:, cols],
+                                        rhs=w, rhs_scale=s, start=True, stop=True)
+                return
+            y = shared["y"][:, 0:C]
             nc.tensor.matmul_mx(out=y, lhsT=w, lhsT_scale=s, rhs=codes[:].bitcast(FP8X4), rhs_scale=planes[:],
                                 start=True, stop=True)
-            if g in VECTOR_COPIES:
-                nc.vector.tensor_copy(y_all[:, g * C:(g + 1) * C], y)
-            elif g < E:
-                nc.scalar.copy(y_all[:, g * C:(g + 1) * C], y)
+            nc.scalar.copy(y_all[:, g * C:(g + 1) * C], y)
 
-        prod = {}
-
-        def combine(r):
-            prod[r] = held([P, T], F32, "last" if r == TOP - 1 else "prod%d" % r)
-            nc.vector.tensor_tensor(prod[r][:], y_all[:].indirect(pos_t[r][:]), gate_t[:, r, :], MULT)
+        def combine(dst, r, cols):
+            idx = pos_t[r][:, cols.start // 16:cols.stop // 16]
+            nc.vector.tensor_tensor(dst[:, cols], y_all[:].indirect(idx), gate_t[:, r, cols], MULT)
 
         idle = psum.tile([P, T], F32, name="turned")
         for i in range(WARM_PASSES):
@@ -224,27 +225,37 @@ def tile_moe_shf_glu_gelu_kernel(
         back(GROUPS - 2)
         turn(GROUPS - 1)
         interleave(GROUPS - 1)
-        combine(0)
-        back(GROUPS - 1)
-        for r in range(1, TOP):
-            combine(r)
-
-        sums = [psum.tile([P, P], F32, name="a", bufs=3) for j in range(3)]
-        sums.append(psum.tile([P, P], F32, name="b", bufs=3))
-        for r in range(TOP - 1):
-            for j in range(4):
-                nc.tensor.matmul(sums[j][:], prod[r][:, j * P:(j + 1) * P], ident[:], is_transpose=True,
-                                 start=(r == 0), stop=(r == TOP - 2))
-        three = [psum.tile([P, 2, P], F32, name="b", bufs=3) for i in range(2)]
-        for j in range(4):
-            flipped = held([P, P], F32, "flipped%d" % j)
-            nc.scalar.copy(flipped[:], sums[j][:])
-            nc.tensor.transpose(three[j // 2][:, j % 2, :], flipped[:], ident[:])
+        whole = slice(0, T)
         halves = (slice(0, C), slice(C, T))
-        part = [held([P, C], F32, "part%d" % i) for i in range(2)]
+        first = held([P, T], F32, "first")
+        second = held([P, T], F32, "second")
+        combine(first, 0, whole)
+        back(GROUPS - 1)
+        ys = held([P, T], F32, "ys")
+        nc.scalar.copy(ys[:], shared["y"][:])
+        combine(second, 1, whole)
+        late = held([P, 2, T], F32, "last")
+        third, last = late[:, 0, :], late[:, 1, :]
+        sums = [psum.tile([P, 2, P], F32, name="a", bufs=3) for i in range(2)]
+
+        def add_turned(banks, src, blocks, start, stop):
+            for j in blocks:
+                nc.tensor.matmul(banks[j // 2][:, j % 2, :], src[:, j * P:(j + 1) * P], ident[:], is_transpose=True,
+                                 start=start and j % 2 == 0, stop=stop and j % 2 == 1)
+
+        add_turned(sums, first, range(4), True, False)
+        add_turned(sums, second, range(4), False, False)
         for i in range(2):
-            nc.vector.tensor_tensor(part[i][:], shared["y"][:, halves[i]], prod[TOP - 1][:, halves[i]], ADD)
+            combine(third, 2, halves[i])
+            add_turned(sums, third, (2 * i, 2 * i + 1), False, True)
+        combine(last, 3, whole)
+        three = [psum.tile([P, 2, P], F32, name="b", bufs=3) for i in range(2)]
+        add_turned(three, ys, range(4), True, False)
+        flipped = held([P, T], F32, "flipped")
+        for i in range(2):
+            nc.scalar.copy(flipped[:, halves[i]], sums[i][:].rearrange("p j t -> p (j t)"))
+            add_turned(three, flipped, (2 * i, 2 * i + 1), False, True)
         for i in range(2):
             res = held([P, C], F32, "res%d" % i)
-            nc.vector.tensor_tensor(res[:], three[i][:].rearrange("p j t -> p (j t)"), part[i][:], ADD)
+            nc.vector.tensor_tensor(res[:], three[i][:].rearrange("p j t -> p (j t)"), last[:, halves[i]], ADD)
             nc.sync.dma_start(out[:, halves[i]], res[:])

@@ -22,6 +22,7 @@ P = 128
 GROUPS = E + T // C
 CHUNKS = ((0, 1), (1, 4), (4, 8))
 EARLY = 5
+COPY_TURN = 4
 WARM_PASSES = 3
 WORD_TILES = 3
 SCALE_TILES = 4
@@ -199,7 +200,10 @@ def tile_moe_shf_glu_gelu_kernel(
             y = shared["y"][:, 0:C]
             nc.tensor.matmul_mx(out=y, lhsT=w, lhsT_scale=s, rhs=codes[:].bitcast(FP8X4), rhs_scale=planes[:],
                                 start=True, stop=True)
-            nc.scalar.copy(y_all[:, g * C:(g + 1) * C], y)
+            if g % COPY_TURN == COPY_TURN // 2:
+                nc.vector.tensor_copy(y_all[:, g * C:(g + 1) * C], y)
+            else:
+                nc.scalar.copy(y_all[:, g * C:(g + 1) * C], y)
 
         def combine(dst, r, cols):
             idx = pos_t[r][:, cols.start // 16:cols.stop // 16]

@@ -25,7 +25,7 @@ EARLY = 5
 COPY_TURN = 4
 WARM_PASSES = 3
 WORD_TILES = 3
-SCALE_TILES = 4
+SCALE_TILES = 3
 HALF = H // 2
 
 
@@ -89,9 +89,8 @@ def tile_moe_shf_glu_gelu_kernel(
         s2s = held([P, N], U8, "s2s")
 
         nc.sync.dma_start(xw[:], x_words[0].rearrange("p n d -> p (n d)").bitcast(I32))
-        spread_plane(xs, x_scales[0], quadrants=(0, 1))
+        spread_plane(xs, x_scales[0])
         offs_t = load_list(offs, "offs_t")
-        spread_plane(xs, x_scales[0], quadrants=(2, 3))
         w1_t = [load_fp4_words(w1_words, *CHUNKS[0], "w1_0")]
         load_planes(s1[0], w1_scales[0:EARLY, 0])
         w3_t = [load_fp4_words(w3_words, *CHUNKS[0], "w3_0")]

@@ -20,13 +20,17 @@ ADD = mybir.AluOpType.add
 
 P = 128
 GROUPS = E + T // C
-CHUNKS = ((0, 1), (1, 4), (4, 8))
-EARLY = 5
+CHUNKS1 = ((0, 2), (2, 5), (5, 8))
+CHUNKS3 = ((0, 4), (4, 8))
+EARLY1 = 4
+EARLY3 = 3
 COPY_TURN = 4
 WARM_PASSES = 3
-WORD_TILES = 3
-SCALE_TILES = 3
+WORD_TILES = 8
+SCALE_TILES = 8
 HALF = H // 2
+FIRST = 14
+LEAD = 4
 
 
 def tile_moe_shf_glu_gelu_kernel(
@@ -53,9 +57,9 @@ def tile_moe_shf_glu_gelu_kernel(
             nc.sync.dma_start(t[:], src[0].rearrange("p n d -> p (n d)").bitcast(I32))
             return t
 
-        def load_fp4_words(src, lo, hi, name):
+        def load_fp4_words(src, lo, hi, name, queue=nc.sync):
             t = held([P, hi - lo, src.shape[3]], U8, name)
-            nc.sync.dma_start(t[:].bitcast(I32), src[lo:hi, 0].rearrange("e p n -> p e n").bitcast(I32))
+            queue.dma_start(t[:].bitcast(I32), src[lo:hi, 0].rearrange("e p n -> p e n").bitcast(I32))
             return t
 
         def spread_plane(t, src, queue=nc.sync, quadrants=range(4)):
@@ -75,54 +79,52 @@ def tile_moe_shf_glu_gelu_kernel(
 
         xw = held([P, T], I32, "xw")
         xs = held([P, T], U8, "xs")
-        s1 = [zeroed_planes(w1_scales[0:EARLY, 0], "s1a", nc.vector)]
-        s3 = [zeroed_planes(w3_scales[0:EARLY, 0], "s3a", nc.vector)]
+        s1 = zeroed_planes(w1_scales, "s1", nc.vector)
+        s3 = zeroed_planes(w3_scales, "s3", nc.gpsimd)
+        zero = held([P, 1], F32, "zero")
+        nc.vector.memset(zero[:], 0.0)
         ident = held([P, P], F32, "ident")
         make_identity(nc, ident[:])
-        warm = held([P, 1], F32, "warm")
-        nc.scalar.activation(warm[:], ident[:, 0:1], GELU)
-        s1.append(zeroed_planes(w1_scales[EARLY:E, 0], "s1b", nc.gpsimd))
-        s3.append(zeroed_planes(w3_scales[EARLY:E, 0], "s3b", nc.gpsimd))
         s2 = zeroed_planes(w2_scales, "s2", nc.gpsimd)
         s1s = held([P, H], U8, "s1s")
         s3s = held([P, H], U8, "s3s")
         s2s = held([P, N], U8, "s2s")
+        warm = held([P, 1], F32, "warm")
+        nc.scalar.activation(warm[:], zero[:], GELU)
+        gate_t = [held([P, T], F32, "gate%d" % r) for r in range(TOP)]
 
         nc.sync.dma_start(xw[:], x_words[0].rearrange("p n d -> p (n d)").bitcast(I32))
         spread_plane(xs, x_scales[0])
         offs_t = load_list(offs, "offs_t")
-        w1_t = [load_fp4_words(w1_words, *CHUNKS[0], "w1_0")]
-        load_planes(s1[0], w1_scales[0:EARLY, 0])
-        w3_t = [load_fp4_words(w3_words, *CHUNKS[0], "w3_0")]
-        load_planes(s3[0], w3_scales[0:EARLY, 0])
-        load_planes(s1[1], w1_scales[EARLY:E, 0], nc.gpsimd)
-        load_planes(s3[1], w3_scales[EARLY:E, 0], nc.gpsimd)
-        w1_t.append(load_fp4_words(w1_words, *CHUNKS[1], "w1_1"))
-        w3_t.append(load_fp4_words(w3_words, *CHUNKS[1], "w3_1"))
+        w1_t = [load_fp4_words(w1_words, *CHUNKS1[0], "w1_0")]
+        load_planes(s1, w1_scales[:, 0])
+        w1_t.append(load_fp4_words(w1_words, *CHUNKS1[1], "w1_1"))
+        load_planes(s3, w3_scales[:, 0])
+        w1_t.append(load_fp4_words(w1_words, *CHUNKS1[2], "w1_2"))
+        w3_t = [load_fp4_words(w3_words, *CHUNKS3[0], "w3_0")]
+        w3_t.append(load_fp4_words(w3_words, *CHUNKS3[1], "w3_1"))
+        w1s_t = load_fp8_words(w1s_words, "w1s_t")
+        spread_plane(s1s, w1s_scales[0])
         load_planes(s2, w2_scales[:, 0])
         w2_t = load_fp4_words(w2_words, 0, E, "w2_t")
-        w1_t.append(load_fp4_words(w1_words, *CHUNKS[2], "w1_2"))
-        w3_t.append(load_fp4_words(w3_words, *CHUNKS[2], "w3_2"))
-        w1s_t = load_fp8_words(w1s_words, "w1s_t")
         w3s_t = load_fp8_words(w3s_words, "w3s_t")
-        w2s_t = load_fp8_words(w2s_words, "w2s_t")
-        spread_plane(s1s, w1s_scales[0], nc.gpsimd)
         spread_plane(s3s, w3s_scales[0])
+        w2s_t = load_fp8_words(w2s_words, "w2s_t")
         spread_plane(s2s, w2s_scales[0])
-        pos_t = [load_list(src, "pos_t%d" % r) for r, src in enumerate((pos1, pos2, pos3, pos4))]
-        gate_t = held([P, TOP, T], F32, "gate_t")
-        nc.sync.dma_start(gate_t[:], gate.rearrange("r p t -> p r t"))
+        pos_t = []
+        for r, src in enumerate((pos1, pos2, pos3, pos4)):
+            pos_t.append(load_list(src, "pos_t%d" % r))
+            nc.sync.dma_start(gate_t[r][:], gate[r])
 
         def first_layer(g, k):
             cols = slice(k * HALF, (k + 1) * HALF)
             if g >= E:
                 return ((w1s_t[:, cols].bitcast(FP8X4), s1s[:, cols]), (w3s_t[:, cols].bitcast(FP8X4), s3s[:, cols]))
-            c = [i for i, (lo, hi) in enumerate(CHUNKS) if lo <= g < hi][0]
-            j = g - CHUNKS[c][0]
-            d, m = (0, g) if g < EARLY else (1, g - EARLY)
+            c1 = [i for i, (lo, hi) in enumerate(CHUNKS1) if lo <= g < hi][0]
+            c3 = [i for i, (lo, hi) in enumerate(CHUNKS3) if lo <= g < hi][0]
             pairs = slice(2 * k * HALF, 2 * (k + 1) * HALF)
-            return ((w1_t[c][:, j, pairs].bitcast(FP4X4), s1[d][:, m, cols]),
-                    (w3_t[c][:, j, pairs].bitcast(FP4X4), s3[d][:, m, cols]))
+            return ((w1_t[c1][:, g - CHUNKS1[c1][0], pairs].bitcast(FP4X4), s1[:, g, cols]),
+                    (w3_t[c3][:, g - CHUNKS3[c3][0], pairs].bitcast(FP4X4), s3[:, g, cols]))
 
         def second_layer(g):
             if g >= E:
@@ -147,26 +149,44 @@ def tile_moe_shf_glu_gelu_kernel(
             cols = slice((g - E) * C, (g - E + 1) * C)
             tokens[g] = (xw[:, cols], xs[:, cols])
 
-        def front(g, k):
+        order = "s j (p u e) -> s u (j p) e"
+        act = {}
+
+        def bank(i):
+            return "bank%d" % (i % 8)
+
+        def gelu_bank(n):
+            return bank(n if n < 10 else n - 8 if n < FIRST else 4)
+
+        lin = {}
+
+        def project(acc, g, w, s):
             words, scales = tokens[g]
-            a = psum.tile([P, 2, HALF], F32, name="a", bufs=3)
-            b = psum.tile([P, 2, HALF], F32, name="b", bufs=3)
-            for acc, (w, s) in zip((a, b), first_layer(g, k)):
-                for j in range(2):
-                    cols = slice(j * P, (j + 1) * P)
-                    nc.tensor.matmul_mx(out=acc[:, j, :], lhsT=words[:, cols].bitcast(FP8X4), lhsT_scale=scales[:, cols],
-                                        rhs=w, rhs_scale=s, start=True, stop=True)
-            order = "s j (p u e) -> s u (j p) e"
-            act = ring.tile([P, 2, P, 2], F32, name="act", bufs=3)
-            nc.scalar.activation(act[:], a[:].rearrange(order, u=2, e=2), GELU)
+            for j in range(2):
+                cols = slice(j * P, (j + 1) * P)
+                nc.tensor.matmul_mx(out=acc[:, j, :], lhsT=words[:, cols].bitcast(FP8X4), lhsT_scale=scales[:, cols],
+                                    rhs=w, rhs_scale=s, start=True, stop=True)
+
+        def activate(g, k):
+            a = psum.tile([P, 2, HALF], F32, name=gelu_bank(2 * g + k))
+            project(a, g, *first_layer(g, k)[0])
+            act[g, k] = ring.tile([P, 2, P, 2], F32, name="act", bufs=FIRST + 2)
+            nc.scalar.activation(act[g, k][:], a[:].rearrange(order, u=2, e=2), GELU)
+
+        def linear(g, k):
+            lin[g, k] = psum.tile([P, 2, HALF], F32, name=bank(6 + (2 * g + k) % 4))
+            project(lin[g, k], g, *first_layer(g, k)[1])
+
+        def multiply(g, k):
+            b = lin[g, k]
             if k == 0:
-                h[g] = ring.tile([P, 2, 2, 2, P], BF16, name="h")
-            nc.vector.tensor_tensor(h[g][:, :, :, k, :], b[:].rearrange(order, u=2, e=2), act[:], MULT)
+                h[g] = ring.tile([P, 2, 2, 2, P], BF16, name="h", bufs=5)
+            nc.vector.tensor_tensor(h[g][:, :, :, k, :], b[:].rearrange(order, u=2, e=2), act[g, k][:], MULT)
 
         turned_of = {}
 
         def turn(g):
-            turned = turned_of[g] = psum.tile([P, 2, 2, P], F32, name="turned")
+            turned = turned_of[g] = psum.tile([P, 2, 2, P], F32, name=bank(2 + g % 2))
             for j in range(2):
                 for u in range(2):
                     pairs = h[g][:, u, j, :, :].rearrange("s k c -> s (k c)").bitcast(F32)
@@ -182,12 +202,12 @@ def tile_moe_shf_glu_gelu_kernel(
                            turned[:].rearrange("p j u s -> p j s u"))
 
         def back(g):
-            codes = ring.tile([P, C], U32, name="codes", align_bytes=64)
-            planes = ring.tile([P, C], U8, name="planes", align_bytes=64)
+            codes = ring.tile([P, C], U32, name="codes", bufs=4, align_bytes=64)
+            planes = ring.tile([P, C], U8, name="planes", bufs=4, align_bytes=64)
             nc.vector.quantize_mx(out=codes[:].bitcast(FP8X4), scales=planes[:], in_=h_t[g][:])
             w, s = second_layer(g)
             if g <= E:
-                shared["y"] = psum.tile([P, T], F32, name="y")
+                shared["y"] = psum.tile([P, T], F32, name=bank(5))
             if g >= E:
                 for j in range(2):
                     cols = slice(j * P, (j + 1) * P)
@@ -199,35 +219,43 @@ def tile_moe_shf_glu_gelu_kernel(
             y = shared["y"][:, 0:C]
             nc.tensor.matmul_mx(out=y, lhsT=w, lhsT_scale=s, rhs=codes[:].bitcast(FP8X4), rhs_scale=planes[:],
                                 start=True, stop=True)
-            if g % COPY_TURN == COPY_TURN // 2:
+            if g >= E:
                 nc.vector.tensor_copy(y_all[:, g * C:(g + 1) * C], y)
             else:
                 nc.scalar.copy(y_all[:, g * C:(g + 1) * C], y)
 
         def combine(dst, r, cols):
             idx = pos_t[r][:, cols.start // 16:cols.stop // 16]
-            nc.vector.tensor_tensor(dst[:, cols], y_all[:].indirect(idx), gate_t[:, r, cols], MULT)
+            nc.vector.tensor_tensor(dst[:, cols], y_all[:].indirect(idx), gate_t[r][:, cols], MULT)
 
-        idle = psum.tile([P, T], F32, name="turned")
+        idle = psum.tile([P, T], F32, name=bank(7))
         for i in range(WARM_PASSES):
             nc.tensor.matmul_mx(out=idle[:], lhsT=xw[:, 0:P].bitcast(FP8X4), lhsT_scale=xs[:, 0:P],
                                 rhs=xw[:].bitcast(FP8X4), rhs_scale=xs[:], start=True, stop=True)
 
-        gather(0)
+        for n in range(FIRST):
+            if n % 2 == 0:
+                gather(n // 2)
+            activate(n // 2, n % 2)
+        for g in range(FIRST // 2, E):
+            gather(g)
+        for i in range(4):
+            linear(i // 2, i % 2)
         for g in range(GROUPS):
-            if g >= 1:
-                turn(g - 1)
-            front(g, 0)
-            if g >= 1:
-                interleave(g - 1)
-            front(g, 1)
-            if g + 1 < E:
-                gather(g + 1)
-            if g >= 2:
+            multiply(g, 0)
+            if g + 2 < GROUPS:
+                linear(g + 2, 0)
+            multiply(g, 1)
+            turn(g)
+            interleave(g)
+            if 2 <= g <= E:
                 back(g - 2)
-        back(GROUPS - 2)
-        turn(GROUPS - 1)
-        interleave(GROUPS - 1)
+            if g >= E:
+                back(g - 1)
+            if FIRST + g < 2 * GROUPS:
+                activate((FIRST + g) // 2, (FIRST + g) % 2)
+            if g + 2 < GROUPS:
+                linear(g + 2, 1)
         whole = slice(0, T)
         halves = (slice(0, C), slice(C, T))
         first = held([P, T], F32, "first")
@@ -239,7 +267,7 @@ def tile_moe_shf_glu_gelu_kernel(
         combine(second, 1, whole)
         late = held([P, 2, T], F32, "last")
         third, last = late[:, 0, :], late[:, 1, :]
-        sums = [psum.tile([P, 2, P], F32, name="a", bufs=3) for i in range(2)]
+        sums = [psum.tile([P, 2, P], F32, name=bank(6 + i)) for i in range(2)]
 
         def add_turned(banks, src, blocks, start, stop):
             for j in blocks:
@@ -252,7 +280,7 @@ def tile_moe_shf_glu_gelu_kernel(
             combine(third, 2, halves[i])
             add_turned(sums, third, (2 * i, 2 * i + 1), False, True)
         combine(last, 3, whole)
-        three = [psum.tile([P, 2, P], F32, name="b", bufs=3) for i in range(2)]
+        three = [psum.tile([P, 2, P], F32, name=bank(8 + i)) for i in range(2)]
         add_turned(three, ys, range(4), True, False)
         flipped = held([P, T], F32, "flipped")
         for i in range(2):

@@ -103,10 +103,10 @@ def tile_moe_shf_glu_gelu_kernel(
         w1_t.append(load_fp4_words(w1_words, *CHUNKS1[2], "w1_2"))
         w3_t = [load_fp4_words(w3_words, *CHUNKS3[0], "w3_0")]
         w3_t.append(load_fp4_words(w3_words, *CHUNKS3[1], "w3_1"))
-        w1s_t = load_fp8_words(w1s_words, "w1s_t")
-        spread_plane(s1s, w1s_scales[0])
         load_planes(s2, w2_scales[:, 0])
         w2_t = load_fp4_words(w2_words, 0, E, "w2_t")
+        w1s_t = load_fp8_words(w1s_words, "w1s_t")
+        spread_plane(s1s, w1s_scales[0])
         w3s_t = load_fp8_words(w3s_words, "w3s_t")
         spread_plane(s3s, w3s_scales[0])
         w2s_t = load_fp8_words(w2s_words, "w2s_t")
@@ -186,7 +186,7 @@ def tile_moe_shf_glu_gelu_kernel(
         turned_of = {}
 
         def turn(g):
-            turned = turned_of[g] = psum.tile([P, 2, 2, P], F32, name=bank(2 + g % 2))
+            turned = turned_of[g] = psum.tile([P, 2, 2, P], F32, name=bank(2 + g % 2 if g < GROUPS - 1 else 4))
             for j in range(2):
                 for u in range(2):
                     pairs = h[g][:, u, j, :, :].rearrange("s k c -> s (k c)").bitcast(F32)
@@ -202,12 +202,12 @@ def tile_moe_shf_glu_gelu_kernel(
                            turned[:].rearrange("p j u s -> p j s u"))
 
         def back(g):
-            codes = ring.tile([P, C], U32, name="codes", bufs=4, align_bytes=64)
-            planes = ring.tile([P, C], U8, name="planes", bufs=4, align_bytes=64)
+            codes = ring.tile([P, C], U32, name="codes", bufs=5, align_bytes=64)
+            planes = ring.tile([P, C], U8, name="planes", bufs=5, align_bytes=64)
             nc.vector.quantize_mx(out=codes[:].bitcast(FP8X4), scales=planes[:], in_=h_t[g][:])
             w, s = second_layer(g)
             if g <= E:
-                shared["y"] = psum.tile([P, T], F32, name=bank(5))
+                shared["y"] = psum.tile([P, T], F32, name=bank(2 if g >= E else 5 if g < E - 3 else 4 + (E - 1 - g) % 2))
             if g >= E:
                 for j in range(2):
                     cols = slice(j * P, (j + 1) * P)
@@ -243,17 +243,24 @@ def tile_moe_shf_glu_gelu_kernel(
             linear(i // 2, i % 2)
         for g in range(GROUPS):
             multiply(g, 0)
-            if g + 2 < GROUPS:
+            if g < 7:
                 linear(g + 2, 0)
+                if g >= 3:
+                    back(g - 3)
+            n = FIRST + g - (FIRST + g >= 2 * E)
+            if FIRST + g != 2 * E and n < 2 * GROUPS:
+                activate(n // 2, n % 2)
             multiply(g, 1)
+            if g == E:
+                for late in range(E - 3, E):
+                    back(late)
             turn(g)
             interleave(g)
-            if 2 <= g <= E:
-                back(g - 2)
-            if g >= E:
+            if 7 <= g < E:
+                linear(g + 2, 0)
+                back(g - 3)
+            if g > E:
                 back(g - 1)
-            if FIRST + g < 2 * GROUPS:
-                activate((FIRST + g) // 2, (FIRST + g) % 2)
             if g + 2 < GROUPS:
                 linear(g + 2, 1)
         whole = slice(0, T)

@@ -20,7 +20,7 @@ ADD = mybir.AluOpType.add
 
 P = 128
 GROUPS = E + T // C
-CHUNKS1 = ((0, 2), (2, 5), (5, 8))
+CHUNKS1 = ((0, 2), (2, 6), (6, 8))
 CHUNKS3 = ((0, 4), (4, 8))
 EARLY1 = 4
 EARLY3 = 3
@@ -29,7 +29,6 @@ WARM_PASSES = 3
 WORD_TILES = 8
 SCALE_TILES = 8
 HALF = H // 2
-FIRST = 14
 LEAD = 4
 
 
@@ -99,14 +98,14 @@ def tile_moe_shf_glu_gelu_kernel(
         w1_t = [load_fp4_words(w1_words, *CHUNKS1[0], "w1_0")]
         load_planes(s1, w1_scales[:, 0])
         w1_t.append(load_fp4_words(w1_words, *CHUNKS1[1], "w1_1"))
+        w1s_t = load_fp8_words(w1s_words, "w1s_t")
+        spread_plane(s1s, w1s_scales[0])
         load_planes(s3, w3_scales[:, 0])
-        w1_t.append(load_fp4_words(w1_words, *CHUNKS1[2], "w1_2"))
         w3_t = [load_fp4_words(w3_words, *CHUNKS3[0], "w3_0")]
+        w1_t.append(load_fp4_words(w1_words, *CHUNKS1[2], "w1_2"))
         w3_t.append(load_fp4_words(w3_words, *CHUNKS3[1], "w3_1"))
         load_planes(s2, w2_scales[:, 0])
         w2_t = load_fp4_words(w2_words, 0, E, "w2_t")
-        w1s_t = load_fp8_words(w1s_words, "w1s_t")
-        spread_plane(s1s, w1s_scales[0])
         w3s_t = load_fp8_words(w3s_words, "w3s_t")
         spread_plane(s3s, w3s_scales[0])
         w2s_t = load_fp8_words(w2s_words, "w2s_t")
@@ -155,9 +154,6 @@ def tile_moe_shf_glu_gelu_kernel(
         def bank(i):
             return "bank%d" % (i % 8)
 
-        def gelu_bank(n):
-            return bank(n if n < 10 else n - 8 if n < FIRST else 4)
-
         lin = {}
 
         def project(acc, g, w, s):
@@ -167,10 +163,10 @@ def tile_moe_shf_glu_gelu_kernel(
                 nc.tensor.matmul_mx(out=acc[:, j, :], lhsT=words[:, cols].bitcast(FP8X4), lhsT_scale=scales[:, cols],
                                     rhs=w, rhs_scale=s, start=True, stop=True)
 
-        def activate(g, k):
-            a = psum.tile([P, 2, HALF], F32, name=gelu_bank(2 * g + k))
+        def activate(g, k, place):
+            a = psum.tile([P, 2, HALF], F32, name=bank(place))
             project(a, g, *first_layer(g, k)[0])
-            act[g, k] = ring.tile([P, 2, P, 2], F32, name="act", bufs=FIRST + 2)
+            act[g, k] = ring.tile([P, 2, P, 2], F32, name="act", bufs=2 * GROUPS)
             nc.scalar.activation(act[g, k][:], a[:].rearrange(order, u=2, e=2), GELU)
 
         def linear(g, k):
@@ -207,7 +203,7 @@ def tile_moe_shf_glu_gelu_kernel(
             nc.vector.quantize_mx(out=codes[:].bitcast(FP8X4), scales=planes[:], in_=h_t[g][:])
             w, s = second_layer(g)
             if g <= E:
-                shared["y"] = psum.tile([P, T], F32, name=bank(2 if g >= E else 5 if g < E - 3 else 4 + (E - 1 - g) % 2))
+                shared["y"] = psum.tile([P, T], F32, name=bank(2 if g >= E else 4 + (E - 1 - g) % 2))
             if g >= E:
                 for j in range(2):
                     cols = slice(j * P, (j + 1) * P)
@@ -233,23 +229,28 @@ def tile_moe_shf_glu_gelu_kernel(
             nc.tensor.matmul_mx(out=idle[:], lhsT=xw[:, 0:P].bitcast(FP8X4), lhsT_scale=xs[:, 0:P],
                                 rhs=xw[:].bitcast(FP8X4), rhs_scale=xs[:], start=True, stop=True)
 
-        for n in range(FIRST):
-            if n % 2 == 0:
-                gather(n // 2)
-            activate(n // 2, n % 2)
-        for g in range(FIRST // 2, E):
+        def both_gelus(g, place):
+            activate(g, 0, place)
+            activate(g, 1, place + 1)
+
+        for g in range(E):
             gather(g)
+            if g < E - 3:
+                both_gelus(g, 2 * g)
+        both_gelus(E, 2)
+        both_gelus(E - 3, 4)
         for i in range(4):
             linear(i // 2, i % 2)
+        both_gelus(E - 2, 2)
+        both_gelus(E - 1, 4)
         for g in range(GROUPS):
             multiply(g, 0)
             if g < 7:
                 linear(g + 2, 0)
                 if g >= 3:
                     back(g - 3)
-            n = FIRST + g - (FIRST + g >= 2 * E)
-            if FIRST + g != 2 * E and n < 2 * GROUPS:
-                activate(n // 2, n % 2)
+            if 1 <= g < 1 + 2:
+                activate(GROUPS - 1, g - 1, 4 + g - 1)
             multiply(g, 1)
             if g == E:
                 for late in range(E - 3, E):

@@ -20,12 +20,11 @@ ADD = mybir.AluOpType.add
 
 P = 128
 GROUPS = E + T // C
-CHUNKS1 = ((0, 2), (2, 6), (6, 8))
+CHUNKS1 = ((0, 6), (6, 8))
 CHUNKS3 = ((0, 4), (4, 8))
-EARLY1 = 4
+EARLY1 = 2
 EARLY3 = 3
 COPY_TURN = 4
-WARM_PASSES = 3
 WORD_TILES = 8
 SCALE_TILES = 8
 HALF = H // 2
@@ -78,31 +77,28 @@ def tile_moe_shf_glu_gelu_kernel(
 
         xw = held([P, T], I32, "xw")
         xs = held([P, T], U8, "xs")
-        s1 = zeroed_planes(w1_scales, "s1", nc.vector)
+        s1 = [zeroed_planes(w1_scales[0:EARLY1, 0], "s1a", nc.vector),
+              zeroed_planes(w1_scales[EARLY1:E, 0], "s1b", nc.vector)]
         s3 = zeroed_planes(w3_scales, "s3", nc.gpsimd)
-        zero = held([P, 1], F32, "zero")
-        nc.vector.memset(zero[:], 0.0)
         ident = held([P, P], F32, "ident")
         make_identity(nc, ident[:])
         s2 = zeroed_planes(w2_scales, "s2", nc.gpsimd)
         s1s = held([P, H], U8, "s1s")
         s3s = held([P, H], U8, "s3s")
         s2s = held([P, N], U8, "s2s")
-        warm = held([P, 1], F32, "warm")
-        nc.scalar.activation(warm[:], zero[:], GELU)
         gate_t = [held([P, T], F32, "gate%d" % r) for r in range(TOP)]
 
         nc.sync.dma_start(xw[:], x_words[0].rearrange("p n d -> p (n d)").bitcast(I32))
         spread_plane(xs, x_scales[0])
         offs_t = load_list(offs, "offs_t")
         w1_t = [load_fp4_words(w1_words, *CHUNKS1[0], "w1_0")]
-        load_planes(s1, w1_scales[:, 0])
-        w1_t.append(load_fp4_words(w1_words, *CHUNKS1[1], "w1_1"))
+        load_planes(s1[0], w1_scales[0:EARLY1, 0])
+        load_planes(s1[1], w1_scales[EARLY1:E, 0])
         w1s_t = load_fp8_words(w1s_words, "w1s_t")
         spread_plane(s1s, w1s_scales[0])
-        load_planes(s3, w3_scales[:, 0])
         w3_t = [load_fp4_words(w3_words, *CHUNKS3[0], "w3_0")]
-        w1_t.append(load_fp4_words(w1_words, *CHUNKS1[2], "w1_2"))
+        load_planes(s3, w3_scales[:, 0])
+        w1_t.append(load_fp4_words(w1_words, *CHUNKS1[1], "w1_1"))
         w3_t.append(load_fp4_words(w3_words, *CHUNKS3[1], "w3_1"))
         load_planes(s2, w2_scales[:, 0])
         w2_t = load_fp4_words(w2_words, 0, E, "w2_t")
@@ -122,7 +118,7 @@ def tile_moe_shf_glu_gelu_kernel(
             c1 = [i for i, (lo, hi) in enumerate(CHUNKS1) if lo <= g < hi][0]
             c3 = [i for i, (lo, hi) in enumerate(CHUNKS3) if lo <= g < hi][0]
             pairs = slice(2 * k * HALF, 2 * (k + 1) * HALF)
-            return ((w1_t[c1][:, g - CHUNKS1[c1][0], pairs].bitcast(FP4X4), s1[:, g, cols]),
+            return ((w1_t[c1][:, g - CHUNKS1[c1][0], pairs].bitcast(FP4X4), (s1[0][:, g, cols] if g < EARLY1 else s1[1][:, g - EARLY1, cols])),
                     (w3_t[c3][:, g - CHUNKS3[c3][0], pairs].bitcast(FP4X4), s3[:, g, cols]))
 
         def second_layer(g):
@@ -223,11 +219,6 @@ def tile_moe_shf_glu_gelu_kernel(
         def combine(dst, r, cols):
             idx = pos_t[r][:, cols.start // 16:cols.stop // 16]
             nc.vector.tensor_tensor(dst[:, cols], y_all[:].indirect(idx), gate_t[r][:, cols], MULT)
-
-        idle = psum.tile([P, T], F32, name=bank(7))
-        for i in range(WARM_PASSES):
-            nc.tensor.matmul_mx(out=idle[:], lhsT=xw[:, 0:P].bitcast(FP8X4), lhsT_scale=xs[:, 0:P],
-                                rhs=xw[:].bitcast(FP8X4), rhs_scale=xs[:], start=True, stop=True)
 
         def both_gelus(g, place):
             activate(g, 0, place)

@@ -111,15 +111,13 @@ def tile_moe_shf_glu_gelu_kernel(
             pos_t.append(load_list(src, "pos_t%d" % r))
             nc.sync.dma_start(gate_t[r][:], gate[r])
 
-        def first_layer(g, k):
-            cols = slice(k * HALF, (k + 1) * HALF)
+        def first_layer(g):
             if g >= E:
-                return ((w1s_t[:, cols].bitcast(FP8X4), s1s[:, cols]), (w3s_t[:, cols].bitcast(FP8X4), s3s[:, cols]))
+                return (w1s_t[:].bitcast(FP8X4), s1s[:]), (w3s_t[:].bitcast(FP8X4), s3s[:])
             c1 = [i for i, (lo, hi) in enumerate(CHUNKS1) if lo <= g < hi][0]
             c3 = [i for i, (lo, hi) in enumerate(CHUNKS3) if lo <= g < hi][0]
-            pairs = slice(2 * k * HALF, 2 * (k + 1) * HALF)
-            return ((w1_t[c1][:, g - CHUNKS1[c1][0], pairs].bitcast(FP4X4), (s1[0][:, g, cols] if g < EARLY1 else s1[1][:, g - EARLY1, cols])),
-                    (w3_t[c3][:, g - CHUNKS3[c3][0], pairs].bitcast(FP4X4), s3[:, g, cols]))
+            return ((w1_t[c1][:, g - CHUNKS1[c1][0], :].bitcast(FP4X4), (s1[0][:, g, :] if g < EARLY1 else s1[1][:, g - EARLY1, :])),
+                    (w3_t[c3][:, g - CHUNKS3[c3][0], :].bitcast(FP4X4), s3[:, g, :]))
 
         def second_layer(g):
             if g >= E:
@@ -144,7 +142,7 @@ def tile_moe_shf_glu_gelu_kernel(
             cols = slice((g - E) * C, (g - E + 1) * C)
             tokens[g] = (xw[:, cols], xs[:, cols])
 
-        order = "s j (p u e) -> s u (j p) e"
+        order = "s (p u e) -> s u p e"
         act = {}
 
         def bank(i):
@@ -152,28 +150,27 @@ def tile_moe_shf_glu_gelu_kernel(
 
         lin = {}
 
-        def project(acc, g, w, s):
+        def project(acc, g, k, w, s):
             words, scales = tokens[g]
-            for j in range(2):
-                cols = slice(j * P, (j + 1) * P)
-                nc.tensor.matmul_mx(out=acc[:, j, :], lhsT=words[:, cols].bitcast(FP8X4), lhsT_scale=scales[:, cols],
-                                    rhs=w, rhs_scale=s, start=True, stop=True)
+            cols = slice(k * P, (k + 1) * P)
+            nc.tensor.matmul_mx(out=acc[:], lhsT=words[:, cols].bitcast(FP8X4), lhsT_scale=scales[:, cols],
+                                rhs=w, rhs_scale=s, start=True, stop=True)
 
         def activate(g, k, place):
-            a = psum.tile([P, 2, HALF], F32, name=bank(place))
-            project(a, g, *first_layer(g, k)[0])
+            a = psum.tile([P, H], F32, name=bank(place))
+            project(a, g, k, *first_layer(g)[0])
             act[g, k] = ring.tile([P, 2, P, 2], F32, name="act", bufs=2 * GROUPS)
             nc.scalar.activation(act[g, k][:], a[:].rearrange(order, u=2, e=2), GELU)
 
         def linear(g, k):
-            lin[g, k] = psum.tile([P, 2, HALF], F32, name=bank(6 + (2 * g + k) % 4))
-            project(lin[g, k], g, *first_layer(g, k)[1])
+            lin[g, k] = psum.tile([P, H], F32, name=bank(6 + (2 * g + k) % 4))
+            project(lin[g, k], g, k, *first_layer(g)[1])
 
         def multiply(g, k):
             b = lin[g, k]
             if k == 0:
-                h[g] = ring.tile([P, 2, 2, 2, P], BF16, name="h", bufs=5)
-            nc.vector.tensor_tensor(h[g][:, :, :, k, :], b[:].rearrange(order, u=2, e=2), act[g, k][:], MULT)
+                h[g] = ring.tile([P, 2, 2, HALF], BF16, name="h", bufs=5)
+            nc.vector.tensor_tensor(h[g][:, k], b[:].rearrange(order, u=2, e=2), act[g, k][:], MULT)
 
         turned_of = {}
 
@@ -181,7 +178,7 @@ def tile_moe_shf_glu_gelu_kernel(
             turned = turned_of[g] = psum.tile([P, 2, 2, P], F32, name=bank(2 + g % 2 if g < GROUPS - 1 else 4))
             for j in range(2):
                 for u in range(2):
-                    pairs = h[g][:, u, j, :, :].rearrange("s k c -> s (k c)").bitcast(F32)
+                    pairs = h[g][:, j, u, :].bitcast(F32)
                     nc.tensor.transpose(turned[:, j, u, :], pairs, ident[:])
 
         def interleave(g):
@@ -233,21 +230,26 @@ def tile_moe_shf_glu_gelu_kernel(
         for i in range(4):
             linear(i // 2, i % 2)
         both_gelus(E - 2, 2)
-        both_gelus(E - 1, 4)
         for g in range(GROUPS):
             multiply(g, 0)
             if g < 7:
                 linear(g + 2, 0)
                 if g >= 3:
                     back(g - 3)
-            if 1 <= g < 1 + 2:
-                activate(GROUPS - 1, g - 1, 4 + g - 1)
+            for n, place in {0: ((14, 4),), 1: ((15, 5),), 2: ((18, 4),), 3: ((19, 4),)}.get(g, ()):
+                activate(n // 2, n % 2, place)
             multiply(g, 1)
             if g == E:
                 for late in range(E - 3, E):
                     back(late)
-            turn(g)
-            interleave(g)
+            if g < 0 or g >= 0:
+                turn(g)
+                interleave(g)
+            elif (g - 0) % 2 == 1:
+                turn(g - 1)
+                turn(g)
+                interleave(g - 1)
+                interleave(g)
             if 7 <= g < E:
                 linear(g + 2, 0)
                 back(g - 3)

@@ -19,16 +19,15 @@ MULT = mybir.AluOpType.mult
 ADD = mybir.AluOpType.add
 
 P = 128
+BANKS = 8
 GROUPS = E + T // C
-CHUNKS1 = ((0, 6), (6, 8))
-CHUNKS3 = ((0, 4), (4, 8))
-EARLY1 = 2
-EARLY3 = 3
-COPY_TURN = 4
-WORD_TILES = 8
-SCALE_TILES = 8
-HALF = H // 2
-LEAD = 4
+FIRST_SCALES = 2
+FIRST_W1 = 6
+FIRST_W3 = 4
+LEAD = 2
+LAG = 3
+DEPTH = LAG + 2
+TURN_BANK, SMALL_BANK, LINEAR_BANK = 2, 4, 6
 
 
 def tile_moe_shf_glu_gelu_kernel(
@@ -39,11 +38,14 @@ def tile_moe_shf_glu_gelu_kernel(
     nc = tc.nc
     with ExitStack() as ctx:
         keep = ctx.enter_context(tc.tile_pool(name="keep", bufs=1))
-        ring = ctx.enter_context(tc.tile_pool(name="ring", bufs=3))
+        ring = ctx.enter_context(tc.tile_pool(name="ring", bufs=LAG))
         psum = ctx.enter_context(tc.psum_pool(name="psum", bufs=1))
 
         def held(shape, dtype, name):
             return keep.tile(shape, dtype, name=name, align_bytes=64)
+
+        def banked(shape, place):
+            return psum.tile(shape, F32, name="bank%d" % (place % BANKS))
 
         def load_list(src, name):
             t = keep.tile(list(src.shape), U16, name=name)
@@ -55,30 +57,30 @@ def tile_moe_shf_glu_gelu_kernel(
             nc.sync.dma_start(t[:], src[0].rearrange("p n d -> p (n d)").bitcast(I32))
             return t
 
-        def load_fp4_words(src, lo, hi, name, queue=nc.sync):
+        def load_fp4_words(src, lo, hi, name):
             t = held([P, hi - lo, src.shape[3]], U8, name)
-            queue.dma_start(t[:].bitcast(I32), src[lo:hi, 0].rearrange("e p n -> p e n").bitcast(I32))
+            nc.sync.dma_start(t[:].bitcast(I32), src[lo:hi, 0].rearrange("e p n -> p e n").bitcast(I32))
             return t
 
-        def spread_plane(t, src, queue=nc.sync, quadrants=range(4)):
-            for q in quadrants:
+        def spread_plane(t, src):
+            for q in range(4):
                 rows = src[4 * q:4 * q + 4, :].bitcast(I32)
-                queue.dma_start(t[32 * q:32 * q + 32, :].bitcast(I32),
-                                rows.unsqueeze(0).to_broadcast([8, 4, rows.shape[1]]))
+                nc.sync.dma_start(t[32 * q:32 * q + 32, :].bitcast(I32),
+                                  rows.unsqueeze(0).to_broadcast([8, 4, rows.shape[1]]))
 
         def zeroed_planes(src, name, engine):
             t = held([P, src.shape[0], src.shape[-1]], U8, name)
             engine.memset(t[:].rearrange("p e n -> p (e n)").bitcast(I32), 0)
             return t
 
-        def load_planes(t, src, queue=nc.sync):
+        def load_planes(t, src):
             for r in range(4):
-                queue.dma_start(t[r:P:32].bitcast(I32), src[:, r:16:4, :].rearrange("e q n -> q e n").bitcast(I32))
+                nc.sync.dma_start(t[r:P:32].bitcast(I32), src[:, r:16:4, :].rearrange("e q n -> q e n").bitcast(I32))
 
         xw = held([P, T], I32, "xw")
         xs = held([P, T], U8, "xs")
-        s1 = [zeroed_planes(w1_scales[0:EARLY1, 0], "s1a", nc.vector),
-              zeroed_planes(w1_scales[EARLY1:E, 0], "s1b", nc.vector)]
+        s1 = [zeroed_planes(w1_scales[0:FIRST_SCALES, 0], "s1a", nc.vector),
+              zeroed_planes(w1_scales[FIRST_SCALES:E, 0], "s1b", nc.vector)]
         s3 = zeroed_planes(w3_scales, "s3", nc.gpsimd)
         ident = held([P, P], F32, "ident")
         make_identity(nc, ident[:])
@@ -91,15 +93,15 @@ def tile_moe_shf_glu_gelu_kernel(
         nc.sync.dma_start(xw[:], x_words[0].rearrange("p n d -> p (n d)").bitcast(I32))
         spread_plane(xs, x_scales[0])
         offs_t = load_list(offs, "offs_t")
-        w1_t = [load_fp4_words(w1_words, *CHUNKS1[0], "w1_0")]
-        load_planes(s1[0], w1_scales[0:EARLY1, 0])
-        load_planes(s1[1], w1_scales[EARLY1:E, 0])
+        w1_t = [load_fp4_words(w1_words, 0, FIRST_W1, "w1_0")]
+        load_planes(s1[0], w1_scales[0:FIRST_SCALES, 0])
+        load_planes(s1[1], w1_scales[FIRST_SCALES:E, 0])
         w1s_t = load_fp8_words(w1s_words, "w1s_t")
         spread_plane(s1s, w1s_scales[0])
-        w3_t = [load_fp4_words(w3_words, *CHUNKS3[0], "w3_0")]
+        w3_t = [load_fp4_words(w3_words, 0, FIRST_W3, "w3_0")]
         load_planes(s3, w3_scales[:, 0])
-        w1_t.append(load_fp4_words(w1_words, *CHUNKS1[1], "w1_1"))
-        w3_t.append(load_fp4_words(w3_words, *CHUNKS3[1], "w3_1"))
+        w1_t.append(load_fp4_words(w1_words, FIRST_W1, E, "w1_1"))
+        w3_t.append(load_fp4_words(w3_words, FIRST_W3, E, "w3_1"))
         load_planes(s2, w2_scales[:, 0])
         w2_t = load_fp4_words(w2_words, 0, E, "w2_t")
         w3s_t = load_fp8_words(w3s_words, "w3s_t")
@@ -111,29 +113,37 @@ def tile_moe_shf_glu_gelu_kernel(
             pos_t.append(load_list(src, "pos_t%d" % r))
             nc.sync.dma_start(gate_t[r][:], gate[r])
 
-        def first_layer(g):
-            if g >= E:
-                return (w1s_t[:].bitcast(FP8X4), s1s[:]), (w3s_t[:].bitcast(FP8X4), s3s[:])
-            c1 = [i for i, (lo, hi) in enumerate(CHUNKS1) if lo <= g < hi][0]
-            c3 = [i for i, (lo, hi) in enumerate(CHUNKS3) if lo <= g < hi][0]
-            return ((w1_t[c1][:, g - CHUNKS1[c1][0], :].bitcast(FP4X4), (s1[0][:, g, :] if g < EARLY1 else s1[1][:, g - EARLY1, :])),
-                    (w3_t[c3][:, g - CHUNKS3[c3][0], :].bitcast(FP4X4), s3[:, g, :]))
+        def expert_of(parts, split, g):
+            return parts[0][:, g, :] if g < split else parts[1][:, g - split, :]
 
-        def second_layer(g):
+        def gelu_weights(g):
             if g >= E:
-                return w2s_t[:].bitcast(FP8X4), s2s[:]
-            return w2_t[:, g, :].bitcast(FP4X4), s2[:, g, :]
+                return w1s_t[:].bitcast(FP8X4), s1s[:]
+            return expert_of(w1_t, FIRST_W1, g).bitcast(FP4X4), expert_of(s1, FIRST_SCALES, g)
+
+        def linear_weights(g):
+            if g >= E:
+                return w3s_t[:].bitcast(FP8X4), s3s[:]
+            return expert_of(w3_t, FIRST_W3, g).bitcast(FP4X4), s3[:, g, :]
 
         tokens = {}
+        act = {}
+        lin = {}
         h = {}
         h_t = {}
-        y_all = held([P, E * C], F32, "y_all")
         shared = {}
+        y_all = held([P, E * C], F32, "y_all")
+        order = "s (p u e) -> s u p e"
+        taken = {TURN_BANK: 0, SMALL_BANK: 0}
+
+        def in_turn(first):
+            taken[first] += 1
+            return first + (taken[first] + 1) % 2
 
         def gather(g):
             idx = offs_t[:, g * C // 16:(g + 1) * C // 16]
-            words = held([P, C], U32, "words%d" % (g % WORD_TILES))
-            scales = held([P, C], U8, "scales%d" % (g % SCALE_TILES))
+            words = held([P, C], U32, "words%d" % g)
+            scales = held([P, C], U8, "scales%d" % g)
             nc.vector.tensor_copy(words[:], xw[:].bitcast(U32).indirect(idx))
             nc.vector.tensor_copy(scales[:], xs[:].indirect(idx))
             tokens[g] = (words[:], scales[:])
@@ -142,152 +152,136 @@ def tile_moe_shf_glu_gelu_kernel(
             cols = slice((g - E) * C, (g - E + 1) * C)
             tokens[g] = (xw[:, cols], xs[:, cols])
 
-        order = "s (p u e) -> s u p e"
-        act = {}
-
-        def bank(i):
-            return "bank%d" % (i % 8)
-
-        lin = {}
-
-        def project(acc, g, k, w, s):
+        def project(acc, g, j, w, s):
             words, scales = tokens[g]
-            cols = slice(k * P, (k + 1) * P)
+            cols = slice(j * P, (j + 1) * P)
             nc.tensor.matmul_mx(out=acc[:], lhsT=words[:, cols].bitcast(FP8X4), lhsT_scale=scales[:, cols],
                                 rhs=w, rhs_scale=s, start=True, stop=True)
 
-        def activate(g, k, place):
-            a = psum.tile([P, H], F32, name=bank(place))
-            project(a, g, k, *first_layer(g)[0])
-            act[g, k] = ring.tile([P, 2, P, 2], F32, name="act", bufs=2 * GROUPS)
-            nc.scalar.activation(act[g, k][:], a[:].rearrange(order, u=2, e=2), GELU)
+        def activate(g, j, place):
+            acc = banked([P, H], place)
+            project(acc, g, j, *gelu_weights(g))
+            act[g, j] = ring.tile([P, 2, P, 2], F32, name="act", bufs=2 * GROUPS)
+            nc.scalar.activation(act[g, j][:], acc[:].rearrange(order, u=2, e=2), GELU)
 
-        def linear(g, k):
-            lin[g, k] = psum.tile([P, H], F32, name=bank(6 + (2 * g + k) % 4))
-            project(lin[g, k], g, k, *first_layer(g)[1])
+        def activate_both(g, place):
+            activate(g, 0, place)
+            activate(g, 1, place + 1)
 
-        def multiply(g, k):
-            b = lin[g, k]
-            if k == 0:
-                h[g] = ring.tile([P, 2, 2, HALF], BF16, name="h", bufs=5)
-            nc.vector.tensor_tensor(h[g][:, k], b[:].rearrange(order, u=2, e=2), act[g, k][:], MULT)
+        def linear(g, j):
+            lin[g, j] = banked([P, H], LINEAR_BANK + (2 * g + j) % (2 * LEAD))
+            project(lin[g, j], g, j, *linear_weights(g))
 
-        turned_of = {}
+        def multiply(g, j):
+            if j == 0:
+                h[g] = ring.tile([P, 2, 2, H // 2], BF16, name="h", bufs=DEPTH)
+            nc.vector.tensor_tensor(h[g][:, j], lin[g, j][:].rearrange(order, u=2, e=2), act[g, j][:], MULT)
 
         def turn(g):
-            turned = turned_of[g] = psum.tile([P, 2, 2, P], F32, name=bank(2 + g % 2 if g < GROUPS - 1 else 4))
+            turned = banked([P, 2, 2, P], in_turn(TURN_BANK))
             for j in range(2):
                 for u in range(2):
-                    pairs = h[g][:, j, u, :].bitcast(F32)
-                    nc.tensor.transpose(turned[:, j, u, :], pairs, ident[:])
-
-        def interleave(g):
-            turned = turned_of[g]
+                    nc.tensor.transpose(turned[:, j, u, :], h[g][:, j, u, :].bitcast(F32), ident[:])
             if g == GROUPS - 1:
-                h_t[g] = held([P, C * 4], BF16, "last")
+                h_t[g] = held([P, C * 4], BF16, "late")
             else:
                 h_t[g] = ring.tile([P, C * 4], BF16, name="h_t", align_bytes=64)
             nc.scalar.copy(h_t[g][:].bitcast(F32).rearrange("p (j s u) -> p j s u", j=2, u=2),
                            turned[:].rearrange("p j u s -> p j s u"))
 
-        def back(g):
-            codes = ring.tile([P, C], U32, name="codes", bufs=5, align_bytes=64)
-            planes = ring.tile([P, C], U8, name="planes", bufs=5, align_bytes=64)
+        def second_layer(g):
+            codes = ring.tile([P, C], U32, name="codes", bufs=DEPTH, align_bytes=64)
+            planes = ring.tile([P, C], U8, name="planes", bufs=DEPTH, align_bytes=64)
             nc.vector.quantize_mx(out=codes[:].bitcast(FP8X4), scales=planes[:], in_=h_t[g][:])
-            w, s = second_layer(g)
-            if g <= E:
-                shared["y"] = psum.tile([P, T], F32, name=bank(2 if g >= E else 4 + (E - 1 - g) % 2))
-            if g >= E:
-                for j in range(2):
-                    cols = slice(j * P, (j + 1) * P)
-                    block = 2 * (g - E) + j
-                    nc.tensor.matmul_mx(out=shared["y"][:, block * N:(block + 1) * N],
-                                        lhsT=codes[:, cols].bitcast(FP8X4), lhsT_scale=planes[:, cols],
-                                        rhs=w, rhs_scale=s, start=True, stop=True)
+            if g < E:
+                y = banked([P, C], in_turn(SMALL_BANK))
+                nc.tensor.matmul_mx(out=y[:], lhsT=w2_t[:, g, :].bitcast(FP4X4), lhsT_scale=s2[:, g, :],
+                                    rhs=codes[:].bitcast(FP8X4), rhs_scale=planes[:], start=True, stop=True)
+                nc.scalar.copy(y_all[:, g * C:(g + 1) * C], y[:])
                 return
-            y = shared["y"][:, 0:C]
-            nc.tensor.matmul_mx(out=y, lhsT=w, lhsT_scale=s, rhs=codes[:].bitcast(FP8X4), rhs_scale=planes[:],
-                                start=True, stop=True)
-            if g >= E:
-                nc.vector.tensor_copy(y_all[:, g * C:(g + 1) * C], y)
-            else:
-                nc.scalar.copy(y_all[:, g * C:(g + 1) * C], y)
-
-        def combine(dst, r, cols):
-            idx = pos_t[r][:, cols.start // 16:cols.stop // 16]
-            nc.vector.tensor_tensor(dst[:, cols], y_all[:].indirect(idx), gate_t[r][:, cols], MULT)
-
-        def both_gelus(g, place):
-            activate(g, 0, place)
-            activate(g, 1, place + 1)
+            if g == E:
+                shared["y"] = banked([P, T], TURN_BANK + E % 2)
+            for j in range(2):
+                cols = slice(j * P, (j + 1) * P)
+                block = 2 * (g - E) + j
+                nc.tensor.matmul_mx(out=shared["y"][:, block * N:(block + 1) * N],
+                                    lhsT=codes[:, cols].bitcast(FP8X4), lhsT_scale=planes[:, cols],
+                                    rhs=w2s_t[:].bitcast(FP8X4), rhs_scale=s2s[:], start=True, stop=True)
 
         for g in range(E):
             gather(g)
-            if g < E - 3:
-                both_gelus(g, 2 * g)
-        both_gelus(E, 2)
-        both_gelus(E - 3, 4)
-        for i in range(4):
-            linear(i // 2, i % 2)
-        both_gelus(E - 2, 2)
-        for g in range(GROUPS):
+            if g < FIRST_W1 - 1:
+                activate_both(g, 2 * g)
+        activate_both(E, TURN_BANK)
+        activate_both(FIRST_W1 - 1, SMALL_BANK)
+        for g in range(LEAD):
+            linear(g, 0)
+            linear(g, 1)
+        activate_both(FIRST_W1, TURN_BANK)
+
+        left = [(g, j) for g in list(range(FIRST_W1 + 1, E)) + list(range(E + 1, GROUPS)) for j in range(2)]
+        for g in range(E - 1):
             multiply(g, 0)
-            if g < 7:
-                linear(g + 2, 0)
-                if g >= 3:
-                    back(g - 3)
-            for n, place in {0: ((14, 4),), 1: ((15, 5),), 2: ((18, 4),), 3: ((19, 4),)}.get(g, ()):
-                activate(n // 2, n % 2, place)
+            linear(g + LEAD, 0)
+            if g >= LAG:
+                second_layer(g - LAG)
+            if g < len(left):
+                activate(*left[g], in_turn(SMALL_BANK))
             multiply(g, 1)
-            if g == E:
-                for late in range(E - 3, E):
-                    back(late)
-            if g < 0 or g >= 0:
-                turn(g)
-                interleave(g)
-            elif (g - 0) % 2 == 1:
-                turn(g - 1)
-                turn(g)
-                interleave(g - 1)
-                interleave(g)
-            if 7 <= g < E:
-                linear(g + 2, 0)
-                back(g - 3)
-            if g > E:
-                back(g - 1)
-            if g + 2 < GROUPS:
-                linear(g + 2, 1)
-        whole = slice(0, T)
-        halves = (slice(0, C), slice(C, T))
-        first = held([P, T], F32, "first")
-        second = held([P, T], F32, "second")
-        combine(first, 0, whole)
-        back(GROUPS - 1)
-        ys = held([P, T], F32, "ys")
-        nc.scalar.copy(ys[:], shared["y"][:])
-        combine(second, 1, whole)
-        late = held([P, 2, T], F32, "last")
-        third, last = late[:, 0, :], late[:, 1, :]
-        sums = [psum.tile([P, 2, P], F32, name=bank(6 + i)) for i in range(2)]
+            turn(g)
+            linear(g + LEAD, 1)
+        multiply(E - 1, 0)
+        multiply(E - 1, 1)
+        turn(E - 1)
+        linear(GROUPS - 1, 0)
+        second_layer(E - 1 - LAG)
+        linear(GROUPS - 1, 1)
+        multiply(E, 0)
+        multiply(E, 1)
+        second_layer(E - LAG)
+        turn(E)
+        for g in range(E - LAG + 1, E):
+            second_layer(g)
+        multiply(GROUPS - 1, 0)
+        multiply(GROUPS - 1, 1)
+        turn(GROUPS - 1)
+        second_layer(E)
+
+        def gated(dst, r, cols):
+            idx = pos_t[r][:, cols.start // 16:cols.stop // 16]
+            nc.vector.tensor_tensor(dst[:, cols], y_all[:].indirect(idx), gate_t[r][:, cols], MULT)
 
         def add_turned(banks, src, blocks, start, stop):
-            for j in blocks:
-                nc.tensor.matmul(banks[j // 2][:, j % 2, :], src[:, j * P:(j + 1) * P], ident[:], is_transpose=True,
-                                 start=start and j % 2 == 0, stop=stop and j % 2 == 1)
+            for b in blocks:
+                nc.tensor.matmul(banks[b // 2][:, b % 2, :], src[:, b * P:(b + 1) * P], ident[:], is_transpose=True,
+                                 start=start and b % 2 == 0, stop=stop and b % 2 == 1)
 
-        add_turned(sums, first, range(4), True, False)
-        add_turned(sums, second, range(4), False, False)
-        for i in range(2):
-            combine(third, 2, halves[i])
-            add_turned(sums, third, (2 * i, 2 * i + 1), False, True)
-        combine(last, 3, whole)
-        three = [psum.tile([P, 2, P], F32, name=bank(8 + i)) for i in range(2)]
-        add_turned(three, ys, range(4), True, False)
-        flipped = held([P, T], F32, "flipped")
-        for i in range(2):
-            nc.scalar.copy(flipped[:, halves[i]], sums[i][:].rearrange("p j t -> p (j t)"))
-            add_turned(three, flipped, (2 * i, 2 * i + 1), False, True)
-        for i in range(2):
-            res = held([P, C], F32, "res%d" % i)
-            nc.vector.tensor_tensor(res[:], three[i][:].rearrange("p j t -> p (j t)"), last[:, halves[i]], ADD)
-            nc.sync.dma_start(out[:, halves[i]], res[:])
+        whole = slice(0, T)
+        sides = (slice(0, T // 2), slice(T // 2, T))
+        first = held([P, T], F32, "first")
+        gated(first, 0, whole)
+        second_layer(GROUPS - 1)
+        ys = held([P, T], F32, "ys")
+        nc.scalar.copy(ys[:], shared["y"][:])
+        late = held([P, TOP - 1, T], F32, "late")
+        second, third, fourth = late[:, 0, :], late[:, 1, :], late[:, 2, :]
+        gated(second, 1, whole)
+        pair = [banked([P, 2, P], LINEAR_BANK + i) for i in range(2)]
+        add_turned(pair, first, range(4), True, False)
+        add_turned(pair, second, range(4), False, True)
+        gated(third, 2, whole)
+        for side in sides:
+            gated(fourth, 3, side)
+        rest = held([P, T], F32, "rest")
+        for side in sides:
+            nc.vector.tensor_tensor(rest[:, side], third[:, side], fourth[:, side], ADD)
+        triple = [banked([P, 2, P], LINEAR_BANK + 2 + i) for i in range(2)]
+        add_turned(triple, ys, range(4), True, False)
+        pair_rows = held([P, T], F32, "pair_rows")
+        for i, side in enumerate(sides):
+            nc.scalar.copy(pair_rows[:, side], pair[i][:].rearrange("p b n -> p (b n)"))
+            add_turned(triple, pair_rows, (2 * i, 2 * i + 1), False, True)
+        for i, side in enumerate(sides):
+            res = held([P, T // 2], F32, "res%d" % i)
+            nc.vector.tensor_tensor(res[:], triple[i][:].rearrange("p b t -> p (b t)"), rest[:, side], ADD)
+            nc.sync.dma_start(out[:, side], res[:])

@@ -14,20 +14,21 @@ U16 = mybir.dt.uint16
 U8 = mybir.dt.uint8
 FP8X4 = mybir.dt.float8_e4m3fn_x4
 FP4X4 = mybir.dt.float4_e2m1fn_x4
+COPY = mybir.ActivationFunctionType.Copy
 GELU = mybir.ActivationFunctionType.Gelu_apprx_tanh
 MULT = mybir.AluOpType.mult
 ADD = mybir.AluOpType.add
 
 P = 128
 BANKS = 8
-GROUPS = E + T // C
+UNITS = T // P
 FIRST_SCALES = 2
 FIRST_W1 = 6
 FIRST_W3 = 4
 LEAD = 2
 LAG = 3
 DEPTH = LAG + 2
-TURN_BANK, SMALL_BANK, LINEAR_BANK = 2, 4, 6
+TURN_BANK, SMALL_BANK, LINEAR_BANK = 0, 2, 4
 
 
 def tile_moe_shf_glu_gelu_kernel(
@@ -62,10 +63,10 @@ def tile_moe_shf_glu_gelu_kernel(
             nc.sync.dma_start(t[:].bitcast(I32), src[lo:hi, 0].rearrange("e p n -> p e n").bitcast(I32))
             return t
 
-        def spread_plane(t, src):
+        def spread_plane(t, src, queues):
             for q in range(4):
                 rows = src[4 * q:4 * q + 4, :].bitcast(I32)
-                nc.sync.dma_start(t[32 * q:32 * q + 32, :].bitcast(I32),
+                queues[q].dma_start(t[32 * q:32 * q + 32, :].bitcast(I32),
                                   rows.unsqueeze(0).to_broadcast([8, 4, rows.shape[1]]))
 
         def zeroed_planes(src, name, engine):
@@ -77,204 +78,234 @@ def tile_moe_shf_glu_gelu_kernel(
             for r in range(4):
                 nc.sync.dma_start(t[r:P:32].bitcast(I32), src[:, r:16:4, :].rearrange("e q n -> q e n").bitcast(I32))
 
+        def load_rows(t, first, src):
+            for q in range(4):
+                nc.sync.dma_start(t[32 * q + first:32 * q + first + 4, :].bitcast(I32), src[4 * q:4 * q + 4, :].bitcast(I32))
+
         xw = held([P, T], I32, "xw")
         xs = held([P, T], U8, "xs")
         s1 = [zeroed_planes(w1_scales[0:FIRST_SCALES, 0], "s1a", nc.vector),
               zeroed_planes(w1_scales[FIRST_SCALES:E, 0], "s1b", nc.vector)]
-        s3 = zeroed_planes(w3_scales, "s3", nc.gpsimd)
+        s3 = zeroed_planes(w3_scales, "s3", nc.vector)
+        s13s = held([P, H], U8, "s13s")
+        nc.vector.memset(s13s[:].bitcast(I32), 0)
+        s2 = zeroed_planes(w2_scales, "s2", nc.vector)
         ident = held([P, P], F32, "ident")
         make_identity(nc, ident[:])
-        s2 = zeroed_planes(w2_scales, "s2", nc.gpsimd)
-        s1s = held([P, H], U8, "s1s")
-        s3s = held([P, H], U8, "s3s")
         s2s = held([P, N], U8, "s2s")
         gate_t = [held([P, T], F32, "gate%d" % r) for r in range(TOP)]
 
-        nc.sync.dma_start(xw[:], x_words[0].rearrange("p n d -> p (n d)").bitcast(I32))
-        spread_plane(xs, x_scales[0])
         offs_t = load_list(offs, "offs_t")
-        w1_t = [load_fp4_words(w1_words, 0, FIRST_W1, "w1_0")]
+        spread_plane(xs, x_scales[0], (nc.sync, nc.sync, nc.scalar, nc.scalar))
+        nc.scalar.dma_start(xw[:], x_words[0].rearrange("p n d -> p (n d)").bitcast(I32))
+        w1_t = [load_fp4_words(w1_words, 0, FIRST_SCALES, "w1_0")]
         load_planes(s1[0], w1_scales[0:FIRST_SCALES, 0])
+        w1_t.append(load_fp4_words(w1_words, FIRST_SCALES, FIRST_W1, "w1_1"))
         load_planes(s1[1], w1_scales[FIRST_SCALES:E, 0])
-        w1s_t = load_fp8_words(w1s_words, "w1s_t")
-        spread_plane(s1s, w1s_scales[0])
+        load_rows(s13s, 0, w1s_scales[0])
+        load_rows(s13s, 4, w3s_scales[0])
         w3_t = [load_fp4_words(w3_words, 0, FIRST_W3, "w3_0")]
+        w1s_t = load_fp8_words(w1s_words, "w1s_t")
         load_planes(s3, w3_scales[:, 0])
-        w1_t.append(load_fp4_words(w1_words, FIRST_W1, E, "w1_1"))
+        w1_t.append(load_fp4_words(w1_words, FIRST_W1, E, "w1_2"))
         w3_t.append(load_fp4_words(w3_words, FIRST_W3, E, "w3_1"))
         load_planes(s2, w2_scales[:, 0])
         w2_t = load_fp4_words(w2_words, 0, E, "w2_t")
         w3s_t = load_fp8_words(w3s_words, "w3s_t")
-        spread_plane(s3s, w3s_scales[0])
         w2s_t = load_fp8_words(w2s_words, "w2s_t")
-        spread_plane(s2s, w2s_scales[0])
+        spread_plane(s2s, w2s_scales[0], (nc.sync,) * 4)
         pos_t = []
         for r, src in enumerate((pos1, pos2, pos3, pos4)):
             pos_t.append(load_list(src, "pos_t%d" % r))
             nc.sync.dma_start(gate_t[r][:], gate[r])
 
-        def expert_of(parts, split, g):
-            return parts[0][:, g, :] if g < split else parts[1][:, g - split, :]
+        def expert_of(parts, bounds, g):
+            k = sum(1 for b in bounds if g >= b)
+            return parts[k][:, g - ([0] + list(bounds))[k], :]
 
         def gelu_weights(g):
-            if g >= E:
-                return w1s_t[:].bitcast(FP8X4), s1s[:]
-            return expert_of(w1_t, FIRST_W1, g).bitcast(FP4X4), expert_of(s1, FIRST_SCALES, g)
+            return expert_of(w1_t, (FIRST_SCALES, FIRST_W1), g).bitcast(FP4X4), expert_of(s1, (FIRST_SCALES,), g)
 
         def linear_weights(g):
-            if g >= E:
-                return w3s_t[:].bitcast(FP8X4), s3s[:]
-            return expert_of(w3_t, FIRST_W3, g).bitcast(FP4X4), s3[:, g, :]
+            return expert_of(w3_t, (FIRST_W3,), g).bitcast(FP4X4), s3[:, g, :]
 
         tokens = {}
         act = {}
         lin = {}
         h = {}
         h_t = {}
-        shared = {}
         y_all = held([P, E * C], F32, "y_all")
-        order = "s (p u e) -> s u p e"
-        taken = {TURN_BANK: 0, SMALL_BANK: 0}
+        taken = {TURN_BANK: 0, SMALL_BANK: 0, LINEAR_BANK: 0}
 
-        def in_turn(first):
+        def in_turn(first, count=2):
             taken[first] += 1
-            return first + (taken[first] + 1) % 2
+            return first + (taken[first] - 1) % count
 
         def gather(g):
             idx = offs_t[:, g * C // 16:(g + 1) * C // 16]
             words = held([P, C], U32, "words%d" % g)
             scales = held([P, C], U8, "scales%d" % g)
-            nc.vector.tensor_copy(words[:], xw[:].bitcast(U32).indirect(idx))
             nc.vector.tensor_copy(scales[:], xs[:].indirect(idx))
+            nc.vector.tensor_copy(words[:], xw[:].bitcast(U32).indirect(idx))
             tokens[g] = (words[:], scales[:])
 
-        for g in range(E, GROUPS):
-            cols = slice((g - E) * C, (g - E + 1) * C)
-            tokens[g] = (xw[:, cols], xs[:, cols])
+        def by_slot(src, name):
+            t = held([P, H], U32, name)
+            nc.scalar.copy(t[:].rearrange("p (d m) -> p m d", d=4), src[:].bitcast(U32).rearrange("p (m d) -> p m d", d=4))
+            return t
 
-        def project(acc, g, j, w, s):
-            words, scales = tokens[g]
-            cols = slice(j * P, (j + 1) * P)
-            nc.tensor.matmul_mx(out=acc[:], lhsT=words[:, cols].bitcast(FP8X4), lhsT_scale=scales[:, cols],
-                                rhs=w, rhs_scale=s, start=True, stop=True)
+        shared = {}
+
+        def project(place, g, j, branch):
+            acc = banked([P, H], place)
+            if g < E:
+                words, scales = tokens[g]
+                w, s = (gelu_weights, linear_weights)[branch](g)
+                cols = slice(j * P, (j + 1) * P)
+                nc.tensor.matmul_mx(out=acc[:], lhsT=words[:, cols].bitcast(FP8X4), lhsT_scale=scales[:, cols],
+                                    rhs=w, rhs_scale=s, start=True, stop=True)
+                return acc[:].rearrange("s (p u e) -> s u p e", u=2, e=2)
+            toks = slice(j * P, (j + 1) * P)
+            for d in range(4):
+                cols = slice(d * P, (d + 1) * P)
+                nc.tensor.matmul_mx(out=acc[:, cols], lhsT=shared[branch][:, cols].bitcast(FP8X4),
+                                    lhsT_scale=shared["planes"][4 * branch:P, cols],
+                                    rhs=xw[:, toks].bitcast(FP8X4), rhs_scale=xs[:, toks], start=True, stop=True)
+            return acc[:].rearrange("p (d t) -> p t d", d=4)
 
         def activate(g, j, place):
-            acc = banked([P, H], place)
-            project(acc, g, j, *gelu_weights(g))
-            act[g, j] = ring.tile([P, 2, P, 2], F32, name="act", bufs=2 * GROUPS)
-            nc.scalar.activation(act[g, j][:], acc[:].rearrange(order, u=2, e=2), GELU)
-
-        def activate_both(g, place):
-            activate(g, 0, place)
-            activate(g, 1, place + 1)
+            acc = project(place, g, j, 0)
+            t = ring.tile([P, H], F32, name="act", bufs=2 * E + UNITS)
+            act[g, j] = t[:].rearrange("p (a b c) -> p a b c", a=2, c=2) if g < E else t[:].rearrange("p (t d) -> p t d", d=4)
+            nc.scalar.activation(act[g, j], acc, GELU)
 
         def linear(g, j):
-            lin[g, j] = banked([P, H], LINEAR_BANK + (2 * g + j) % (2 * LEAD))
-            project(lin[g, j], g, j, *linear_weights(g))
+            lin[g, j] = project(in_turn(LINEAR_BANK, 2 * LEAD), g, j, 1)
 
         def multiply(g, j):
-            if j == 0:
-                h[g] = ring.tile([P, 2, 2, H // 2], BF16, name="h", bufs=DEPTH)
-            nc.vector.tensor_tensor(h[g][:, j], lin[g, j][:].rearrange(order, u=2, e=2), act[g, j][:], MULT)
+            if g == E:
+                if j % 2 == 0:
+                    hs.append(held([P, C * 4], BF16, ("hs", "late")[j // 2]))
+                dst = hs[-1][:, j % 2 * H:(j % 2 + 1) * H].rearrange("p (t d) -> p t d", d=4)
+            else:
+                if j == 0:
+                    h[g] = ring.tile([P, 2, 2, P, 2], BF16, name="h", bufs=DEPTH)
+                dst = h[g][:, j]
+            nc.vector.tensor_tensor(dst, lin[g, j], act[g, j], MULT)
 
         def turn(g):
             turned = banked([P, 2, 2, P], in_turn(TURN_BANK))
             for j in range(2):
                 for u in range(2):
-                    nc.tensor.transpose(turned[:, j, u, :], h[g][:, j, u, :].bitcast(F32), ident[:])
-            if g == GROUPS - 1:
+                    nc.tensor.transpose(turned[:, j, u, :], h[g][:, j, u].rearrange("s p e -> s (p e)").bitcast(F32), ident[:])
+            if g == E - 1:
                 h_t[g] = held([P, C * 4], BF16, "late")
             else:
                 h_t[g] = ring.tile([P, C * 4], BF16, name="h_t", align_bytes=64)
             nc.scalar.copy(h_t[g][:].bitcast(F32).rearrange("p (j s u) -> p j s u", j=2, u=2),
                            turned[:].rearrange("p j u s -> p j s u"))
 
-        def second_layer(g):
+        def quantise(src):
             codes = ring.tile([P, C], U32, name="codes", bufs=DEPTH, align_bytes=64)
             planes = ring.tile([P, C], U8, name="planes", bufs=DEPTH, align_bytes=64)
-            nc.vector.quantize_mx(out=codes[:].bitcast(FP8X4), scales=planes[:], in_=h_t[g][:])
-            if g < E:
-                y = banked([P, C], in_turn(SMALL_BANK))
-                nc.tensor.matmul_mx(out=y[:], lhsT=w2_t[:, g, :].bitcast(FP4X4), lhsT_scale=s2[:, g, :],
-                                    rhs=codes[:].bitcast(FP8X4), rhs_scale=planes[:], start=True, stop=True)
-                nc.scalar.copy(y_all[:, g * C:(g + 1) * C], y[:])
-                return
-            if g == E:
-                shared["y"] = banked([P, T], TURN_BANK + E % 2)
+            nc.vector.quantize_mx(out=codes[:].bitcast(FP8X4), scales=planes[:], in_=src[:])
+            return codes, planes
+
+        def second_layer(g):
+            codes, planes = quantise(h_t[g])
+            y = banked([P, C], in_turn(SMALL_BANK))
+            nc.tensor.matmul_mx(out=y[:], lhsT=w2_t[:, g, :].bitcast(FP4X4), lhsT_scale=s2[:, g, :],
+                                rhs=codes[:].bitcast(FP8X4), rhs_scale=planes[:], start=True, stop=True)
+            nc.scalar.copy(y_all[:, g * C:(g + 1) * C], y[:])
+
+        hs = []
+
+        ys = held([P, T], F32, "ys")
+
+        def shared_layer(k, codes, planes, place):
+            rows = banked([P, C], place)
             for j in range(2):
                 cols = slice(j * P, (j + 1) * P)
-                block = 2 * (g - E) + j
-                nc.tensor.matmul_mx(out=shared["y"][:, block * N:(block + 1) * N],
-                                    lhsT=codes[:, cols].bitcast(FP8X4), lhsT_scale=planes[:, cols],
+                nc.tensor.matmul_mx(out=rows[:, cols], lhsT=codes[:, cols].bitcast(FP8X4), lhsT_scale=planes[:, cols],
                                     rhs=w2s_t[:].bitcast(FP8X4), rhs_scale=s2s[:], start=True, stop=True)
+            nc.scalar.copy(ys[:, k * C:(k + 1) * C], rows[:])
 
         for g in range(E):
             gather(g)
-            if g < FIRST_W1 - 1:
-                activate_both(g, 2 * g)
-        activate_both(E, TURN_BANK)
-        activate_both(FIRST_W1 - 1, SMALL_BANK)
+            if g < FIRST_W1:
+                activate(g, 0, (2 * g) % 4)
+                activate(g, 1, (2 * g + 1) % 4)
+        shared[0] = by_slot(w1s_t, "w1s_slots")
         for g in range(LEAD):
             linear(g, 0)
             linear(g, 1)
-        activate_both(FIRST_W1, TURN_BANK)
+        for g in range(FIRST_W1, E):
+            activate(g, 0, (2 * g) % 4)
+            activate(g, 1, (2 * g + 1) % 4)
+        shared["planes"] = held([P, H], U8, "s13s_slots")
+        nc.vector.tensor_copy(shared["planes"][:].rearrange("p (d m) -> p d m", d=4), s13s[:].rearrange("p (m d) -> p d m", d=4))
 
-        left = [(g, j) for g in list(range(FIRST_W1 + 1, E)) + list(range(E + 1, GROUPS)) for j in range(2)]
-        for g in range(E - 1):
+        halves = [(g, j) for g in range(E) for j in range(2)] + [(E, j) for j in range(UNITS)]
+        for g in range(E):
             multiply(g, 0)
-            linear(g + LEAD, 0)
+            if g < E - 1:
+                linear(*halves[2 * (g + LEAD)])
             if g >= LAG:
                 second_layer(g - LAG)
-            if g < len(left):
-                activate(*left[g], in_turn(SMALL_BANK))
+            if 1 <= g <= UNITS:
+                activate(E, g - 1, in_turn(SMALL_BANK))
             multiply(g, 1)
             turn(g)
-            linear(g + LEAD, 1)
-        multiply(E - 1, 0)
-        multiply(E - 1, 1)
-        turn(E - 1)
-        linear(GROUPS - 1, 0)
-        second_layer(E - 1 - LAG)
-        linear(GROUPS - 1, 1)
+            if g == UNITS + 1:
+                shared[1] = by_slot(w3s_t, "w3s_slots")
+            if g < E - 1:
+                linear(*halves[2 * (g + LEAD) + 1])
+        linear(E, 2)
+        linear(E, 3)
         multiply(E, 0)
+        second_layer(E - 3)
         multiply(E, 1)
-        second_layer(E - LAG)
-        turn(E)
-        for g in range(E - LAG + 1, E):
-            second_layer(g)
-        multiply(GROUPS - 1, 0)
-        multiply(GROUPS - 1, 1)
-        turn(GROUPS - 1)
-        second_layer(E)
-
-        def gated(dst, r, cols):
-            idx = pos_t[r][:, cols.start // 16:cols.stop // 16]
-            nc.vector.tensor_tensor(dst[:, cols], y_all[:].indirect(idx), gate_t[r][:, cols], MULT)
+        second_layer(E - 2)
+        second_layer(E - 1)
+        shared_layer(0, *quantise(hs[0]), TURN_BANK)
+        multiply(E, 2)
+        multiply(E, 3)
 
         def add_turned(banks, src, blocks, start, stop):
             for b in blocks:
                 nc.tensor.matmul(banks[b // 2][:, b % 2, :], src[:, b * P:(b + 1) * P], ident[:], is_transpose=True,
                                  start=start and b % 2 == 0, stop=stop and b % 2 == 1)
 
-        whole = slice(0, T)
         sides = (slice(0, T // 2), slice(T // 2, T))
+
+        def entries(r, side):
+            return y_all[:].indirect(pos_t[r][:, side.start // 16:side.stop // 16])
+
+        picked = [held([P, T // 2], F32, "picked%d" % i) for i in range(2)]
+        for i, side in enumerate(sides):
+            nc.scalar.activation(picked[i][:], entries(2, side), COPY)
+        last = held([P, T], F32, "last")
+        nc.scalar.activation(last[:], entries(3, slice(0, T)), COPY)
         first = held([P, T], F32, "first")
-        gated(first, 0, whole)
-        second_layer(GROUPS - 1)
-        ys = held([P, T], F32, "ys")
-        nc.scalar.copy(ys[:], shared["y"][:])
-        late = held([P, TOP - 1, T], F32, "late")
-        second, third, fourth = late[:, 0, :], late[:, 1, :], late[:, 2, :]
-        gated(second, 1, whole)
+        nc.vector.tensor_tensor(first[:, sides[0]], entries(0, sides[0]), gate_t[0][:, sides[0]], MULT)
+        shared_layer(1, *quantise(hs[1]), TURN_BANK + 1)
+        nc.vector.tensor_tensor(first[:, sides[1]], entries(0, sides[1]), gate_t[0][:, sides[1]], MULT)
+        third = held([P, T], F32, "third")
         pair = [banked([P, 2, P], LINEAR_BANK + i) for i in range(2)]
         add_turned(pair, first, range(4), True, False)
-        add_turned(pair, second, range(4), False, True)
-        gated(third, 2, whole)
-        for side in sides:
-            gated(fourth, 3, side)
+        for i, side in enumerate(sides):
+            nc.vector.tensor_tensor(third[:, side], picked[i][:], gate_t[2][:, side], MULT)
+            add_turned(pair, third, (2 * i, 2 * i + 1), False, True)
+        second = []
+        for i, side in enumerate(sides):
+            second.append(held([P, T // 2], F32, "picked%d" % i))
+            nc.vector.tensor_tensor(second[i][:], entries(1, side), gate_t[1][:, side], MULT)
+        fourth = held([P, T], F32, "fourth")
         rest = held([P, T], F32, "rest")
         for side in sides:
-            nc.vector.tensor_tensor(rest[:, side], third[:, side], fourth[:, side], ADD)
+            nc.vector.tensor_tensor(fourth[:, side], last[:, side], gate_t[3][:, side], MULT)
+        for i, side in enumerate(sides):
+            nc.vector.tensor_tensor(rest[:, side], second[i][:], fourth[:, side], ADD)
         triple = [banked([P, 2, P], LINEAR_BANK + 2 + i) for i in range(2)]
         add_turned(triple, ys, range(4), True, False)
         pair_rows = held([P, T], F32, "pair_rows")

@@ -27,7 +27,7 @@ FIRST_W1 = 6
 FIRST_W3 = 4
 LEAD = 2
 LAG = 3
-DEPTH = LAG + 2
+PAIRED = 6
 TURN_BANK, SMALL_BANK, LINEAR_BANK = 0, 2, 4
 
 
@@ -86,14 +86,14 @@ def tile_moe_shf_glu_gelu_kernel(
         xs = held([P, T], U8, "xs")
         s1 = [zeroed_planes(w1_scales[0:FIRST_SCALES, 0], "s1a", nc.vector),
               zeroed_planes(w1_scales[FIRST_SCALES:E, 0], "s1b", nc.vector)]
-        s3 = zeroed_planes(w3_scales, "s3", nc.vector)
         s13s = held([P, H], U8, "s13s")
         nc.vector.memset(s13s[:].bitcast(I32), 0)
-        s2 = zeroed_planes(w2_scales, "s2", nc.vector)
+        s3 = zeroed_planes(w3_scales, "s3", nc.vector)
         ident = held([P, P], F32, "ident")
         make_identity(nc, ident[:])
+        s2 = zeroed_planes(w2_scales, "s2", nc.gpsimd)
         s2s = held([P, N], U8, "s2s")
-        gate_t = [held([P, T], F32, "gate%d" % r) for r in range(TOP)]
+        gate_t = held([P, TOP, T], F32, "gate_t")
 
         offs_t = load_list(offs, "offs_t")
         spread_plane(xs, x_scales[0], (nc.sync, nc.sync, nc.scalar, nc.scalar))
@@ -114,10 +114,8 @@ def tile_moe_shf_glu_gelu_kernel(
         w3s_t = load_fp8_words(w3s_words, "w3s_t")
         w2s_t = load_fp8_words(w2s_words, "w2s_t")
         spread_plane(s2s, w2s_scales[0], (nc.sync,) * 4)
-        pos_t = []
-        for r, src in enumerate((pos1, pos2, pos3, pos4)):
-            pos_t.append(load_list(src, "pos_t%d" % r))
-            nc.sync.dma_start(gate_t[r][:], gate[r])
+        pos_t = [load_list(src, "pos_t%d" % r) for r, src in enumerate((pos1, pos2, pos3, pos4))]
+        nc.sync.dma_start(gate_t[:], gate.rearrange("r p t -> p r t"))
 
         def expert_of(parts, bounds, g):
             k = sum(1 for b in bounds if g >= b)
@@ -132,14 +130,18 @@ def tile_moe_shf_glu_gelu_kernel(
         tokens = {}
         act = {}
         lin = {}
+        lin_bank = {}
         h = {}
         h_t = {}
+        hs = []
+        shared = {}
         y_all = held([P, E * C], F32, "y_all")
-        taken = {TURN_BANK: 0, SMALL_BANK: 0, LINEAR_BANK: 0}
+        ys = held([P, T], F32, "ys")
+        taken = {TURN_BANK: 0, SMALL_BANK: 0}
 
-        def in_turn(first, count=2):
+        def in_turn(first):
             taken[first] += 1
-            return first + (taken[first] - 1) % count
+            return first + (taken[first] - 1) % 2
 
         def gather(g):
             idx = offs_t[:, g * C // 16:(g + 1) * C // 16]
@@ -149,12 +151,8 @@ def tile_moe_shf_glu_gelu_kernel(
             nc.vector.tensor_copy(words[:], xw[:].bitcast(U32).indirect(idx))
             tokens[g] = (words[:], scales[:])
 
-        def by_slot(src, name):
-            t = held([P, H], U32, name)
-            nc.scalar.copy(t[:].rearrange("p (d m) -> p m d", d=4), src[:].bitcast(U32).rearrange("p (m d) -> p m d", d=4))
-            return t
-
-        shared = {}
+        def by_slot(engine, dst, src):
+            engine(dst.rearrange("p (d m) -> p d m", d=4), src.rearrange("p (m d) -> p d m", d=4))
 
         def project(place, g, j, branch):
             acc = banked([P, H], place)
@@ -168,19 +166,28 @@ def tile_moe_shf_glu_gelu_kernel(
             toks = slice(j * P, (j + 1) * P)
             for d in range(4):
                 cols = slice(d * P, (d + 1) * P)
-                nc.tensor.matmul_mx(out=acc[:, cols], lhsT=shared[branch][:, cols].bitcast(FP8X4),
+                nc.tensor.matmul_mx(out=acc[:, cols], lhsT=shared["words"][:, branch, cols].bitcast(FP8X4),
                                     lhsT_scale=shared["planes"][4 * branch:P, cols],
                                     rhs=xw[:, toks].bitcast(FP8X4), rhs_scale=xs[:, toks], start=True, stop=True)
             return acc[:].rearrange("p (d t) -> p t d", d=4)
 
-        def activate(g, j, place):
-            acc = project(place, g, j, 0)
+        def gelu(g, j, acc):
             t = ring.tile([P, H], F32, name="act", bufs=2 * E + UNITS)
             act[g, j] = t[:].rearrange("p (a b c) -> p a b c", a=2, c=2) if g < E else t[:].rearrange("p (t d) -> p t d", d=4)
             nc.scalar.activation(act[g, j], acc, GELU)
 
-        def linear(g, j):
-            lin[g, j] = project(in_turn(LINEAR_BANK, 2 * LEAD), g, j, 1)
+        def activate_both(g):
+            if g in (0, FIRST_W1):
+                gelu(g, 0, project(0, g, 0, 0))
+                gelu(g, 1, project(1, g, 1, 0))
+                return
+            later = project((2 * g) % 4, g, 1, 0)
+            gelu(g, 0, project((2 * g + 1) % 4, g, 0, 0))
+            gelu(g, 1, later)
+
+        def linear(g, j, place):
+            lin_bank[g, j] = place
+            lin[g, j] = project(place, g, j, 1)
 
         def multiply(g, j):
             if g == E:
@@ -189,7 +196,7 @@ def tile_moe_shf_glu_gelu_kernel(
                 dst = hs[-1][:, j % 2 * H:(j % 2 + 1) * H].rearrange("p (t d) -> p t d", d=4)
             else:
                 if j == 0:
-                    h[g] = ring.tile([P, 2, 2, P, 2], BF16, name="h", bufs=DEPTH)
+                    h[g] = ring.tile([P, 2, 2, P, 2], BF16, name="h", bufs=2)
                 dst = h[g][:, j]
             nc.vector.tensor_tensor(dst, lin[g, j], act[g, j], MULT)
 
@@ -198,31 +205,32 @@ def tile_moe_shf_glu_gelu_kernel(
             for j in range(2):
                 for u in range(2):
                     nc.tensor.transpose(turned[:, j, u, :], h[g][:, j, u].rearrange("s p e -> s (p e)").bitcast(F32), ident[:])
-            if g == E - 1:
-                h_t[g] = held([P, C * 4], BF16, "late")
-            else:
-                h_t[g] = ring.tile([P, C * 4], BF16, name="h_t", align_bytes=64)
-            nc.scalar.copy(h_t[g][:].bitcast(F32).rearrange("p (j s u) -> p j s u", j=2, u=2),
+            if g >= PAIRED or g % 2 == 0:
+                h_t[g] = held([P, (2 if g < PAIRED else 1) * C * 4], BF16, "late" if g == E - 1 else "h_t%d" % g)
+            k = g % 2 if g < PAIRED else 0
+            dst = h_t[g - k][:, k * C * 4:(k + 1) * C * 4]
+            nc.scalar.copy(dst.bitcast(F32).rearrange("p (j s u) -> p j s u", j=2, u=2),
                            turned[:].rearrange("p j u s -> p j s u"))
 
         def quantise(src):
-            codes = ring.tile([P, C], U32, name="codes", bufs=DEPTH, align_bytes=64)
-            planes = ring.tile([P, C], U8, name="planes", bufs=DEPTH, align_bytes=64)
+            width = src.shape[1] // 4
+            codes = ring.tile([P, width], U32, name="codes", bufs=E, align_bytes=64)
+            planes = ring.tile([P, width], U8, name="planes", bufs=E, align_bytes=64)
             nc.vector.quantize_mx(out=codes[:].bitcast(FP8X4), scales=planes[:], in_=src[:])
             return codes, planes
 
-        def second_layer(g):
+        def second_layer(g, place=None):
             codes, planes = quantise(h_t[g])
-            y = banked([P, C], in_turn(SMALL_BANK))
-            nc.tensor.matmul_mx(out=y[:], lhsT=w2_t[:, g, :].bitcast(FP4X4), lhsT_scale=s2[:, g, :],
-                                rhs=codes[:].bitcast(FP8X4), rhs_scale=planes[:], start=True, stop=True)
-            nc.scalar.copy(y_all[:, g * C:(g + 1) * C], y[:])
+            width = codes.shape[1]
+            y = banked([P, width], in_turn(SMALL_BANK) if place is None else place)
+            for k in range(width // C):
+                cols = slice(k * C, (k + 1) * C)
+                nc.tensor.matmul_mx(out=y[:, cols], lhsT=w2_t[:, g + k, :].bitcast(FP4X4), lhsT_scale=s2[:, g + k, :],
+                                    rhs=codes[:, cols].bitcast(FP8X4), rhs_scale=planes[:, cols], start=True, stop=True)
+            nc.scalar.copy(y_all[:, g * C:g * C + width], y[:])
 
-        hs = []
-
-        ys = held([P, T], F32, "ys")
-
-        def shared_layer(k, codes, planes, place):
+        def shared_layer(k, place):
+            codes, planes = quantise(hs[k])
             rows = banked([P, C], place)
             for j in range(2):
                 cols = slice(j * P, (j + 1) * P)
@@ -232,42 +240,38 @@ def tile_moe_shf_glu_gelu_kernel(
 
         for g in range(E):
             gather(g)
-            if g < FIRST_W1:
-                activate(g, 0, (2 * g) % 4)
-                activate(g, 1, (2 * g + 1) % 4)
-        shared[0] = by_slot(w1s_t, "w1s_slots")
-        for g in range(LEAD):
-            linear(g, 0)
-            linear(g, 1)
-        for g in range(FIRST_W1, E):
-            activate(g, 0, (2 * g) % 4)
-            activate(g, 1, (2 * g + 1) % 4)
-        shared["planes"] = held([P, H], U8, "s13s_slots")
-        nc.vector.tensor_copy(shared["planes"][:].rearrange("p (d m) -> p d m", d=4), s13s[:].rearrange("p (m d) -> p d m", d=4))
+            if g == FIRST_W1:
+                for k in range(2 * LEAD):
+                    linear(k // 2, k % 2 if k < 2 else 1 - k % 2, LINEAR_BANK + k)
+            activate_both(g)
+        shared["planes"] = held([P, H], U8, "s1b")
+        shared["words"] = held([P, 2, H], U32, "w1_2")
+        by_slot(nc.gpsimd.tensor_copy, shared["planes"][:], s13s[:])
+        by_slot(nc.gpsimd.tensor_copy, shared["words"][:, 0], w1s_t[:].bitcast(U32))
+        by_slot(nc.gpsimd.tensor_copy, shared["words"][:, 1], w3s_t[:].bitcast(U32))
 
-        halves = [(g, j) for g in range(E) for j in range(2)] + [(E, j) for j in range(UNITS)]
+        def ahead(g, j):
+            return (g + LEAD, 1 - j) if g + LEAD < E else (E, 2 * (g + LEAD - E) + 1 - j)
+
         for g in range(E):
             multiply(g, 0)
+            if 0 <= g - 2 < UNITS:
+                gelu(E, g - 2, project(in_turn(SMALL_BANK), E, g - 2, 0))
             if g < E - 1:
-                linear(*halves[2 * (g + LEAD)])
-            if g >= LAG:
-                second_layer(g - LAG)
-            if 1 <= g <= UNITS:
-                activate(E, g - 1, in_turn(SMALL_BANK))
+                linear(*ahead(g, 0), lin_bank[g, 0])
             multiply(g, 1)
-            turn(g)
-            if g == UNITS + 1:
-                shared[1] = by_slot(w3s_t, "w3s_slots")
             if g < E - 1:
-                linear(*halves[2 * (g + LEAD) + 1])
-        linear(E, 2)
-        linear(E, 3)
+                linear(*ahead(g, 1), lin_bank[g, 1])
+            turn(g)
+            if g >= LAG and (g - LAG) % 2 == 0:
+                second_layer(g - LAG)
+        linear(E, 3, lin_bank[E - 1, 0])
+        linear(E, 2, lin_bank[E - 1, 1])
         multiply(E, 0)
-        second_layer(E - 3)
         multiply(E, 1)
-        second_layer(E - 2)
-        second_layer(E - 1)
-        shared_layer(0, *quantise(hs[0]), TURN_BANK)
+        second_layer(E - 2, TURN_BANK)
+        second_layer(E - 1, lin_bank[E, 0])
+        shared_layer(0, lin_bank[E, 1])
         multiply(E, 2)
         multiply(E, 3)
 
@@ -276,36 +280,29 @@ def tile_moe_shf_glu_gelu_kernel(
                 nc.tensor.matmul(banks[b // 2][:, b % 2, :], src[:, b * P:(b + 1) * P], ident[:], is_transpose=True,
                                  start=start and b % 2 == 0, stop=stop and b % 2 == 1)
 
+        whole = slice(0, T)
         sides = (slice(0, T // 2), slice(T // 2, T))
 
         def entries(r, side):
             return y_all[:].indirect(pos_t[r][:, side.start // 16:side.stop // 16])
 
-        picked = [held([P, T // 2], F32, "picked%d" % i) for i in range(2)]
-        for i, side in enumerate(sides):
-            nc.scalar.activation(picked[i][:], entries(2, side), COPY)
-        last = held([P, T], F32, "last")
-        nc.scalar.activation(last[:], entries(3, slice(0, T)), COPY)
-        first = held([P, T], F32, "first")
-        nc.vector.tensor_tensor(first[:, sides[0]], entries(0, sides[0]), gate_t[0][:, sides[0]], MULT)
-        shared_layer(1, *quantise(hs[1]), TURN_BANK + 1)
-        nc.vector.tensor_tensor(first[:, sides[1]], entries(0, sides[1]), gate_t[0][:, sides[1]], MULT)
-        third = held([P, T], F32, "third")
+        picked = [held([P, T], F32, "picked%d" % i) for i in range(2)]
+        for i in range(2):
+            nc.scalar.activation(picked[i][:], entries(2 + i, whole), COPY)
+        terms = [held([P, T], F32, "term%d" % r) for r in range(TOP)]
+        nc.vector.tensor_tensor(terms[0][:, sides[0]], entries(0, sides[0]), gate_t[:, 0, sides[0]], MULT)
+        shared_layer(1, TURN_BANK + 1)
+        nc.vector.tensor_tensor(terms[0][:, sides[1]], entries(0, sides[1]), gate_t[:, 0, sides[1]], MULT)
         pair = [banked([P, 2, P], LINEAR_BANK + i) for i in range(2)]
-        add_turned(pair, first, range(4), True, False)
-        for i, side in enumerate(sides):
-            nc.vector.tensor_tensor(third[:, side], picked[i][:], gate_t[2][:, side], MULT)
-            add_turned(pair, third, (2 * i, 2 * i + 1), False, True)
-        second = []
-        for i, side in enumerate(sides):
-            second.append(held([P, T // 2], F32, "picked%d" % i))
-            nc.vector.tensor_tensor(second[i][:], entries(1, side), gate_t[1][:, side], MULT)
-        fourth = held([P, T], F32, "fourth")
+        add_turned(pair, terms[0], range(4), True, False)
+        nc.vector.tensor_tensor(terms[2][:], picked[0][:], gate_t[:, 2, :], MULT)
+        add_turned(pair, terms[2], range(4), False, True)
+        nc.vector.tensor_tensor(terms[1][:, sides[0]], entries(1, sides[0]), gate_t[:, 1, sides[0]], MULT)
+        nc.vector.tensor_tensor(terms[3][:], picked[1][:], gate_t[:, 3, :], MULT)
+        nc.vector.tensor_tensor(terms[1][:, sides[1]], entries(1, sides[1]), gate_t[:, 1, sides[1]], MULT)
         rest = held([P, T], F32, "rest")
         for side in sides:
-            nc.vector.tensor_tensor(fourth[:, side], last[:, side], gate_t[3][:, side], MULT)
-        for i, side in enumerate(sides):
-            nc.vector.tensor_tensor(rest[:, side], second[i][:], fourth[:, side], ADD)
+            nc.vector.tensor_tensor(rest[:, side], terms[1][:, side], terms[3][:, side], ADD)
         triple = [banked([P, 2, P], LINEAR_BANK + 2 + i) for i in range(2)]
         add_turned(triple, ys, range(4), True, False)
         pair_rows = held([P, T], F32, "pair_rows")

@@ -87,13 +87,13 @@ def tile_moe_shf_glu_gelu_kernel(
         s1 = [zeroed_planes(w1_scales[0:FIRST_SCALES, 0], "s1a", nc.vector),
               zeroed_planes(w1_scales[FIRST_SCALES:E, 0], "s1b", nc.vector)]
         s13s = held([P, H], U8, "s13s")
-        nc.vector.memset(s13s[:].bitcast(I32), 0)
+        nc.gpsimd.memset(s13s[:].bitcast(I32), 0)
         s3 = zeroed_planes(w3_scales, "s3", nc.vector)
         ident = held([P, P], F32, "ident")
         make_identity(nc, ident[:])
         s2 = zeroed_planes(w2_scales, "s2", nc.gpsimd)
         s2s = held([P, N], U8, "s2s")
-        gate_t = held([P, TOP, T], F32, "gate_t")
+        gate_t = [held([P, 2, T], F32, "gate%d" % i) for i in range(2)]
 
         offs_t = load_list(offs, "offs_t")
         spread_plane(xs, x_scales[0], (nc.sync, nc.sync, nc.scalar, nc.scalar))
@@ -103,19 +103,21 @@ def tile_moe_shf_glu_gelu_kernel(
         w1_t.append(load_fp4_words(w1_words, FIRST_SCALES, FIRST_W1, "w1_1"))
         load_planes(s1[1], w1_scales[FIRST_SCALES:E, 0])
         load_rows(s13s, 0, w1s_scales[0])
-        load_rows(s13s, 4, w3s_scales[0])
         w3_t = [load_fp4_words(w3_words, 0, FIRST_W3, "w3_0")]
         w1s_t = load_fp8_words(w1s_words, "w1s_t")
         load_planes(s3, w3_scales[:, 0])
         w1_t.append(load_fp4_words(w1_words, FIRST_W1, E, "w1_2"))
+        load_rows(s13s, 4, w3s_scales[0])
         w3_t.append(load_fp4_words(w3_words, FIRST_W3, E, "w3_1"))
         load_planes(s2, w2_scales[:, 0])
         w2_t = load_fp4_words(w2_words, 0, E, "w2_t")
         w3s_t = load_fp8_words(w3s_words, "w3s_t")
         w2s_t = load_fp8_words(w2s_words, "w2s_t")
         spread_plane(s2s, w2s_scales[0], (nc.sync,) * 4)
-        pos_t = [load_list(src, "pos_t%d" % r) for r, src in enumerate((pos1, pos2, pos3, pos4))]
-        nc.sync.dma_start(gate_t[:], gate.rearrange("r p t -> p r t"))
+        pos_t = {r: load_list(src, "pos_t%d" % r) for r, src in ((2, pos3), (3, pos4), (0, pos1))}
+        nc.sync.dma_start(gate_t[0][:], gate[0:TOP:2].rearrange("r p t -> p r t"))
+        pos_t[1] = load_list(pos2, "pos_t1")
+        nc.sync.dma_start(gate_t[1][:], gate[1:TOP:2].rearrange("r p t -> p r t"))
 
         def expert_of(parts, bounds, g):
             k = sum(1 for b in bounds if g >= b)
@@ -151,8 +153,10 @@ def tile_moe_shf_glu_gelu_kernel(
             nc.vector.tensor_copy(words[:], xw[:].bitcast(U32).indirect(idx))
             tokens[g] = (words[:], scales[:])
 
-        def by_slot(engine, dst, src):
-            engine(dst.rearrange("p (d m) -> p d m", d=4), src.rearrange("p (m d) -> p d m", d=4))
+        def by_slot(branch, src):
+            shared[branch] = held([P, H], U32, "slots%d" % branch)
+            nc.scalar.copy(shared[branch][:].rearrange("p (d m) -> p m d", d=4),
+                           src[:].bitcast(U32).rearrange("p (m d) -> p m d", d=4))
 
         def project(place, g, j, branch):
             acc = banked([P, H], place)
@@ -166,7 +170,7 @@ def tile_moe_shf_glu_gelu_kernel(
             toks = slice(j * P, (j + 1) * P)
             for d in range(4):
                 cols = slice(d * P, (d + 1) * P)
-                nc.tensor.matmul_mx(out=acc[:, cols], lhsT=shared["words"][:, branch, cols].bitcast(FP8X4),
+                nc.tensor.matmul_mx(out=acc[:, cols], lhsT=shared[branch][:, cols].bitcast(FP8X4),
                                     lhsT_scale=shared["planes"][4 * branch:P, cols],
                                     rhs=xw[:, toks].bitcast(FP8X4), rhs_scale=xs[:, toks], start=True, stop=True)
             return acc[:].rearrange("p (d t) -> p t d", d=4)
@@ -241,14 +245,14 @@ def tile_moe_shf_glu_gelu_kernel(
         for g in range(E):
             gather(g)
             if g == FIRST_W1:
+                by_slot(0, w1s_t)
                 for k in range(2 * LEAD):
                     linear(k // 2, k % 2 if k < 2 else 1 - k % 2, LINEAR_BANK + k)
             activate_both(g)
-        shared["planes"] = held([P, H], U8, "s1b")
-        shared["words"] = held([P, 2, H], U32, "w1_2")
-        by_slot(nc.gpsimd.tensor_copy, shared["planes"][:], s13s[:])
-        by_slot(nc.gpsimd.tensor_copy, shared["words"][:, 0], w1s_t[:].bitcast(U32))
-        by_slot(nc.gpsimd.tensor_copy, shared["words"][:, 1], w3s_t[:].bitcast(U32))
+        joined = held([P, H], U8, "joined")
+        nc.gpsimd.tensor_copy(joined[:].bitcast(I32), s13s[:].bitcast(I32))
+        shared["planes"] = held([P, H], U8, "planes_s")
+        nc.vector.tensor_copy(shared["planes"][:].rearrange("p (d m) -> p d m", d=4), joined[:].rearrange("p (m d) -> p d m", d=4))
 
         def ahead(g, j):
             return (g + LEAD, 1 - j) if g + LEAD < E else (E, 2 * (g + LEAD - E) + 1 - j)
@@ -263,6 +267,8 @@ def tile_moe_shf_glu_gelu_kernel(
             if g < E - 1:
                 linear(*ahead(g, 1), lin_bank[g, 1])
             turn(g)
+            if g == 4:
+                by_slot(1, w3s_t)
             if g >= LAG and (g - LAG) % 2 == 0:
                 second_layer(g - LAG)
         linear(E, 3, lin_bank[E - 1, 0])
@@ -287,28 +293,31 @@ def tile_moe_shf_glu_gelu_kernel(
             return y_all[:].indirect(pos_t[r][:, side.start // 16:side.stop // 16])
 
         picked = [held([P, T], F32, "picked%d" % i) for i in range(2)]
-        for i in range(2):
-            nc.scalar.activation(picked[i][:], entries(2 + i, whole), COPY)
+        for side in sides:
+            nc.scalar.activation(picked[0][:, side], entries(2, side), COPY)
+        nc.scalar.activation(picked[1][:], entries(3, whole), COPY)
         terms = [held([P, T], F32, "term%d" % r) for r in range(TOP)]
-        nc.vector.tensor_tensor(terms[0][:, sides[0]], entries(0, sides[0]), gate_t[:, 0, sides[0]], MULT)
+        nc.vector.tensor_tensor(terms[0][:, sides[0]], entries(0, sides[0]), gate_t[0][:, 0, sides[0]], MULT)
         shared_layer(1, TURN_BANK + 1)
-        nc.vector.tensor_tensor(terms[0][:, sides[1]], entries(0, sides[1]), gate_t[:, 0, sides[1]], MULT)
+        nc.vector.tensor_tensor(terms[0][:, sides[1]], entries(0, sides[1]), gate_t[0][:, 0, sides[1]], MULT)
         pair = [banked([P, 2, P], LINEAR_BANK + i) for i in range(2)]
         add_turned(pair, terms[0], range(4), True, False)
-        nc.vector.tensor_tensor(terms[2][:], picked[0][:], gate_t[:, 2, :], MULT)
-        add_turned(pair, terms[2], range(4), False, True)
-        nc.vector.tensor_tensor(terms[1][:, sides[0]], entries(1, sides[0]), gate_t[:, 1, sides[0]], MULT)
-        nc.vector.tensor_tensor(terms[3][:], picked[1][:], gate_t[:, 3, :], MULT)
-        nc.vector.tensor_tensor(terms[1][:, sides[1]], entries(1, sides[1]), gate_t[:, 1, sides[1]], MULT)
+        for i, side in enumerate(sides):
+            nc.vector.tensor_tensor(terms[2][:, side], picked[0][:, side], gate_t[0][:, 1, side], MULT)
+            add_turned(pair, terms[2], (2 * i, 2 * i + 1), False, True)
+        nc.vector.tensor_tensor(terms[1][:, sides[0]], entries(1, sides[0]), gate_t[1][:, 0, sides[0]], MULT)
+        nc.vector.tensor_tensor(terms[3][:], picked[1][:], gate_t[1][:, 1, :], MULT)
+        nc.vector.tensor_tensor(terms[1][:, sides[1]], entries(1, sides[1]), gate_t[1][:, 0, sides[1]], MULT)
         rest = held([P, T], F32, "rest")
         for side in sides:
             nc.vector.tensor_tensor(rest[:, side], terms[1][:, side], terms[3][:, side], ADD)
         triple = [banked([P, 2, P], LINEAR_BANK + 2 + i) for i in range(2)]
-        add_turned(triple, ys, range(4), True, False)
+        add_turned(triple, ys, (0, 1), True, False)
         pair_rows = held([P, T], F32, "pair_rows")
         for i, side in enumerate(sides):
             nc.scalar.copy(pair_rows[:, side], pair[i][:].rearrange("p b n -> p (b n)"))
-            add_turned(triple, pair_rows, (2 * i, 2 * i + 1), False, True)
+            add_turned(triple, pair_rows, (2 * i, 2 * i + 1), i == 1, i == 0)
+        add_turned(triple, ys, (2, 3), False, True)
         for i, side in enumerate(sides):
             res = held([P, T // 2], F32, "res%d" % i)
             nc.vector.tensor_tensor(res[:], triple[i][:].rearrange("p b t -> p (b t)"), rest[:, side], ADD)

@@ -206,7 +206,7 @@ def tile_moe_shf_glu_gelu_kernel(
 
         def turn(g):
             turned = banked([P, 2, 2, P], in_turn(TURN_BANK))
-            for j in range(2):
+            for j in (1, 0):
                 for u in range(2):
                     nc.tensor.transpose(turned[:, j, u, :], h[g][:, j, u].rearrange("s p e -> s (p e)").bitcast(F32), ident[:])
             if g >= PAIRED or g % 2 == 0:
@@ -259,8 +259,8 @@ def tile_moe_shf_glu_gelu_kernel(
 
         for g in range(E):
             multiply(g, 0)
-            if 0 <= g - 2 < UNITS:
-                gelu(E, g - 2, project(in_turn(SMALL_BANK), E, g - 2, 0))
+            if 0 <= g - LEAD < UNITS - 1:
+                gelu(E, g - LEAD, project(in_turn(SMALL_BANK), E, g - LEAD, 0))
             if g < E - 1:
                 linear(*ahead(g, 0), lin_bank[g, 0])
             multiply(g, 1)
@@ -271,6 +271,7 @@ def tile_moe_shf_glu_gelu_kernel(
                 by_slot(1, w3s_t)
             if g >= LAG and (g - LAG) % 2 == 0:
                 second_layer(g - LAG)
+        gelu(E, 3, project(in_turn(SMALL_BANK), E, 3, 0))
         linear(E, 3, lin_bank[E - 1, 0])
         linear(E, 2, lin_bank[E - 1, 1])
         multiply(E, 0)

@@ -3,7 +3,7 @@ from contextlib import ExitStack
 import concourse.mybir as mybir
 from concourse.masks import make_identity
 
-K, T, E, C, H, N, TOP = 512, 512, 8, 256, 512, 128, 4
+T, E, C, H, N, TOP = 512, 8, 256, 512, 128, 4
 FLOPS = 3019898880
 
 F32 = mybir.dt.float32
@@ -20,15 +20,21 @@ MULT = mybir.AluOpType.mult
 ADD = mybir.AluOpType.add
 
 P = 128
-BANKS = 8
-UNITS = T // P
-FIRST_SCALES = 2
-FIRST_W1 = 6
+PER_COLUMN = 16
+SHARED = E
+SHARED_PARTS = T // P
+W3S_ROWS = 4
+
+FIRST_EXPERTS = 2
+GELU_AHEAD = 6
 FIRST_W3 = 4
+
 LEAD = 2
 LAG = 3
-PAIRED = 6
+PAIRED = E - 2
+
 TURN_BANK, SMALL_BANK, LINEAR_BANK = 0, 2, 4
+GELU_BANKS = LINEAR_BANK
 
 
 def tile_moe_shf_glu_gelu_kernel(
@@ -39,14 +45,14 @@ def tile_moe_shf_glu_gelu_kernel(
     nc = tc.nc
     with ExitStack() as ctx:
         keep = ctx.enter_context(tc.tile_pool(name="keep", bufs=1))
-        ring = ctx.enter_context(tc.tile_pool(name="ring", bufs=LAG))
+        ring = ctx.enter_context(tc.tile_pool(name="ring", bufs=1))
         psum = ctx.enter_context(tc.psum_pool(name="psum", bufs=1))
 
         def held(shape, dtype, name):
             return keep.tile(shape, dtype, name=name, align_bytes=64)
 
-        def banked(shape, place):
-            return psum.tile(shape, F32, name="bank%d" % (place % BANKS))
+        def banked(shape, bank):
+            return psum.tile(shape, F32, name="bank%d" % bank)
 
         def load_list(src, name):
             t = keep.tile(list(src.shape), U16, name=name)
@@ -67,7 +73,7 @@ def tile_moe_shf_glu_gelu_kernel(
             for q in range(4):
                 rows = src[4 * q:4 * q + 4, :].bitcast(I32)
                 queues[q].dma_start(t[32 * q:32 * q + 32, :].bitcast(I32),
-                                  rows.unsqueeze(0).to_broadcast([8, 4, rows.shape[1]]))
+                                    rows.unsqueeze(0).to_broadcast([8, 4, rows.shape[1]]))
 
         def zeroed_planes(src, name, engine):
             t = held([P, src.shape[0], src.shape[-1]], U8, name)
@@ -80,14 +86,15 @@ def tile_moe_shf_glu_gelu_kernel(
 
         def load_rows(t, first, src):
             for q in range(4):
-                nc.sync.dma_start(t[32 * q + first:32 * q + first + 4, :].bitcast(I32), src[4 * q:4 * q + 4, :].bitcast(I32))
+                nc.sync.dma_start(t[32 * q + first:32 * q + first + 4, :].bitcast(I32),
+                                  src[4 * q:4 * q + 4, :].bitcast(I32))
 
         xw = held([P, T], I32, "xw")
         xs = held([P, T], U8, "xs")
-        s1 = [zeroed_planes(w1_scales[0:FIRST_SCALES, 0], "s1a", nc.vector),
-              zeroed_planes(w1_scales[FIRST_SCALES:E, 0], "s1b", nc.vector)]
+        s1 = [zeroed_planes(w1_scales[0:FIRST_EXPERTS, 0], "s1a", nc.vector),
+              zeroed_planes(w1_scales[FIRST_EXPERTS:E, 0], "s1b", nc.vector)]
         s13s = held([P, H], U8, "s13s")
-        nc.gpsimd.memset(s13s[:].bitcast(I32), 0)
+        nc.vector.memset(s13s[:].bitcast(I32), 0)
         s3 = zeroed_planes(w3_scales, "s3", nc.vector)
         ident = held([P, P], F32, "ident")
         make_identity(nc, ident[:])
@@ -98,16 +105,16 @@ def tile_moe_shf_glu_gelu_kernel(
         offs_t = load_list(offs, "offs_t")
         spread_plane(xs, x_scales[0], (nc.sync, nc.sync, nc.scalar, nc.scalar))
         nc.scalar.dma_start(xw[:], x_words[0].rearrange("p n d -> p (n d)").bitcast(I32))
-        w1_t = [load_fp4_words(w1_words, 0, FIRST_SCALES, "w1_0")]
-        load_planes(s1[0], w1_scales[0:FIRST_SCALES, 0])
-        w1_t.append(load_fp4_words(w1_words, FIRST_SCALES, FIRST_W1, "w1_1"))
-        load_planes(s1[1], w1_scales[FIRST_SCALES:E, 0])
+        w1_t = [load_fp4_words(w1_words, 0, FIRST_EXPERTS, "w1_0")]
+        load_planes(s1[0], w1_scales[0:FIRST_EXPERTS, 0])
+        w1_t.append(load_fp4_words(w1_words, FIRST_EXPERTS, GELU_AHEAD, "w1_1"))
+        load_planes(s1[1], w1_scales[FIRST_EXPERTS:E, 0])
         load_rows(s13s, 0, w1s_scales[0])
         w3_t = [load_fp4_words(w3_words, 0, FIRST_W3, "w3_0")]
         w1s_t = load_fp8_words(w1s_words, "w1s_t")
         load_planes(s3, w3_scales[:, 0])
-        w1_t.append(load_fp4_words(w1_words, FIRST_W1, E, "w1_2"))
-        load_rows(s13s, 4, w3s_scales[0])
+        w1_t.append(load_fp4_words(w1_words, GELU_AHEAD, E, "w1_2"))
+        load_rows(s13s, W3S_ROWS, w3s_scales[0])
         w3_t.append(load_fp4_words(w3_words, FIRST_W3, E, "w3_1"))
         load_planes(s2, w2_scales[:, 0])
         w2_t = load_fp4_words(w2_words, 0, E, "w2_t")
@@ -119,15 +126,15 @@ def tile_moe_shf_glu_gelu_kernel(
         pos_t[1] = load_list(pos2, "pos_t1")
         nc.sync.dma_start(gate_t[1][:], gate[1:TOP:2].rearrange("r p t -> p r t"))
 
-        def expert_of(parts, bounds, g):
-            k = sum(1 for b in bounds if g >= b)
-            return parts[k][:, g - ([0] + list(bounds))[k], :]
+        def expert_of(loads, starts, g):
+            k = sum(1 for start in starts if g >= start) - 1
+            return loads[k][:, g - starts[k], :]
 
         def gelu_weights(g):
-            return expert_of(w1_t, (FIRST_SCALES, FIRST_W1), g).bitcast(FP4X4), expert_of(s1, (FIRST_SCALES,), g)
+            return expert_of(w1_t, (0, FIRST_EXPERTS, GELU_AHEAD), g).bitcast(FP4X4), expert_of(s1, (0, FIRST_EXPERTS), g)
 
         def linear_weights(g):
-            return expert_of(w3_t, (FIRST_W3,), g).bitcast(FP4X4), s3[:, g, :]
+            return expert_of(w3_t, (0, FIRST_W3), g).bitcast(FP4X4), s3[:, g, :]
 
         tokens = {}
         act = {}
@@ -136,7 +143,7 @@ def tile_moe_shf_glu_gelu_kernel(
         h = {}
         h_t = {}
         hs = []
-        shared = {}
+        sorted_words = {}
         y_all = held([P, E * C], F32, "y_all")
         ys = held([P, T], F32, "ys")
         taken = {TURN_BANK: 0, SMALL_BANK: 0}
@@ -146,73 +153,80 @@ def tile_moe_shf_glu_gelu_kernel(
             return first + (taken[first] - 1) % 2
 
         def gather(g):
-            idx = offs_t[:, g * C // 16:(g + 1) * C // 16]
+            idx = offs_t[:, g * C // PER_COLUMN:(g + 1) * C // PER_COLUMN]
             words = held([P, C], U32, "words%d" % g)
             scales = held([P, C], U8, "scales%d" % g)
             nc.vector.tensor_copy(scales[:], xs[:].indirect(idx))
             nc.vector.tensor_copy(words[:], xw[:].bitcast(U32).indirect(idx))
             tokens[g] = (words[:], scales[:])
 
-        def by_slot(branch, src):
-            shared[branch] = held([P, H], U32, "slots%d" % branch)
-            nc.scalar.copy(shared[branch][:].rearrange("p (d m) -> p m d", d=4),
-                           src[:].bitcast(U32).rearrange("p (m d) -> p m d", d=4))
+        def sort_words(branch, src):
+            sorted_words[branch] = held([P, H], U32, "sorted%d" % branch)
+            nc.scalar.copy(sorted_words[branch][:].rearrange("k (d p) -> k p d", d=4),
+                           src[:].bitcast(U32).rearrange("k (p d) -> k p d", d=4))
 
-        def project(place, g, j, branch):
-            acc = banked([P, H], place)
-            if g < E:
+        def project(bank, g, j, branch):
+            acc = banked([P, H], bank)
+            toks = slice(j * P, (j + 1) * P)
+            if g != SHARED:
                 words, scales = tokens[g]
                 w, s = (gelu_weights, linear_weights)[branch](g)
-                cols = slice(j * P, (j + 1) * P)
-                nc.tensor.matmul_mx(out=acc[:], lhsT=words[:, cols].bitcast(FP8X4), lhsT_scale=scales[:, cols],
+                nc.tensor.matmul_mx(out=acc[:], lhsT=words[:, toks].bitcast(FP8X4), lhsT_scale=scales[:, toks],
                                     rhs=w, rhs_scale=s, start=True, stop=True)
                 return acc[:].rearrange("s (p u e) -> s u p e", u=2, e=2)
-            toks = slice(j * P, (j + 1) * P)
             for d in range(4):
                 cols = slice(d * P, (d + 1) * P)
-                nc.tensor.matmul_mx(out=acc[:, cols], lhsT=shared[branch][:, cols].bitcast(FP8X4),
-                                    lhsT_scale=shared["planes"][4 * branch:P, cols],
+                nc.tensor.matmul_mx(out=acc[:, cols], lhsT=sorted_words[branch][:, cols].bitcast(FP8X4),
+                                    lhsT_scale=sorted_planes[W3S_ROWS * branch:P, cols],
                                     rhs=xw[:, toks].bitcast(FP8X4), rhs_scale=xs[:, toks], start=True, stop=True)
             return acc[:].rearrange("p (d t) -> p t d", d=4)
 
         def gelu(g, j, acc):
-            t = ring.tile([P, H], F32, name="act", bufs=2 * E + UNITS)
-            act[g, j] = t[:].rearrange("p (a b c) -> p a b c", a=2, c=2) if g < E else t[:].rearrange("p (t d) -> p t d", d=4)
+            t = ring.tile([P, H], F32, name="act", bufs=2 * E + SHARED_PARTS)
+            if g != SHARED:
+                act[g, j] = t[:].rearrange("s (u p e) -> s u p e", u=2, e=2)
+            else:
+                act[g, j] = t[:].rearrange("p (t d) -> p t d", d=4)
             nc.scalar.activation(act[g, j], acc, GELU)
 
-        def activate_both(g):
-            if g in (0, FIRST_W1):
-                gelu(g, 0, project(0, g, 0, 0))
-                gelu(g, 1, project(1, g, 1, 0))
-                return
-            later = project((2 * g) % 4, g, 1, 0)
-            gelu(g, 0, project((2 * g + 1) % 4, g, 0, 0))
-            gelu(g, 1, later)
+        def gelu_both(g):
+            first_bank = 2 * g % GELU_BANKS
+            if g in (0, GELU_AHEAD):
+                gelu(g, 0, project(first_bank, g, 0, 0))
+                gelu(g, 1, project(first_bank + 1, g, 1, 0))
+            else:
+                other = project(first_bank, g, 1, 0)
+                gelu(g, 0, project(first_bank + 1, g, 0, 0))
+                gelu(g, 1, other)
 
-        def linear(g, j, place):
-            lin_bank[g, j] = place
-            lin[g, j] = project(place, g, j, 1)
+        def gelu_shared(j):
+            gelu(SHARED, j, project(in_turn(SMALL_BANK), SHARED, j, 0))
+
+        def linear(g, j, bank):
+            lin_bank[g, j] = bank
+            lin[g, j] = project(bank, g, j, 1)
 
         def multiply(g, j):
-            if g == E:
+            if g == SHARED:
                 if j % 2 == 0:
                     hs.append(held([P, C * 4], BF16, ("hs", "late")[j // 2]))
                 dst = hs[-1][:, j % 2 * H:(j % 2 + 1) * H].rearrange("p (t d) -> p t d", d=4)
             else:
                 if j == 0:
-                    h[g] = ring.tile([P, 2, 2, P, 2], BF16, name="h", bufs=2)
+                    h[g] = ring.tile([P, 2, 2, P, 2], BF16, name="h", bufs=LEAD)
                 dst = h[g][:, j]
             nc.vector.tensor_tensor(dst, lin[g, j], act[g, j], MULT)
 
         def turn(g):
             turned = banked([P, 2, 2, P], in_turn(TURN_BANK))
-            for j in (1, 0):
+            for j in (1, 0) if g < E - 1 else (0, 1):
                 for u in range(2):
-                    nc.tensor.transpose(turned[:, j, u, :], h[g][:, j, u].rearrange("s p e -> s (p e)").bitcast(F32), ident[:])
-            if g >= PAIRED or g % 2 == 0:
+                    nc.tensor.transpose(turned[:, j, u, :], h[g][:, j, u].rearrange("s p e -> s (p e)").bitcast(F32),
+                                        ident[:])
+            place = g % 2 if g < PAIRED else 0
+            if place == 0:
                 h_t[g] = held([P, (2 if g < PAIRED else 1) * C * 4], BF16, "late" if g == E - 1 else "h_t%d" % g)
-            k = g % 2 if g < PAIRED else 0
-            dst = h_t[g - k][:, k * C * 4:(k + 1) * C * 4]
+            dst = h_t[g - place][:, place * C * 4:(place + 1) * C * 4]
             nc.scalar.copy(dst.bitcast(F32).rearrange("p (j s u) -> p j s u", j=2, u=2),
                            turned[:].rearrange("p j u s -> p j s u"))
 
@@ -223,64 +237,70 @@ def tile_moe_shf_glu_gelu_kernel(
             nc.vector.quantize_mx(out=codes[:].bitcast(FP8X4), scales=planes[:], in_=src[:])
             return codes, planes
 
-        def second_layer(g, place=None):
+        def second_layer(g, bank):
             codes, planes = quantise(h_t[g])
             width = codes.shape[1]
-            y = banked([P, width], in_turn(SMALL_BANK) if place is None else place)
+            y = banked([P, width], bank)
             for k in range(width // C):
                 cols = slice(k * C, (k + 1) * C)
                 nc.tensor.matmul_mx(out=y[:, cols], lhsT=w2_t[:, g + k, :].bitcast(FP4X4), lhsT_scale=s2[:, g + k, :],
                                     rhs=codes[:, cols].bitcast(FP8X4), rhs_scale=planes[:, cols], start=True, stop=True)
             nc.scalar.copy(y_all[:, g * C:g * C + width], y[:])
 
-        def shared_layer(k, place):
+        def shared_layer(k, bank):
             codes, planes = quantise(hs[k])
-            rows = banked([P, C], place)
+            y = banked([P, C], bank)
             for j in range(2):
                 cols = slice(j * P, (j + 1) * P)
-                nc.tensor.matmul_mx(out=rows[:, cols], lhsT=codes[:, cols].bitcast(FP8X4), lhsT_scale=planes[:, cols],
+                nc.tensor.matmul_mx(out=y[:, cols], lhsT=codes[:, cols].bitcast(FP8X4), lhsT_scale=planes[:, cols],
                                     rhs=w2s_t[:].bitcast(FP8X4), rhs_scale=s2s[:], start=True, stop=True)
-            nc.scalar.copy(ys[:, k * C:(k + 1) * C], rows[:])
+            nc.scalar.copy(ys[:, k * C:(k + 1) * C], y[:])
 
         for g in range(E):
             gather(g)
-            if g == FIRST_W1:
-                by_slot(0, w1s_t)
-                for k in range(2 * LEAD):
-                    linear(k // 2, k % 2 if k < 2 else 1 - k % 2, LINEAR_BANK + k)
-            activate_both(g)
-        joined = held([P, H], U8, "joined")
-        nc.gpsimd.tensor_copy(joined[:].bitcast(I32), s13s[:].bitcast(I32))
-        shared["planes"] = held([P, H], U8, "planes_s")
-        nc.vector.tensor_copy(shared["planes"][:].rearrange("p (d m) -> p d m", d=4), joined[:].rearrange("p (m d) -> p d m", d=4))
+            if g == GELU_AHEAD:
+                sort_words(0, w1s_t)
+                parts = [(e, j) for e in range(LEAD) for j in ((0, 1) if e == 0 else (1, 0))]
+                for k, part in enumerate(parts):
+                    linear(*part, LINEAR_BANK + k)
+            gelu_both(g)
+        sorted_planes = held([P, H], U8, "planes_s")
+        nc.vector.tensor_copy(sorted_planes[:].rearrange("k (d p) -> k d p", d=4),
+                              s13s[:].rearrange("k (p d) -> k d p", d=4))
 
-        def ahead(g, j):
-            return (g + LEAD, 1 - j) if g + LEAD < E else (E, 2 * (g + LEAD - E) + 1 - j)
+        def linear_ahead(g, j):
+            ahead = g + LEAD
+            part = (ahead, 1 - j) if ahead < E else (SHARED, 2 * (ahead - E) + 1 - j)
+            linear(*part, lin_bank[g, j])
 
-        for g in range(E):
+        for g in range(E - 1):
             multiply(g, 0)
-            if 0 <= g - LEAD < UNITS - 1:
-                gelu(E, g - LEAD, project(in_turn(SMALL_BANK), E, g - LEAD, 0))
-            if g < E - 1:
-                linear(*ahead(g, 0), lin_bank[g, 0])
+            if 0 <= g - LEAD < SHARED_PARTS - 1:
+                gelu_shared(g - LEAD)
+            linear_ahead(g, 0)
             multiply(g, 1)
-            if g < E - 1:
-                linear(*ahead(g, 1), lin_bank[g, 1])
+            linear_ahead(g, 1)
             turn(g)
-            if g == 4:
-                by_slot(1, w3s_t)
+            if g == E - 2 * LEAD:
+                sort_words(1, w3s_t)
             if g >= LAG and (g - LAG) % 2 == 0:
-                second_layer(g - LAG)
-        gelu(E, 3, project(in_turn(SMALL_BANK), E, 3, 0))
-        linear(E, 3, lin_bank[E - 1, 0])
-        linear(E, 2, lin_bank[E - 1, 1])
-        multiply(E, 0)
-        multiply(E, 1)
-        second_layer(E - 2, TURN_BANK)
-        second_layer(E - 1, lin_bank[E, 0])
-        shared_layer(0, lin_bank[E, 1])
-        multiply(E, 2)
-        multiply(E, 3)
+                second_layer(g - LAG, in_turn(SMALL_BANK))
+
+        last = E - 1
+        multiply(last, 0)
+        multiply(last, 1)
+        turn(last)
+        second_layer(last - LAG, in_turn(SMALL_BANK))
+        gelu_shared(SHARED_PARTS - 1)
+        linear_ahead(last, 0)
+        linear_ahead(last, 1)
+        multiply(SHARED, 0)
+        multiply(SHARED, 1)
+        second_layer(last - 1, TURN_BANK)
+        second_layer(last, lin_bank[SHARED, 0])
+        shared_layer(0, lin_bank[SHARED, 1])
+        multiply(SHARED, 2)
+        multiply(SHARED, 3)
 
         def add_turned(banks, src, blocks, start, stop):
             for b in blocks:
@@ -289,36 +309,40 @@ def tile_moe_shf_glu_gelu_kernel(
 
         whole = slice(0, T)
         sides = (slice(0, T // 2), slice(T // 2, T))
+        blocks_of = ((0, 1), (2, 3))
 
-        def entries(r, side):
-            return y_all[:].indirect(pos_t[r][:, side.start // 16:side.stop // 16])
+        def entries(r, cols):
+            return y_all[:].indirect(pos_t[r][:, cols.start // PER_COLUMN:cols.stop // PER_COLUMN])
 
-        picked = [held([P, T], F32, "picked%d" % i) for i in range(2)]
+        def gated(r, cols, src):
+            nc.vector.tensor_tensor(terms[r][:, cols], src, gate_t[r % 2][:, r // 2, cols], MULT)
+
+        picked = {r: held([P, T], F32, "picked%d" % r) for r in (2, 3)}
         for side in sides:
-            nc.scalar.activation(picked[0][:, side], entries(2, side), COPY)
-        nc.scalar.activation(picked[1][:], entries(3, whole), COPY)
+            nc.scalar.activation(picked[2][:, side], entries(2, side), COPY)
+        nc.scalar.activation(picked[3][:], entries(3, whole), COPY)
         terms = [held([P, T], F32, "term%d" % r) for r in range(TOP)]
-        nc.vector.tensor_tensor(terms[0][:, sides[0]], entries(0, sides[0]), gate_t[0][:, 0, sides[0]], MULT)
+        gated(0, sides[0], entries(0, sides[0]))
         shared_layer(1, TURN_BANK + 1)
-        nc.vector.tensor_tensor(terms[0][:, sides[1]], entries(0, sides[1]), gate_t[0][:, 0, sides[1]], MULT)
+        gated(0, sides[1], entries(0, sides[1]))
         pair = [banked([P, 2, P], LINEAR_BANK + i) for i in range(2)]
         add_turned(pair, terms[0], range(4), True, False)
         for i, side in enumerate(sides):
-            nc.vector.tensor_tensor(terms[2][:, side], picked[0][:, side], gate_t[0][:, 1, side], MULT)
-            add_turned(pair, terms[2], (2 * i, 2 * i + 1), False, True)
-        nc.vector.tensor_tensor(terms[1][:, sides[0]], entries(1, sides[0]), gate_t[1][:, 0, sides[0]], MULT)
-        nc.vector.tensor_tensor(terms[3][:], picked[1][:], gate_t[1][:, 1, :], MULT)
-        nc.vector.tensor_tensor(terms[1][:, sides[1]], entries(1, sides[1]), gate_t[1][:, 0, sides[1]], MULT)
+            gated(2, side, picked[2][:, side])
+            add_turned(pair, terms[2], blocks_of[i], False, True)
+        gated(1, sides[0], entries(1, sides[0]))
+        gated(3, whole, picked[3][:])
+        gated(1, sides[1], entries(1, sides[1]))
         rest = held([P, T], F32, "rest")
         for side in sides:
             nc.vector.tensor_tensor(rest[:, side], terms[1][:, side], terms[3][:, side], ADD)
         triple = [banked([P, 2, P], LINEAR_BANK + 2 + i) for i in range(2)]
-        add_turned(triple, ys, (0, 1), True, False)
+        add_turned(triple, ys, blocks_of[0], True, False)
         pair_rows = held([P, T], F32, "pair_rows")
         for i, side in enumerate(sides):
             nc.scalar.copy(pair_rows[:, side], pair[i][:].rearrange("p b n -> p (b n)"))
-            add_turned(triple, pair_rows, (2 * i, 2 * i + 1), i == 1, i == 0)
-        add_turned(triple, ys, (2, 3), False, True)
+            add_turned(triple, pair_rows, blocks_of[i], i == 1, i == 0)
+        add_turned(triple, ys, blocks_of[1], False, True)
         for i, side in enumerate(sides):
             res = held([P, T // 2], F32, "res%d" % i)
             nc.vector.tensor_tensor(res[:], triple[i][:].rearrange("p b t -> p (b t)"), rest[:, side], ADD)

@@ -116,9 +116,9 @@ def tile_moe_shf_glu_gelu_kernel(
         w1_t.append(load_fp4_words(w1_words, GELU_AHEAD, E, "w1_2"))
         load_rows(s13s, W3S_ROWS, w3s_scales[0])
         w3_t.append(load_fp4_words(w3_words, FIRST_W3, E, "w3_1"))
+        w3s_t = load_fp8_words(w3s_words, "w3s_t")
         load_planes(s2, w2_scales[:, 0])
         w2_t = load_fp4_words(w2_words, 0, E, "w2_t")
-        w3s_t = load_fp8_words(w3s_words, "w3s_t")
         w2s_t = load_fp8_words(w2s_words, "w2s_t")
         spread_plane(s2s, w2s_scales[0], (nc.sync,) * 4)
         pos_t = {r: load_list(src, "pos_t%d" % r) for r, src in ((2, pos3), (3, pos4), (0, pos1))}
@@ -161,9 +161,9 @@ def tile_moe_shf_glu_gelu_kernel(
             tokens[g] = (words[:], scales[:])
 
         def sort_words(branch, src):
-            sorted_words[branch] = held([P, H], U32, "sorted%d" % branch)
-            nc.scalar.copy(sorted_words[branch][:].rearrange("k (d p) -> k p d", d=4),
-                           src[:].bitcast(U32).rearrange("k (p d) -> k p d", d=4))
+            sorted_words[branch] = held([P, H], I32, "act0_%d" % branch)
+            nc.gpsimd.tensor_copy(sorted_words[branch][:].rearrange("k (d p) -> k d p", d=4),
+                                  src[:].rearrange("k (p d) -> k d p", d=4))
 
         def project(bank, g, j, branch):
             acc = banked([P, H], bank)
@@ -182,7 +182,7 @@ def tile_moe_shf_glu_gelu_kernel(
             return acc[:].rearrange("p (d t) -> p t d", d=4)
 
         def gelu(g, j, acc):
-            t = ring.tile([P, H], F32, name="act", bufs=2 * E + SHARED_PARTS)
+            t = held([P, H], F32, "act%d_%d" % (g, j))
             if g != SHARED:
                 act[g, j] = t[:].rearrange("s (u p e) -> s u p e", u=2, e=2)
             else:
@@ -259,7 +259,6 @@ def tile_moe_shf_glu_gelu_kernel(
         for g in range(E):
             gather(g)
             if g == GELU_AHEAD:
-                sort_words(0, w1s_t)
                 parts = [(e, j) for e in range(LEAD) for j in ((0, 1) if e == 0 else (1, 0))]
                 for k, part in enumerate(parts):
                     linear(*part, LINEAR_BANK + k)
@@ -281,7 +280,8 @@ def tile_moe_shf_glu_gelu_kernel(
             multiply(g, 1)
             linear_ahead(g, 1)
             turn(g)
-            if g == E - 2 * LEAD:
+            if g == 0:
+                sort_words(0, w1s_t)
                 sort_words(1, w3s_t)
             if g >= LAG and (g - LAG) % 2 == 0:
                 second_layer(g - LAG, in_turn(SMALL_BANK))

@@ -116,9 +116,9 @@ def tile_moe_shf_glu_gelu_kernel(
         w1_t.append(load_fp4_words(w1_words, GELU_AHEAD, E, "w1_2"))
         load_rows(s13s, W3S_ROWS, w3s_scales[0])
         w3_t.append(load_fp4_words(w3_words, FIRST_W3, E, "w3_1"))
-        w3s_t = load_fp8_words(w3s_words, "w3s_t")
         load_planes(s2, w2_scales[:, 0])
         w2_t = load_fp4_words(w2_words, 0, E, "w2_t")
+        w3s_t = load_fp8_words(w3s_words, "w3s_t")
         w2s_t = load_fp8_words(w2s_words, "w2s_t")
         spread_plane(s2s, w2s_scales[0], (nc.sync,) * 4)
         pos_t = {r: load_list(src, "pos_t%d" % r) for r, src in ((2, pos3), (3, pos4), (0, pos1))}
@@ -161,9 +161,13 @@ def tile_moe_shf_glu_gelu_kernel(
             tokens[g] = (words[:], scales[:])
 
         def sort_words(branch, src):
-            sorted_words[branch] = held([P, H], I32, "act0_%d" % branch)
-            nc.gpsimd.tensor_copy(sorted_words[branch][:].rearrange("k (d p) -> k d p", d=4),
-                                  src[:].rearrange("k (p d) -> k d p", d=4))
+            sorted_words[branch] = held([P, H], U32, "sorted%d" % branch)
+            if branch == 0:
+                nc.gpsimd.tensor_copy(sorted_words[branch][:].rearrange("k (d p) -> k d p", d=4),
+                                      src[:].bitcast(U32).rearrange("k (p d) -> k d p", d=4))
+            else:
+                nc.scalar.copy(sorted_words[branch][:].rearrange("k (d p) -> k p d", d=4),
+                               src[:].bitcast(U32).rearrange("k (p d) -> k p d", d=4))
 
         def project(bank, g, j, branch):
             acc = banked([P, H], bank)
@@ -182,7 +186,7 @@ def tile_moe_shf_glu_gelu_kernel(
             return acc[:].rearrange("p (d t) -> p t d", d=4)
 
         def gelu(g, j, acc):
-            t = held([P, H], F32, "act%d_%d" % (g, j))
+            t = ring.tile([P, H], F32, name="act", bufs=2 * E + SHARED_PARTS)
             if g != SHARED:
                 act[g, j] = t[:].rearrange("s (u p e) -> s u p e", u=2, e=2)
             else:
@@ -259,6 +263,7 @@ def tile_moe_shf_glu_gelu_kernel(
         for g in range(E):
             gather(g)
             if g == GELU_AHEAD:
+                sort_words(0, w1s_t)
                 parts = [(e, j) for e in range(LEAD) for j in ((0, 1) if e == 0 else (1, 0))]
                 for k, part in enumerate(parts):
                     linear(*part, LINEAR_BANK + k)
@@ -280,8 +285,7 @@ def tile_moe_shf_glu_gelu_kernel(
             multiply(g, 1)
             linear_ahead(g, 1)
             turn(g)
-            if g == 0:
-                sort_words(0, w1s_t)
+            if g == E - 2 * LEAD:
                 sort_words(1, w3s_t)
             if g >= LAG and (g - LAG) % 2 == 0:
                 second_layer(g - LAG, in_turn(SMALL_BANK))

@@ -110,11 +110,11 @@ def tile_moe_shf_glu_gelu_kernel(
         w1_t.append(load_fp4_words(w1_words, FIRST_EXPERTS, GELU_AHEAD, "w1_1"))
         load_planes(s1[1], w1_scales[FIRST_EXPERTS:E, 0])
         load_rows(s13s, 0, w1s_scales[0])
+        load_rows(s13s, W3S_ROWS, w3s_scales[0])
         w3_t = [load_fp4_words(w3_words, 0, FIRST_W3, "w3_0")]
-        w1s_t = load_fp8_words(w1s_words, "w1s_t")
         load_planes(s3, w3_scales[:, 0])
         w1_t.append(load_fp4_words(w1_words, GELU_AHEAD, E, "w1_2"))
-        load_rows(s13s, W3S_ROWS, w3s_scales[0])
+        w1s_t = load_fp8_words(w1s_words, "w1s_t")
         w3_t.append(load_fp4_words(w3_words, FIRST_W3, E, "w3_1"))
         load_planes(s2, w2_scales[:, 0])
         w2_t = load_fp4_words(w2_words, 0, E, "w2_t")
@@ -162,12 +162,8 @@ def tile_moe_shf_glu_gelu_kernel(
 
         def sort_words(branch, src):
             sorted_words[branch] = held([P, H], U32, "sorted%d" % branch)
-            if branch == 0:
-                nc.gpsimd.tensor_copy(sorted_words[branch][:].rearrange("k (d p) -> k d p", d=4),
-                                      src[:].bitcast(U32).rearrange("k (p d) -> k d p", d=4))
-            else:
-                nc.scalar.copy(sorted_words[branch][:].rearrange("k (d p) -> k p d", d=4),
-                               src[:].bitcast(U32).rearrange("k (p d) -> k p d", d=4))
+            nc.scalar.copy(sorted_words[branch][:].rearrange("k (d p) -> k p d", d=4),
+                           src[:].bitcast(U32).rearrange("k (p d) -> k p d", d=4))
 
         def project(bank, g, j, branch):
             acc = banked([P, H], bank)
@@ -269,7 +265,7 @@ def tile_moe_shf_glu_gelu_kernel(
                     linear(*part, LINEAR_BANK + k)
             gelu_both(g)
         sorted_planes = held([P, H], U8, "planes_s")
-        nc.vector.tensor_copy(sorted_planes[:].rearrange("k (d p) -> k d p", d=4),
+        nc.gpsimd.tensor_copy(sorted_planes[:].rearrange("k (d p) -> k d p", d=4),
                               s13s[:].rearrange("k (p d) -> k d p", d=4))
 
         def linear_ahead(g, j):

@@ -31,6 +31,7 @@ FIRST_W3 = 4
 
 LEAD = 2
 LAG = 3
+SHARED_GELU_AT = (2, 4, 6)
 PAIRED = E - 2
 
 TURN_BANK, SMALL_BANK, LINEAR_BANK = 0, 2, 4
@@ -213,7 +214,7 @@ def tile_moe_shf_glu_gelu_kernel(
                 dst = hs[-1][:, j % 2 * H:(j % 2 + 1) * H].rearrange("p (t d) -> p t d", d=4)
             else:
                 if j == 0:
-                    h[g] = ring.tile([P, 2, 2, P, 2], BF16, name="h", bufs=LEAD)
+                    h[g] = held([P, 2, 2, P, 2], BF16, "h%d" % (LEAD if g >= LEAD and g % 2 == 0 else g))
                 dst = h[g][:, j]
             nc.vector.tensor_tensor(dst, lin[g, j], act[g, j], MULT)
 
@@ -275,8 +276,8 @@ def tile_moe_shf_glu_gelu_kernel(
 
         for g in range(E - 1):
             multiply(g, 0)
-            if 0 <= g - LEAD < SHARED_PARTS - 1:
-                gelu_shared(g - LEAD)
+            if g in SHARED_GELU_AT:
+                gelu_shared(SHARED_GELU_AT.index(g))
             linear_ahead(g, 0)
             multiply(g, 1)
             linear_ahead(g, 1)

@@ -34,7 +34,7 @@ LAG = 3
 SHARED_GELU_AT = (2, 4, 6)
 PAIRED = E - 2
 
-TURN_BANK, SMALL_BANK, LINEAR_BANK = 0, 2, 4
+TURN_BANK, SMALL_BANK, LINEAR_BANK = 2, 0, 4
 GELU_BANKS = LINEAR_BANK
 
 
@@ -112,8 +112,8 @@ def tile_moe_shf_glu_gelu_kernel(
         load_planes(s1[1], w1_scales[FIRST_EXPERTS:E, 0])
         load_rows(s13s, 0, w1s_scales[0])
         load_rows(s13s, W3S_ROWS, w3s_scales[0])
-        w3_t = [load_fp4_words(w3_words, 0, FIRST_W3, "w3_0")]
         load_planes(s3, w3_scales[:, 0])
+        w3_t = [load_fp4_words(w3_words, 0, FIRST_W3, "w3_0")]
         w1_t.append(load_fp4_words(w1_words, GELU_AHEAD, E, "w1_2"))
         w1s_t = load_fp8_words(w1s_words, "w1s_t")
         w3_t.append(load_fp4_words(w3_words, FIRST_W3, E, "w3_1"))
@@ -153,13 +153,16 @@ def tile_moe_shf_glu_gelu_kernel(
             taken[first] += 1
             return first + (taken[first] - 1) % 2
 
-        def gather(g):
-            idx = offs_t[:, g * C // PER_COLUMN:(g + 1) * C // PER_COLUMN]
-            words = held([P, C], U32, "words%d" % g)
-            scales = held([P, C], U8, "scales%d" % g)
-            nc.vector.tensor_copy(scales[:], xs[:].indirect(idx))
-            nc.vector.tensor_copy(words[:], xw[:].bitcast(U32).indirect(idx))
-            tokens[g] = (words[:], scales[:])
+        def gather_scales(g):
+            t = held([P, C], U8, "scales%d" % g)
+            nc.vector.tensor_copy(t[:], xs[:].indirect(offs_t[:, g * C // PER_COLUMN:(g + 1) * C // PER_COLUMN]))
+            return t[:]
+
+        def gather_words(g, name):
+            t = held([P, C], U32, name)
+            nc.vector.tensor_copy(t[:], xw[:].bitcast(U32).indirect(
+                offs_t[:, g * C // PER_COLUMN:(g + 1) * C // PER_COLUMN]))
+            return t[:]
 
         def sort_words(branch, src):
             sorted_words[branch] = held([P, H], U32, "sorted%d" % branch)
@@ -183,7 +186,7 @@ def tile_moe_shf_glu_gelu_kernel(
             return acc[:].rearrange("p (d t) -> p t d", d=4)
 
         def gelu(g, j, acc):
-            t = ring.tile([P, H], F32, name="act", bufs=2 * E + SHARED_PARTS)
+            t = held([P, H], F32, "act%d_%d" % (g, j))
             if g != SHARED:
                 act[g, j] = t[:].rearrange("s (u p e) -> s u p e", u=2, e=2)
             else:
@@ -257,14 +260,16 @@ def tile_moe_shf_glu_gelu_kernel(
                                     rhs=w2s_t[:].bitcast(FP8X4), rhs_scale=s2s[:], start=True, stop=True)
             nc.scalar.copy(ys[:, k * C:(k + 1) * C], y[:])
 
-        for g in range(E):
-            gather(g)
+        for g in range(E - 1):
+            scales = gather_scales(g)
+            tokens[g] = (gather_words(g, "words%d" % g), scales)
             if g == GELU_AHEAD:
                 sort_words(0, w1s_t)
                 parts = [(e, j) for e in range(LEAD) for j in ((0, 1) if e == 0 else (1, 0))]
                 for k, part in enumerate(parts):
                     linear(*part, LINEAR_BANK + k)
             gelu_both(g)
+        late_scales = gather_scales(E - 1)
         sorted_planes = held([P, H], U8, "planes_s")
         nc.gpsimd.tensor_copy(sorted_planes[:].rearrange("k (d p) -> k d p", d=4),
                               s13s[:].rearrange("k (p d) -> k d p", d=4))
@@ -282,6 +287,10 @@ def tile_moe_shf_glu_gelu_kernel(
             multiply(g, 1)
             linear_ahead(g, 1)
             turn(g)
+            if g == 0:
+                tokens[E - 1] = (gather_words(E - 1, "act0_0"), late_scales)
+                for j in range(2):
+                    gelu(E - 1, j, project(in_turn(SMALL_BANK), E - 1, j, 0))
             if g == E - 2 * LEAD:
                 sort_words(1, w3s_t)
             if g >= LAG and (g - LAG) % 2 == 0:

from contextlib import ExitStack

import concourse.mybir as mybir
from concourse.masks import make_identity

T, E, C, H, N, TOP = 512, 8, 256, 512, 128, 4
FLOPS = 3019898880

F32 = mybir.dt.float32
BF16 = mybir.dt.bfloat16
I32 = mybir.dt.int32
U32 = mybir.dt.uint32
U16 = mybir.dt.uint16
U8 = mybir.dt.uint8
FP8X4 = mybir.dt.float8_e4m3fn_x4
FP4X4 = mybir.dt.float4_e2m1fn_x4
COPY = mybir.ActivationFunctionType.Copy
GELU = mybir.ActivationFunctionType.Gelu_apprx_tanh
MULT = mybir.AluOpType.mult
ADD = mybir.AluOpType.add

P = 128
PER_COLUMN = 16
SHARED = E
SHARED_PARTS = T // P
W3S_ROWS = 4

FIRST_EXPERTS = 2
GELU_AHEAD = 6
FIRST_W3 = 4

LEAD = 2
LAG = 3
SHARED_GELU_AT = (2, 4, 6)
PAIRED = E - 2

TURN_BANK, SMALL_BANK, LINEAR_BANK = 2, 0, 4
GELU_BANKS = LINEAR_BANK


def tile_moe_shf_glu_gelu_kernel(
    tc, x_words, x_scales, w1_words, w1_scales, w3_words, w3_scales, w2_words, w2_scales,
    w1s_words, w1s_scales, w3s_words, w3s_scales, w2s_words, w2s_scales,
    gate, offs, pos1, pos2, pos3, pos4, out,
):
    nc = tc.nc
    with ExitStack() as ctx:
        keep = ctx.enter_context(tc.tile_pool(name="keep", bufs=1))
        ring = ctx.enter_context(tc.tile_pool(name="ring", bufs=1))
        psum = ctx.enter_context(tc.psum_pool(name="psum", bufs=1))

        def held(shape, dtype, name):
            return keep.tile(shape, dtype, name=name, align_bytes=64)

        def banked(shape, bank):
            return psum.tile(shape, F32, name="bank%d" % bank)

        def load_list(src, name):
            t = keep.tile(list(src.shape), U16, name=name)
            nc.sync.dma_start(t[:], src)
            return t

        def load_fp8_words(src, name):
            t = held([P, src.shape[2]], I32, name)
            nc.sync.dma_start(t[:], src[0].rearrange("p n d -> p (n d)").bitcast(I32))
            return t

        def load_fp4_words(src, lo, hi, name):
            t = held([P, hi - lo, src.shape[3]], U8, name)
            nc.sync.dma_start(t[:].bitcast(I32), src[lo:hi, 0].rearrange("e p n -> p e n").bitcast(I32))
            return t

        def spread_plane(t, src, queues):
            for q in range(4):
                rows = src[4 * q:4 * q + 4, :].bitcast(I32)
                queues[q].dma_start(t[32 * q:32 * q + 32, :].bitcast(I32),
                                    rows.unsqueeze(0).to_broadcast([8, 4, rows.shape[1]]))

        def zeroed_planes(src, name, engine):
            t = held([P, src.shape[0], src.shape[-1]], U8, name)
            engine.memset(t[:].rearrange("p e n -> p (e n)").bitcast(I32), 0)
            return t

        def load_planes(t, src):
            for r in range(4):
                nc.sync.dma_start(t[r:P:32].bitcast(I32), src[:, r:16:4, :].rearrange("e q n -> q e n").bitcast(I32))

        def load_rows(t, first, src):
            for q in range(4):
                nc.sync.dma_start(t[32 * q + first:32 * q + first + 4, :].bitcast(I32),
                                  src[4 * q:4 * q + 4, :].bitcast(I32))

        xw = held([P, T], I32, "xw")
        xs = held([P, T], U8, "xs")
        s1 = [zeroed_planes(w1_scales[0:FIRST_EXPERTS, 0], "s1a", nc.vector),
              zeroed_planes(w1_scales[FIRST_EXPERTS:E, 0], "s1b", nc.vector)]
        s13s = held([P, H], U8, "s13s")
        nc.vector.memset(s13s[:].bitcast(I32), 0)
        s3 = zeroed_planes(w3_scales, "s3", nc.vector)
        ident = held([P, P], F32, "ident")
        make_identity(nc, ident[:])
        s2 = zeroed_planes(w2_scales, "s2", nc.gpsimd)
        s2s = held([P, N], U8, "s2s")
        gate_t = [held([P, 2, T], F32, "gate%d" % i) for i in range(2)]

        offs_t = load_list(offs, "offs_t")
        spread_plane(xs, x_scales[0], (nc.sync, nc.sync, nc.scalar, nc.scalar))
        nc.scalar.dma_start(xw[:], x_words[0].rearrange("p n d -> p (n d)").bitcast(I32))
        w1_t = [load_fp4_words(w1_words, 0, FIRST_EXPERTS, "w1_0")]
        load_planes(s1[0], w1_scales[0:FIRST_EXPERTS, 0])
        w1_t.append(load_fp4_words(w1_words, FIRST_EXPERTS, GELU_AHEAD, "w1_1"))
        load_planes(s1[1], w1_scales[FIRST_EXPERTS:E, 0])
        load_rows(s13s, 0, w1s_scales[0])
        load_rows(s13s, W3S_ROWS, w3s_scales[0])
        load_planes(s3, w3_scales[:, 0])
        w3_t = [load_fp4_words(w3_words, 0, FIRST_W3, "w3_0")]
        w1_t.append(load_fp4_words(w1_words, GELU_AHEAD, E, "w1_2"))
        w1s_t = load_fp8_words(w1s_words, "w1s_t")
        w3_t.append(load_fp4_words(w3_words, FIRST_W3, E, "w3_1"))
        load_planes(s2, w2_scales[:, 0])
        w2_t = load_fp4_words(w2_words, 0, E, "w2_t")
        w3s_t = load_fp8_words(w3s_words, "w3s_t")
        w2s_t = load_fp8_words(w2s_words, "w2s_t")
        spread_plane(s2s, w2s_scales[0], (nc.sync,) * 4)
        pos_t = {r: load_list(src, "pos_t%d" % r) for r, src in ((2, pos3), (3, pos4), (0, pos1))}
        nc.sync.dma_start(gate_t[0][:], gate[0:TOP:2].rearrange("r p t -> p r t"))
        pos_t[1] = load_list(pos2, "pos_t1")
        nc.sync.dma_start(gate_t[1][:], gate[1:TOP:2].rearrange("r p t -> p r t"))

        def expert_of(loads, starts, g):
            k = sum(1 for start in starts if g >= start) - 1
            return loads[k][:, g - starts[k], :]

        def gelu_weights(g):
            return expert_of(w1_t, (0, FIRST_EXPERTS, GELU_AHEAD), g).bitcast(FP4X4), expert_of(s1, (0, FIRST_EXPERTS), g)

        def linear_weights(g):
            return expert_of(w3_t, (0, FIRST_W3), g).bitcast(FP4X4), s3[:, g, :]

        tokens = {}
        act = {}
        lin = {}
        lin_bank = {}
        h = {}
        h_t = {}
        hs = []
        sorted_words = {}
        y_all = held([P, E * C], F32, "y_all")
        ys = held([P, T], F32, "ys")
        taken = {TURN_BANK: 0, SMALL_BANK: 0}

        def in_turn(first):
            taken[first] += 1
            return first + (taken[first] - 1) % 2

        def gather_scales(g):
            t = held([P, C], U8, "scales%d" % g)
            nc.vector.tensor_copy(t[:], xs[:].indirect(offs_t[:, g * C // PER_COLUMN:(g + 1) * C // PER_COLUMN]))
            return t[:]

        def gather_words(g, name):
            t = held([P, C], U32, name)
            nc.vector.tensor_copy(t[:], xw[:].bitcast(U32).indirect(
                offs_t[:, g * C // PER_COLUMN:(g + 1) * C // PER_COLUMN]))
            return t[:]

        def sort_words(branch, src):
            sorted_words[branch] = held([P, H], U32, "sorted%d" % branch)
            nc.scalar.copy(sorted_words[branch][:].rearrange("k (d p) -> k p d", d=4),
                           src[:].bitcast(U32).rearrange("k (p d) -> k p d", d=4))

        def project(bank, g, j, branch):
            acc = banked([P, H], bank)
            toks = slice(j * P, (j + 1) * P)
            if g != SHARED:
                words, scales = tokens[g]
                w, s = (gelu_weights, linear_weights)[branch](g)
                nc.tensor.matmul_mx(out=acc[:], lhsT=words[:, toks].bitcast(FP8X4), lhsT_scale=scales[:, toks],
                                    rhs=w, rhs_scale=s, start=True, stop=True)
                return acc[:].rearrange("s (p u e) -> s u p e", u=2, e=2)
            for d in range(4):
                cols = slice(d * P, (d + 1) * P)
                nc.tensor.matmul_mx(out=acc[:, cols], lhsT=sorted_words[branch][:, cols].bitcast(FP8X4),
                                    lhsT_scale=sorted_planes[W3S_ROWS * branch:P, cols],
                                    rhs=xw[:, toks].bitcast(FP8X4), rhs_scale=xs[:, toks], start=True, stop=True)
            return acc[:].rearrange("p (d t) -> p t d", d=4)

        def gelu(g, j, acc):
            t = held([P, H], F32, "act%d_%d" % (g, j))
            if g != SHARED:
                act[g, j] = t[:].rearrange("s (u p e) -> s u p e", u=2, e=2)
            else:
                act[g, j] = t[:].rearrange("p (t d) -> p t d", d=4)
            nc.scalar.activation(act[g, j], acc, GELU)

        def gelu_both(g):
            first_bank = 2 * g % GELU_BANKS
            if g in (0, GELU_AHEAD):
                gelu(g, 0, project(first_bank, g, 0, 0))
                gelu(g, 1, project(first_bank + 1, g, 1, 0))
            else:
                other = project(first_bank, g, 1, 0)
                gelu(g, 0, project(first_bank + 1, g, 0, 0))
                gelu(g, 1, other)

        def gelu_shared(j):
            gelu(SHARED, j, project(in_turn(SMALL_BANK), SHARED, j, 0))

        def linear(g, j, bank):
            lin_bank[g, j] = bank
            lin[g, j] = project(bank, g, j, 1)

        def multiply(g, j):
            if g == SHARED:
                if j % 2 == 0:
                    hs.append(held([P, C * 4], BF16, ("hs", "late")[j // 2]))
                dst = hs[-1][:, j % 2 * H:(j % 2 + 1) * H].rearrange("p (t d) -> p t d", d=4)
            else:
                if j == 0:
                    h[g] = held([P, 2, 2, P, 2], BF16, "h%d" % (LEAD if g >= LEAD and g % 2 == 0 else g))
                dst = h[g][:, j]
            nc.vector.tensor_tensor(dst, lin[g, j], act[g, j], MULT)

        def turn(g):
            turned = banked([P, 2, 2, P], in_turn(TURN_BANK))
            for j in (1, 0) if g < E - 1 else (0, 1):
                for u in range(2):
                    nc.tensor.transpose(turned[:, j, u, :], h[g][:, j, u].rearrange("s p e -> s (p e)").bitcast(F32),
                                        ident[:])
            place = g % 2 if g < PAIRED else 0
            if place == 0:
                h_t[g] = held([P, (2 if g < PAIRED else 1) * C * 4], BF16, "late" if g == E - 1 else "h_t%d" % g)
            dst = h_t[g - place][:, place * C * 4:(place + 1) * C * 4]
            nc.scalar.copy(dst.bitcast(F32).rearrange("p (j s u) -> p j s u", j=2, u=2),
                           turned[:].rearrange("p j u s -> p j s u"))

        def quantise(src):
            width = src.shape[1] // 4
            codes = ring.tile([P, width], U32, name="codes", bufs=E, align_bytes=64)
            planes = ring.tile([P, width], U8, name="planes", bufs=E, align_bytes=64)
            nc.vector.quantize_mx(out=codes[:].bitcast(FP8X4), scales=planes[:], in_=src[:])
            return codes, planes

        def second_layer(g, bank):
            codes, planes = quantise(h_t[g])
            width = codes.shape[1]
            y = banked([P, width], bank)
            for k in range(width // C):
                cols = slice(k * C, (k + 1) * C)
                nc.tensor.matmul_mx(out=y[:, cols], lhsT=w2_t[:, g + k, :].bitcast(FP4X4), lhsT_scale=s2[:, g + k, :],
                                    rhs=codes[:, cols].bitcast(FP8X4), rhs_scale=planes[:, cols], start=True, stop=True)
            nc.scalar.copy(y_all[:, g * C:g * C + width], y[:])

        def shared_layer(k, bank):
            codes, planes = quantise(hs[k])
            y = banked([P, C], bank)
            for j in range(2):
                cols = slice(j * P, (j + 1) * P)
                nc.tensor.matmul_mx(out=y[:, cols], lhsT=codes[:, cols].bitcast(FP8X4), lhsT_scale=planes[:, cols],
                                    rhs=w2s_t[:].bitcast(FP8X4), rhs_scale=s2s[:], start=True, stop=True)
            nc.scalar.copy(ys[:, k * C:(k + 1) * C], y[:])

        for g in range(E - 1):
            scales = gather_scales(g)
            tokens[g] = (gather_words(g, "words%d" % g), scales)
            if g == GELU_AHEAD:
                sort_words(0, w1s_t)
                parts = [(e, j) for e in range(LEAD) for j in ((0, 1) if e == 0 else (1, 0))]
                for k, part in enumerate(parts):
                    linear(*part, LINEAR_BANK + k)
            gelu_both(g)
        late_scales = gather_scales(E - 1)
        sorted_planes = held([P, H], U8, "planes_s")
        nc.gpsimd.tensor_copy(sorted_planes[:].rearrange("k (d p) -> k d p", d=4),
                              s13s[:].rearrange("k (p d) -> k d p", d=4))

        def linear_ahead(g, j):
            ahead = g + LEAD
            part = (ahead, 1 - j) if ahead < E else (SHARED, 2 * (ahead - E) + 1 - j)
            linear(*part, lin_bank[g, j])

        for g in range(E - 1):
            multiply(g, 0)
            if g in SHARED_GELU_AT:
                gelu_shared(SHARED_GELU_AT.index(g))
            linear_ahead(g, 0)
            multiply(g, 1)
            linear_ahead(g, 1)
            turn(g)
            if g == 0:
                tokens[E - 1] = (gather_words(E - 1, "act0_0"), late_scales)
                for j in range(2):
                    gelu(E - 1, j, project(in_turn(SMALL_BANK), E - 1, j, 0))
            if g == E - 2 * LEAD:
                sort_words(1, w3s_t)
            if g >= LAG and (g - LAG) % 2 == 0:
                second_layer(g - LAG, in_turn(SMALL_BANK))

        last = E - 1
        multiply(last, 0)
        multiply(last, 1)
        turn(last)
        second_layer(last - LAG, in_turn(SMALL_BANK))
        gelu_shared(SHARED_PARTS - 1)
        linear_ahead(last, 0)
        linear_ahead(last, 1)
        multiply(SHARED, 0)
        multiply(SHARED, 1)
        second_layer(last - 1, TURN_BANK)
        second_layer(last, lin_bank[SHARED, 0])
        shared_layer(0, lin_bank[SHARED, 1])
        multiply(SHARED, 2)
        multiply(SHARED, 3)

        def add_turned(banks, src, blocks, start, stop):
            for b in blocks:
                nc.tensor.matmul(banks[b // 2][:, b % 2, :], src[:, b * P:(b + 1) * P], ident[:], is_transpose=True,
                                 start=start and b % 2 == 0, stop=stop and b % 2 == 1)

        whole = slice(0, T)
        sides = (slice(0, T // 2), slice(T // 2, T))
        blocks_of = ((0, 1), (2, 3))

        def entries(r, cols):
            return y_all[:].indirect(pos_t[r][:, cols.start // PER_COLUMN:cols.stop // PER_COLUMN])

        def gated(r, cols, src):
            nc.vector.tensor_tensor(terms[r][:, cols], src, gate_t[r % 2][:, r // 2, cols], MULT)

        picked = {r: held([P, T], F32, "picked%d" % r) for r in (2, 3)}
        for side in sides:
            nc.scalar.activation(picked[2][:, side], entries(2, side), COPY)
        nc.scalar.activation(picked[3][:], entries(3, whole), COPY)
        terms = [held([P, T], F32, "term%d" % r) for r in range(TOP)]
        gated(0, sides[0], entries(0, sides[0]))
        shared_layer(1, TURN_BANK + 1)
        gated(0, sides[1], entries(0, sides[1]))
        pair = [banked([P, 2, P], LINEAR_BANK + i) for i in range(2)]
        add_turned(pair, terms[0], range(4), True, False)
        for i, side in enumerate(sides):
            gated(2, side, picked[2][:, side])
            add_turned(pair, terms[2], blocks_of[i], False, True)
        gated(1, sides[0], entries(1, sides[0]))
        gated(3, whole, picked[3][:])
        gated(1, sides[1], entries(1, sides[1]))
        rest = held([P, T], F32, "rest")
        for side in sides:
            nc.vector.tensor_tensor(rest[:, side], terms[1][:, side], terms[3][:, side], ADD)
        triple = [banked([P, 2, P], LINEAR_BANK + 2 + i) for i in range(2)]
        add_turned(triple, ys, blocks_of[0], True, False)
        pair_rows = held([P, T], F32, "pair_rows")
        for i, side in enumerate(sides):
            nc.scalar.copy(pair_rows[:, side], pair[i][:].rearrange("p b n -> p (b n)"))
            add_turned(triple, pair_rows, blocks_of[i], i == 1, i == 0)
        add_turned(triple, ys, blocks_of[1], False, True)
        for i, side in enumerate(sides):
            res = held([P, T // 2], F32, "res%d" % i)
            nc.vector.tensor_tensor(res[:], triple[i][:].rearrange("p b t -> p (b t)"), rest[:, side], ADD)
            nc.sync.dma_start(out[:, side], res[:])
